import numpy as np
import ml_dtypes


def mxq(x, axis, fmt="e4m3"):
    dtype, down = {"e4m3": (ml_dtypes.float8_e4m3fn, 7), "e5m2": (ml_dtypes.float8_e5m2, 14)}[fmt]
    v = np.moveaxis(np.asarray(x, np.float32).astype(ml_dtypes.bfloat16).astype(np.float64), axis, -1)
    blocks = v.reshape(v.shape[:-1] + (-1, 32))
    amax = np.abs(blocks).max(-1, keepdims=True)
    byte = np.maximum(np.where(amax > 0, np.frexp(amax)[1] - 1 + 127, 0) - down, 1)
    scale = np.exp2(byte - 127.0)
    codes = (blocks / scale).astype(np.float32).astype(dtype).astype(np.float64)
    return np.moveaxis((codes * scale).reshape(v.shape), -1, axis)


WIDE = False


def mx_kscale(k):
    if not WIDE:
        return np.ones(k)
    levels = np.array([18, -18])
    if k % 512:
        return np.exp2(np.random.permutation(np.resize(levels, k // 32))).repeat(32)
    a = np.empty((k // 512, 16))
    for p in range(k // 512):
        a[p, :8] = np.random.permutation(np.resize(levels, 8))
        for g in range(8):
            far = levels[np.abs(levels - a[p, g]) >= 10]
            a[p, g + 8] = far[np.random.randint(len(far))]
    return np.exp2(a.ravel()).repeat(32)


def f64(x):
    return np.asarray(x).astype(np.float64)


def striped(idx):
    return np.tile(np.asarray(idx).reshape(-1, 16).T, (8, 1)).astype(np.uint16)


def unstriped(offs):
    return offs[:16].T.reshape(-1).astype(np.int64)


B, N, T, D, R = 1, 512, 2048, 512, 1024
LR = 0.1
WD = 0.5


def setup_inputs():
    n = np.random.standard_normal
    idx = np.random.permutation(T)[:B * N]
    s = mx_kscale(D)[:, None]
    z = mx_kscale(R)[:, None]
    x = n((B, D, R))
    return {
        "xT": (x * s).astype(np.float32),
        "wT": (n((D, T)) * (1.00 / np.sqrt(D)) / s).astype(np.float32),
        "y": np.random.randint(0, 2, (B, R, N)).astype(np.float32),
        "wt": (np.random.uniform(0.5, 1.5, (B, R, 1)) * 1.0 / np.sqrt(R) * z).astype(np.float32),
        "xm": (x.transpose(0, 2, 1) / z / s[:, 0]).astype(np.float32),
        "offs": striped(idx),
    }


def reference(xT, wT, y, wt, xm, offs):
    idx = unstriped(offs)
    pick = lambda x: x[:, idx].reshape(x.shape[0], B, N).transpose(1, 0, 2)
    w = pick(f64(wT))
    a = mxq(f64(xT), 1, "e4m3").transpose(0, 2, 1) @ mxq(w, 1, "e4m3")
    g = f64(wt) * (1.0 / (1.0 + np.exp(-a)) - f64(y))
    dw = mxq(f64(xm), 1, "e4m3").transpose(0, 2, 1) @ mxq(g, 1, "e5m2")
    nw = (1.0 - LR * WD) * w - LR * dw
    tables = []
    for old, new in ((wT, nw),):
        table = f64(old)
        table[:, idx] = new.transpose(1, 0, 2).reshape(D, B * N)
        tables.append(table)
    return tables[0]

@@ -1,0 +1,205 @@
+from contextlib import ExitStack
+
+import concourse.mybir as mybir
+
+N, T, D, R = 512, 2048, 512, 1024
+LR, WD = 0.1, 0.5
+FLOPS = 2 * 2 * R * D * N
+
+F32 = mybir.dt.float32
+BF16 = mybir.dt.bfloat16
+U32 = mybir.dt.uint32
+U16 = mybir.dt.uint16
+U8 = mybir.dt.uint8
+E4M3 = mybir.dt.float8_e4m3fn_x4
+E5M2 = mybir.dt.float8_e5m2_x4
+ALU = mybir.AluOpType
+ACT = mybir.ActivationFunctionType
+
+P = 128
+PACK = 4
+K_PASS = P * PACK
+PASSES = R // K_PASS
+
+W_ON_SCALAR = 40
+X_ON_SCALAR = [64,0]
+G_ON_SCALAR = [0,0]
+FUSED = [True,True]
+YW_ON_SCALAR = [0,0]
+POOL_ADD = []
+
+
+def tile_attend_gnce_sgd_kernel(tc, xT, wT, y, wt, xm, offs, out):
+    nc = tc.nc
+    with ExitStack() as ctx:
+        sb = ctx.enter_context(tc.tile_pool(name="sb", bufs=1))
+        ps_a = ctx.enter_context(tc.psum_pool(name="ps_a", bufs=4))
+        ps_dw = ctx.enter_context(tc.psum_pool(name="ps_dw", bufs=1))
+
+        def f32_tile(name, shape, tag=None):
+            return sb.tile(shape, F32, name=name, tag=tag or name, align_bytes=64)
+
+        def bf_tile(name, tag=None):
+            return sb.tile([P, K_PASS * PACK], BF16, name=name, tag=tag or name, align_bytes=64)
+
+        def mx_tiles(name):
+            return (sb.tile([P, K_PASS], U32, name=name + "_codes", align_bytes=64),
+                    sb.tile([P, K_PASS], U8, name=name + "_scales", align_bytes=64))
+
+        offsets = sb.tile([P, N // 16], U16, name="offsets")
+        wt_sb = f32_tile("wt_sb", [P, PASSES, PACK])
+        warm = f32_tile("warm", [P, 8])
+        table = [f32_tile("table%d" % t, [P, T]) for t in range(PACK)]
+        result = [f32_tile("result%d" % t, [P, T]) for t in range(PACK - 1)]
+        x_raw = [f32_tile("x_raw%d" % g, [P, PACK, K_PASS]) for g in range(PASSES)]
+        y_raw = [f32_tile("y_raw%d" % g, [P, PACK, N]) for g in range(PASSES)]
+        m_raw = [f32_tile("m_raw%d" % g, [P, PACK, D]) for g in range(PASSES)]
+
+        w_rows = wT.rearrange("(p t) c -> p t c", t=PACK)
+        out_rows = out.rearrange("(p t) c -> p t c", t=PACK)
+        x_rows = xT[0].rearrange("(p t) r -> p t r", t=PACK)
+        y_rows = y[0].rearrange("(g p j) i -> g p j i", g=PASSES, j=PACK)
+        m_rows = xm[0].rearrange("(g p j) d -> g p j d", g=PASSES, j=PACK)
+
+        nc.sync.dma_start(table[0][:], w_rows[:, 0, :])
+        nc.sync.dma_start(offsets[:], offs)
+        nc.sync.dma_start(wt_sb[:], wt[0].rearrange("(g p j) one -> p g (j one)", g=PASSES, j=PACK))
+        for t in range(1, PACK):
+            nc.sync.dma_start(table[t][:], w_rows[:, t, :])
+        nc.sync.dma_start(x_raw[0][:], x_rows[:, :, 0 * K_PASS:(0 + 1) * K_PASS])
+        nc.sync.dma_start(x_raw[1][:], x_rows[:, :, 1 * K_PASS:(1 + 1) * K_PASS])
+        for h in range(2):
+            nc.sync.dma_start(y_raw[0][:, 2 * h:2 * h + 2, :], y_rows[0][:, 2 * h:2 * h + 2, :])
+        for h in range(2):
+            nc.sync.dma_start(y_raw[1][:, 2 * h:2 * h + 2, :], y_rows[1][:, 2 * h:2 * h + 2, :])
+        nc.sync.dma_start(m_raw[0][:], m_rows[0])
+        for h in range(2):
+            nc.sync.dma_start(m_raw[1][:, :, 256 * h:256 * h + 256], m_rows[1][:, :, 256 * h:256 * h + 256])
+
+        nc.scalar.activation(warm[:], wt_sb[:].rearrange("p g j -> p (g j)"), ACT.Sigmoid)
+
+        def interleave(dst, src, on_scalar):
+            d4 = dst[:].rearrange("p (c i t) -> p c t i", i=4, t=PACK)
+            s4 = src[:].rearrange("p t (c i) -> p c t i", i=4)
+            if on_scalar > 0:
+                nc.scalar.copy(d4[:, :on_scalar], s4[:, :on_scalar])
+            if on_scalar < P:
+                nc.vector.tensor_copy(d4[:, on_scalar:], s4[:, on_scalar:])
+
+        def interleave_permuted(engine_copy, dst, src, m0, m1):
+            if m1 > m0:
+                engine_copy(
+                    dst[:].rearrange("p (a m k) -> p m k a", a=PACK, k=PACK)[:, m0:m1],
+                    src[:].rearrange("p k (m a) -> p m k a", a=PACK)[:, m0:m1])
+
+        def interleave_xm(dst, g, h, m0, m1):
+            nc.scalar.copy(
+                dst[:].rearrange("p (g a m k) -> p g m k a", g=PASSES, a=2, k=PACK)[:, g, m0:m1],
+                m_raw[g][:].rearrange("p k (m a) -> p m k a", a=PACK)[:, m0:m1, :, 2 * h:2 * h + 2])
+
+        def quantize(mx, src, fmt, c0, c1):
+            nc.vector.quantize_mx(out=mx[0][:, c0:c1].bitcast(fmt), scales=mx[1][:, c0:c1],
+                                  in_=src[:, PACK * c0:PACK * c1])
+
+        w_picked = f32_tile("w_picked", [P, PACK, N])
+        w_decayed = [f32_tile("w_decayed%d" % t, [P, N]) for t in range(PACK - 1)]
+        for t in range(PACK):
+            nc.vector.tensor_copy(w_picked[:, t, :], table[t][:].indirect(offsets[:]))
+            if t < PACK - 1:
+                nc.scalar.activation(result[t][:], table[t][:], ACT.Copy)
+                nc.vector.tensor_scalar(w_decayed[t][:], w_picked[:, t, :], 1.0 - LR * WD, None, ALU.mult)
+        w_bf = bf_tile("w_bf")
+        interleave(w_bf, w_picked, W_ON_SCALAR)
+        w_mx = mx_tiles("w")
+        quantize(w_mx, w_bf, E4M3, 0, N)
+
+        x_mx = [mx_tiles("x%d" % g) for g in range(PASSES)]
+        err = [f32_tile("err%d" % g, [P, PACK, N]) for g in range(PASSES)]
+        g_bf = [bf_tile("g_bf%d" % g) for g in range(PASSES)]
+        g_mx = [mx_tiles("g%d" % g) for g in range(PASSES)]
+        m_lo = bf_tile("m_lo")
+        m_mx = [mx_tiles("m_half%d" % h) for h in range(2)]
+        dw = [ps_dw.tile([P, N], F32, name="dw%d" % t) for t in range(PACK)]
+
+        for g in range(PASSES):
+            x_bf = bf_tile("x_bf")
+            interleave_permuted(nc.scalar.copy, x_bf, x_raw[g], 0, X_ON_SCALAR[g])
+            interleave_permuted(nc.vector.tensor_copy, x_bf, x_raw[g], X_ON_SCALAR[g], P)
+            quantize(x_mx[g], x_bf, E4M3, 0, K_PASS)
+            for j in range(PACK):
+                cols = slice(j * P, (j + 1) * P)
+                logits = ps_a.tile([P, N], F32, name="logits")
+                nc.tensor.matmul_mx(
+                    out=logits[:],
+                    lhsT=x_mx[g][0][:, cols].bitcast(E4M3), lhsT_scale=x_mx[g][1][:, cols],
+                    rhs=w_mx[0][:].bitcast(E4M3), rhs_scale=w_mx[1][:],
+                    start=True, stop=True)
+                nc.scalar.activation(err[g][:, j, :], logits[:], ACT.Sigmoid)
+
+        def grad_matmul(g, t):
+            c0 = (2 * g + t % 2) * P
+            cols = slice(c0, c0 + P)
+            nc.tensor.matmul_mx(
+                out=dw[t][:],
+                lhsT=m_mx[t // 2][0][:, cols].bitcast(E4M3), lhsT_scale=m_mx[t // 2][1][:, cols],
+                rhs=g_mx[g][0][:].bitcast(E5M2), rhs_scale=g_mx[g][1][:],
+                start=(g == 0), stop=(g == PASSES - 1))
+
+        for g in range(PASSES):
+            if FUSED[g]:
+                for j in range(PACK):
+                    nc.vector.tensor_tensor(err[g][:, j, :], err[g][:, j, :], y_raw[g][:, j, :], ALU.subtract)
+                nc.vector.tensor_tensor(
+                    g_bf[g][:].rearrange("p (c i j) -> p c j i", i=4, j=PACK),
+                    err[g][:].rearrange("p j (c i) -> p c j i", i=4),
+                    wt_sb[:, g, :].unsqueeze(1).unsqueeze(3).to_broadcast([P, N // 4, PACK, 4]),
+                    ALU.mult)
+            else:
+                for j in range(PACK):
+                    if j < YW_ON_SCALAR[g]:
+                        nc.scalar.activation(y_raw[g][:, j, :], y_raw[g][:, j, :], ACT.Copy, scale=wt_sb[:, g, j:j + 1])
+                    else:
+                        nc.vector.tensor_scalar(y_raw[g][:, j, :], y_raw[g][:, j, :], wt_sb[:, g, j:j + 1], None, ALU.mult)
+                for j in range(PACK):
+                    nc.vector.scalar_tensor_tensor(err[g][:, j, :], err[g][:, j, :], wt_sb[:, g, j:j + 1],
+                                                   y_raw[g][:, j, :], ALU.mult, ALU.subtract)
+                interleave(g_bf[g], err[g], G_ON_SCALAR[g])
+            for h in range(2):
+                interleave_xm(m_lo, g, 0, 64 * h, 64 * h + 64)
+            quantize(m_mx[0], m_lo, E4M3, 2 * P * g, 2 * P * (g + 1))
+            quantize(g_mx[g], g_bf[g], E5M2, 0, N)
+            for t in range(2):
+                grad_matmul(g, t)
+
+        step = [f32_tile("step%d" % t, [P, N]) for t in range(2)]
+        new_cols = [f32_tile("new_cols%d" % t, [P, N]) for t in range(PACK)]
+
+        def update(t):
+            if t in POOL_ADD:
+                nc.scalar.activation(step[t % 2][:], dw[t][:], ACT.Copy, scale=-LR)
+                nc.gpsimd.tensor_tensor(new_cols[t][:], step[t % 2][:], w_decayed[t][:], ALU.add)
+            else:
+                nc.vector.scalar_tensor_tensor(new_cols[t][:], dw[t][:], -LR, w_decayed[t][:], ALU.mult, ALU.add)
+
+        def scatter(t):
+            nc.vector.tensor_copy(result[t][:].indirect(offsets[:]), new_cols[t][:])
+            nc.sync.dma_start(out_rows[:, t, :], result[t][:])
+
+        m_hi = bf_tile("m_hi")
+        for g in range(PASSES):
+            interleave_xm(m_hi, g, 1, 0, P)
+        quantize(m_mx[1], m_hi, E4M3, 0, 4 * P)
+        for t in range(2, PACK):
+            for g in range(PASSES):
+                grad_matmul(g, t)
+        last = PACK - 1
+        w_decayed.append(f32_tile("w_decayed3", [P, N], "x_raw1"))
+        result.append(f32_tile("result3", [P, T], "y_raw1"))
+        nc.scalar.activation(w_decayed[last][:], w_picked[:, last, :], ACT.Copy, scale=1.0 - LR * WD)
+        for q in range(4):
+            nc.scalar.activation(result[last][:, q * 512:(q + 1) * 512], table[last][:, q * 512:(q + 1) * 512], ACT.Copy)
+        update(0)
+        for t in range(PACK):
+            if t + 1 < PACK:
+                update(t + 1)
+            scatter(t)

@@ -26,7 +26,7 @@ X_ON_SCALAR = [64,0]
 G_ON_SCALAR = [0,0]
 FUSED = [True,True]
 YW_ON_SCALAR = [0,0]
-POOL_ADD = []
+POOL_ADD = [1,2,3]
 
 
 def tile_attend_gnce_sgd_kernel(tc, xT, wT, y, wt, xm, offs, out):
@@ -73,8 +73,7 @@ def tile_attend_gnce_sgd_kernel(tc, xT, wT, y, wt, xm, offs, out):
         for h in range(2):
             nc.sync.dma_start(y_raw[1][:, 2 * h:2 * h + 2, :], y_rows[1][:, 2 * h:2 * h + 2, :])
         nc.sync.dma_start(m_raw[0][:], m_rows[0])
-        for h in range(2):
-            nc.sync.dma_start(m_raw[1][:, :, 256 * h:256 * h + 256], m_rows[1][:, :, 256 * h:256 * h + 256])
+        nc.sync.dma_start(m_raw[1][:], m_rows[1])
 
         nc.scalar.activation(warm[:], wt_sb[:].rearrange("p g j -> p (g j)"), ACT.Sigmoid)
 
@@ -171,13 +170,13 @@ def tile_attend_gnce_sgd_kernel(tc, xT, wT, y, wt, xm, offs, out):
             for t in range(2):
                 grad_matmul(g, t)
 
-        step = [f32_tile("step%d" % t, [P, N]) for t in range(2)]
+        step = [f32_tile("step%d" % t, [P, N]) for t in range(PACK)]
         new_cols = [f32_tile("new_cols%d" % t, [P, N]) for t in range(PACK)]
 
         def update(t):
             if t in POOL_ADD:
-                nc.scalar.activation(step[t % 2][:], dw[t][:], ACT.Copy, scale=-LR)
-                nc.gpsimd.tensor_tensor(new_cols[t][:], step[t % 2][:], w_decayed[t][:], ALU.add)
+                nc.scalar.activation(step[t][:], dw[t][:], ACT.Copy, scale=-LR)
+                nc.gpsimd.tensor_tensor(new_cols[t][:], step[t][:], w_decayed[t][:], ALU.add)
             else:
                 nc.vector.scalar_tensor_tensor(new_cols[t][:], dw[t][:], -LR, w_decayed[t][:], ALU.mult, ALU.add)
 

@@ -21,8 +21,8 @@ PACK = 4
 K_PASS = P * PACK
 PASSES = R // K_PASS
 
-W_ON_SCALAR = 40
-X_ON_SCALAR = [64,0]
+W_ON_SCALAR = 64
+X_ON_SCALAR = [1,0]
 G_ON_SCALAR = [0,0]
 FUSED = [True,True]
 YW_ON_SCALAR = [0,0]
@@ -75,7 +75,8 @@ def tile_attend_gnce_sgd_kernel(tc, xT, wT, y, wt, xm, offs, out):
         nc.sync.dma_start(m_raw[0][:], m_rows[0])
         nc.sync.dma_start(m_raw[1][:], m_rows[1])
 
-        nc.scalar.activation(warm[:], wt_sb[:].rearrange("p g j -> p (g j)"), ACT.Sigmoid)
+        nc.gpsimd.memset(warm[:], 0.0)
+        nc.scalar.activation(warm[:], warm[:], ACT.Sigmoid)
 
         def interleave(dst, src, on_scalar):
             d4 = dst[:].rearrange("p (c i t) -> p c t i", i=4, t=PACK)
@@ -85,11 +86,10 @@ def tile_attend_gnce_sgd_kernel(tc, xT, wT, y, wt, xm, offs, out):
             if on_scalar < P:
                 nc.vector.tensor_copy(d4[:, on_scalar:], s4[:, on_scalar:])
 
-        def interleave_permuted(engine_copy, dst, src, m0, m1):
-            if m1 > m0:
-                engine_copy(
-                    dst[:].rearrange("p (a m k) -> p m k a", a=PACK, k=PACK)[:, m0:m1],
-                    src[:].rearrange("p k (m a) -> p m k a", a=PACK)[:, m0:m1])
+        def interleave_permuted(engine_copy, dst, src, a0, a1):
+            engine_copy(
+                dst[:].rearrange("p (a m k) -> p m k a", a=PACK, k=PACK)[:, :, :, a0:a1],
+                src[:].rearrange("p k (m a) -> p m k a", a=PACK)[:, :, :, a0:a1])
 
         def interleave_xm(dst, g, h, m0, m1):
             nc.scalar.copy(
@@ -103,8 +103,11 @@ def tile_attend_gnce_sgd_kernel(tc, xT, wT, y, wt, xm, offs, out):
         w_picked = f32_tile("w_picked", [P, PACK, N])
         w_decayed = [f32_tile("w_decayed%d" % t, [P, N]) for t in range(PACK - 1)]
         for t in range(PACK):
-            nc.vector.tensor_copy(w_picked[:, t, :], table[t][:].indirect(offsets[:]))
-            if t < PACK - 1:
+            if t == PACK - 1:
+                for h in range(2):
+                    nc.vector.tensor_copy(w_picked[:, t, 256 * h:256 * h + 256], table[t][:].indirect(offsets[:, 16 * h:16 * h + 16]))
+            else:
+                nc.vector.tensor_copy(w_picked[:, t, :], table[t][:].indirect(offsets[:]))
                 nc.scalar.activation(result[t][:], table[t][:], ACT.Copy)
                 nc.vector.tensor_scalar(w_decayed[t][:], w_picked[:, t, :], 1.0 - LR * WD, None, ALU.mult)
         w_bf = bf_tile("w_bf")
@@ -122,9 +125,14 @@ def tile_attend_gnce_sgd_kernel(tc, xT, wT, y, wt, xm, offs, out):
 
         for g in range(PASSES):
             x_bf = bf_tile("x_bf")
-            interleave_permuted(nc.scalar.copy, x_bf, x_raw[g], 0, X_ON_SCALAR[g])
-            interleave_permuted(nc.vector.tensor_copy, x_bf, x_raw[g], X_ON_SCALAR[g], P)
-            quantize(x_mx[g], x_bf, E4M3, 0, K_PASS)
+            if X_ON_SCALAR[g]:
+                interleave_permuted(nc.vector.tensor_copy, x_bf, x_raw[g], 0, 2)
+                interleave_permuted(nc.scalar.copy, x_bf, x_raw[g], 2, PACK)
+                quantize(x_mx[g], x_bf, E4M3, 0, 2 * P)
+                quantize(x_mx[g], x_bf, E4M3, 2 * P, 4 * P)
+            else:
+                interleave_permuted(nc.vector.tensor_copy, x_bf, x_raw[g], 0, PACK)
+                quantize(x_mx[g], x_bf, E4M3, 0, K_PASS)
             for j in range(PACK):
                 cols = slice(j * P, (j + 1) * P)
                 logits = ps_a.tile([P, N], F32, name="logits")
@@ -145,24 +153,19 @@ def tile_attend_gnce_sgd_kernel(tc, xT, wT, y, wt, xm, offs, out):
                 start=(g == 0), stop=(g == PASSES - 1))
 
         for g in range(PASSES):
+            g4 = g_bf[g][:].rearrange("p (c i j) -> p c j i", i=4, j=PACK)
+            e4 = err[g][:].rearrange("p j (c i) -> p c j i", i=4)
             if FUSED[g]:
-                for j in range(PACK):
-                    nc.vector.tensor_tensor(err[g][:, j, :], err[g][:, j, :], y_raw[g][:, j, :], ALU.subtract)
+                for h in range(4):
+                    js = slice(h, h + 1)
+                    nc.vector.tensor_tensor(err[g][:, js, :], err[g][:, js, :], y_raw[g][:, js, :], ALU.subtract)
                 nc.vector.tensor_tensor(
-                    g_bf[g][:].rearrange("p (c i j) -> p c j i", i=4, j=PACK),
-                    err[g][:].rearrange("p j (c i) -> p c j i", i=4),
-                    wt_sb[:, g, :].unsqueeze(1).unsqueeze(3).to_broadcast([P, N // 4, PACK, 4]),
-                    ALU.mult)
+                    g4, e4, wt_sb[:, g, :].unsqueeze(1).unsqueeze(3).to_broadcast([P, N // 4, PACK, 4]), ALU.mult)
             else:
                 for j in range(PACK):
-                    if j < YW_ON_SCALAR[g]:
-                        nc.scalar.activation(y_raw[g][:, j, :], y_raw[g][:, j, :], ACT.Copy, scale=wt_sb[:, g, j:j + 1])
-                    else:
-                        nc.vector.tensor_scalar(y_raw[g][:, j, :], y_raw[g][:, j, :], wt_sb[:, g, j:j + 1], None, ALU.mult)
-                for j in range(PACK):
-                    nc.vector.scalar_tensor_tensor(err[g][:, j, :], err[g][:, j, :], wt_sb[:, g, j:j + 1],
-                                                   y_raw[g][:, j, :], ALU.mult, ALU.subtract)
-                interleave(g_bf[g], err[g], G_ON_SCALAR[g])
+                    nc.scalar.activation(err[g][:, j, :], err[g][:, j, :], ACT.Copy, scale=wt_sb[:, g, j:j + 1])
+                    nc.vector.tensor_scalar(y_raw[g][:, j, :], y_raw[g][:, j, :], wt_sb[:, g, j:j + 1], None, ALU.mult)
+                nc.vector.tensor_tensor(g4, e4, y_raw[g][:].rearrange("p j (c i) -> p c j i", i=4), ALU.subtract)
             for h in range(2):
                 interleave_xm(m_lo, g, 0, 64 * h, 64 * h + 64)
             quantize(m_mx[0], m_lo, E4M3, 2 * P * g, 2 * P * (g + 1))
@@ -184,7 +187,7 @@ def tile_attend_gnce_sgd_kernel(tc, xT, wT, y, wt, xm, offs, out):
             nc.vector.tensor_copy(result[t][:].indirect(offsets[:]), new_cols[t][:])
             nc.sync.dma_start(out_rows[:, t, :], result[t][:])
 
-        m_hi = bf_tile("m_hi")
+        m_hi = bf_tile("m_hi", None)
         for g in range(PASSES):
             interleave_xm(m_hi, g, 1, 0, P)
         quantize(m_mx[1], m_hi, E4M3, 0, 4 * P)

@@ -19,189 +19,172 @@ ACT = mybir.ActivationFunctionType
 P = 128
 PACK = 4
 K_PASS = P * PACK
-PASSES = R // K_PASS
-
-W_ON_SCALAR = 64
-X_ON_SCALAR = [1,0]
-G_ON_SCALAR = [0,0]
-FUSED = [True,True]
-YW_ON_SCALAR = [0,0]
-POOL_ADD = [1,2,3]
+GROUPS = R // K_PASS
+LAST = PACK - 1
+RUN = 4
+LIST_COLS = N // 16
+LOGIT_BANKS = 4
+LATE_COPY_PIECES = 4
 
 
 def tile_attend_gnce_sgd_kernel(tc, xT, wT, y, wt, xm, offs, out):
     nc = tc.nc
     with ExitStack() as ctx:
         sb = ctx.enter_context(tc.tile_pool(name="sb", bufs=1))
-        ps_a = ctx.enter_context(tc.psum_pool(name="ps_a", bufs=4))
+        ps_a = ctx.enter_context(tc.psum_pool(name="ps_a", bufs=LOGIT_BANKS))
         ps_dw = ctx.enter_context(tc.psum_pool(name="ps_dw", bufs=1))
 
         def f32_tile(name, shape, tag=None):
             return sb.tile(shape, F32, name=name, tag=tag or name, align_bytes=64)
 
-        def bf_tile(name, tag=None):
-            return sb.tile([P, K_PASS * PACK], BF16, name=name, tag=tag or name, align_bytes=64)
+        def bf16_tile(name):
+            return sb.tile([P, K_PASS * PACK], BF16, name=name, align_bytes=64)
 
         def mx_tiles(name):
             return (sb.tile([P, K_PASS], U32, name=name + "_codes", align_bytes=64),
                     sb.tile([P, K_PASS], U8, name=name + "_scales", align_bytes=64))
 
-        offsets = sb.tile([P, N // 16], U16, name="offsets")
-        wt_sb = f32_tile("wt_sb", [P, PASSES, PACK])
-        warm = f32_tile("warm", [P, 8])
+        def quantize(mx, src, fmt, word0, word1):
+            nc.vector.quantize_mx(out=mx[0][:, word0:word1].bitcast(fmt), scales=mx[1][:, word0:word1],
+                                  in_=src[:, PACK * word0:PACK * word1])
+
+        offsets = sb.tile([P, LIST_COLS], U16, name="offsets")
+        wt_sb = f32_tile("wt_sb", [P, GROUPS, PACK])
         table = [f32_tile("table%d" % t, [P, T]) for t in range(PACK)]
-        result = [f32_tile("result%d" % t, [P, T]) for t in range(PACK - 1)]
-        x_raw = [f32_tile("x_raw%d" % g, [P, PACK, K_PASS]) for g in range(PASSES)]
-        y_raw = [f32_tile("y_raw%d" % g, [P, PACK, N]) for g in range(PASSES)]
-        m_raw = [f32_tile("m_raw%d" % g, [P, PACK, D]) for g in range(PASSES)]
+        result = [f32_tile("result%d" % t, [P, T]) for t in range(LAST)]
+        x_raw = [f32_tile("x_raw%d" % u, [P, PACK, K_PASS]) for u in range(GROUPS)]
+        y_raw = [f32_tile("y_raw%d" % u, [P, PACK, N]) for u in range(GROUPS)]
+        xm_raw = [f32_tile("xm_raw%d" % u, [P, PACK, D]) for u in range(GROUPS)]
 
-        w_rows = wT.rearrange("(p t) c -> p t c", t=PACK)
-        out_rows = out.rearrange("(p t) c -> p t c", t=PACK)
-        x_rows = xT[0].rearrange("(p t) r -> p t r", t=PACK)
-        y_rows = y[0].rearrange("(g p j) i -> g p j i", g=PASSES, j=PACK)
-        m_rows = xm[0].rearrange("(g p j) d -> g p j d", g=PASSES, j=PACK)
+        table_hbm = wT.rearrange("(p t) c -> p t c", t=PACK)
+        out_hbm = out.rearrange("(p t) c -> p t c", t=PACK)
+        x_hbm = xT[0].rearrange("(p t) r -> p t r", t=PACK)
+        y_hbm = y[0].rearrange("(u p j) i -> u p j i", u=GROUPS, j=PACK)
+        xm_hbm = xm[0].rearrange("(u p j) d -> u p j d", u=GROUPS, j=PACK)
 
-        nc.sync.dma_start(table[0][:], w_rows[:, 0, :])
+        nc.sync.dma_start(table[0][:], table_hbm[:, 0, :])
         nc.sync.dma_start(offsets[:], offs)
-        nc.sync.dma_start(wt_sb[:], wt[0].rearrange("(g p j) one -> p g (j one)", g=PASSES, j=PACK))
+        nc.sync.dma_start(wt_sb[:], wt[0].rearrange("(u p j) one -> p u (j one)", u=GROUPS, j=PACK))
         for t in range(1, PACK):
-            nc.sync.dma_start(table[t][:], w_rows[:, t, :])
-        nc.sync.dma_start(x_raw[0][:], x_rows[:, :, 0 * K_PASS:(0 + 1) * K_PASS])
-        nc.sync.dma_start(x_raw[1][:], x_rows[:, :, 1 * K_PASS:(1 + 1) * K_PASS])
-        for h in range(2):
-            nc.sync.dma_start(y_raw[0][:, 2 * h:2 * h + 2, :], y_rows[0][:, 2 * h:2 * h + 2, :])
-        for h in range(2):
-            nc.sync.dma_start(y_raw[1][:, 2 * h:2 * h + 2, :], y_rows[1][:, 2 * h:2 * h + 2, :])
-        nc.sync.dma_start(m_raw[0][:], m_rows[0])
-        nc.sync.dma_start(m_raw[1][:], m_rows[1])
-
-        nc.gpsimd.memset(warm[:], 0.0)
-        nc.scalar.activation(warm[:], warm[:], ACT.Sigmoid)
-
-        def interleave(dst, src, on_scalar):
-            d4 = dst[:].rearrange("p (c i t) -> p c t i", i=4, t=PACK)
-            s4 = src[:].rearrange("p t (c i) -> p c t i", i=4)
-            if on_scalar > 0:
-                nc.scalar.copy(d4[:, :on_scalar], s4[:, :on_scalar])
-            if on_scalar < P:
-                nc.vector.tensor_copy(d4[:, on_scalar:], s4[:, on_scalar:])
-
-        def interleave_permuted(engine_copy, dst, src, a0, a1):
-            engine_copy(
-                dst[:].rearrange("p (a m k) -> p m k a", a=PACK, k=PACK)[:, :, :, a0:a1],
-                src[:].rearrange("p k (m a) -> p m k a", a=PACK)[:, :, :, a0:a1])
-
-        def interleave_xm(dst, g, h, m0, m1):
-            nc.scalar.copy(
-                dst[:].rearrange("p (g a m k) -> p g m k a", g=PASSES, a=2, k=PACK)[:, g, m0:m1],
-                m_raw[g][:].rearrange("p k (m a) -> p m k a", a=PACK)[:, m0:m1, :, 2 * h:2 * h + 2])
-
-        def quantize(mx, src, fmt, c0, c1):
-            nc.vector.quantize_mx(out=mx[0][:, c0:c1].bitcast(fmt), scales=mx[1][:, c0:c1],
-                                  in_=src[:, PACK * c0:PACK * c1])
+            nc.sync.dma_start(table[t][:], table_hbm[:, t, :])
+        for u in range(GROUPS):
+            nc.sync.dma_start(x_raw[u][:], x_hbm[:, :, u * K_PASS:(u + 1) * K_PASS])
+        for u in range(GROUPS):
+            for j0 in (0, 2):
+                nc.sync.dma_start(y_raw[u][:, j0:j0 + 2, :], y_hbm[u][:, j0:j0 + 2, :])
+        for u in range(GROUPS):
+            nc.sync.dma_start(xm_raw[u][:], xm_hbm[u])
 
         w_picked = f32_tile("w_picked", [P, PACK, N])
-        w_decayed = [f32_tile("w_decayed%d" % t, [P, N]) for t in range(PACK - 1)]
-        for t in range(PACK):
-            if t == PACK - 1:
-                for h in range(2):
-                    nc.vector.tensor_copy(w_picked[:, t, 256 * h:256 * h + 256], table[t][:].indirect(offsets[:, 16 * h:16 * h + 16]))
-            else:
-                nc.vector.tensor_copy(w_picked[:, t, :], table[t][:].indirect(offsets[:]))
-                nc.scalar.activation(result[t][:], table[t][:], ACT.Copy)
-                nc.vector.tensor_scalar(w_decayed[t][:], w_picked[:, t, :], 1.0 - LR * WD, None, ALU.mult)
-        w_bf = bf_tile("w_bf")
-        interleave(w_bf, w_picked, W_ON_SCALAR)
+        w_decayed = [f32_tile("w_decayed%d" % t, [P, N]) for t in range(LAST)]
+        for t in range(LAST):
+            nc.vector.tensor_copy(w_picked[:, t, :], table[t][:].indirect(offsets[:]))
+            nc.scalar.activation(result[t][:], table[t][:], ACT.Copy)
+            nc.vector.tensor_scalar(w_decayed[t][:], w_picked[:, t, :], 1.0 - LR * WD, None, ALU.mult)
+        for h in range(2):
+            entries = slice(h * N // 2, (h + 1) * N // 2)
+            list_cols = slice(h * LIST_COLS // 2, (h + 1) * LIST_COLS // 2)
+            nc.vector.tensor_copy(w_picked[:, LAST, entries], table[LAST][:].indirect(offsets[:, list_cols]))
+
+        w_bf = bf16_tile("w_bf")
+        w_dst = w_bf[:].rearrange("p (c i t) -> p c t i", i=RUN, t=PACK)
+        w_src = w_picked[:].rearrange("p t (c i) -> p c t i", i=RUN)
+        half_runs = N // RUN // 2
+        nc.scalar.copy(w_dst[:, :half_runs], w_src[:, :half_runs])
+        nc.vector.tensor_copy(w_dst[:, half_runs:], w_src[:, half_runs:])
         w_mx = mx_tiles("w")
         quantize(w_mx, w_bf, E4M3, 0, N)
 
-        x_mx = [mx_tiles("x%d" % g) for g in range(PASSES)]
-        err = [f32_tile("err%d" % g, [P, PACK, N]) for g in range(PASSES)]
-        g_bf = [bf_tile("g_bf%d" % g) for g in range(PASSES)]
-        g_mx = [mx_tiles("g%d" % g) for g in range(PASSES)]
-        m_lo = bf_tile("m_lo")
-        m_mx = [mx_tiles("m_half%d" % h) for h in range(2)]
+        x_mx = [mx_tiles("x%d" % u) for u in range(GROUPS)]
+        err = [f32_tile("err%d" % u, [P, PACK, N]) for u in range(GROUPS)]
+        g_bf = [bf16_tile("g_bf%d" % u) for u in range(GROUPS)]
+        g_mx = [mx_tiles("g%d" % u) for u in range(GROUPS)]
+        xm_bf_first = bf16_tile("xm_bf_first")
+        xm_mx = [mx_tiles("xm_pair%d" % pair) for pair in range(2)]
         dw = [ps_dw.tile([P, N], F32, name="dw%d" % t) for t in range(PACK)]
 
-        for g in range(PASSES):
-            x_bf = bf_tile("x_bf")
-            if X_ON_SCALAR[g]:
-                interleave_permuted(nc.vector.tensor_copy, x_bf, x_raw[g], 0, 2)
-                interleave_permuted(nc.scalar.copy, x_bf, x_raw[g], 2, PACK)
-                quantize(x_mx[g], x_bf, E4M3, 0, 2 * P)
-                quantize(x_mx[g], x_bf, E4M3, 2 * P, 4 * P)
+        def interleave_x(copy, dst, u, j0, j1):
+            copy(dst[:].rearrange("p (j m t) -> p m t j", j=PACK, t=PACK)[:, :, :, j0:j1],
+                 x_raw[u][:].rearrange("p t (m j) -> p m t j", j=PACK)[:, :, :, j0:j1])
+
+        for u in range(GROUPS):
+            x_bf = bf16_tile("x_bf")
+            if u == 0:
+                interleave_x(nc.vector.tensor_copy, x_bf, u, 0, 2)
+                interleave_x(nc.scalar.copy, x_bf, u, 2, PACK)
+                quantize(x_mx[u], x_bf, E4M3, 0, 2 * P)
+                quantize(x_mx[u], x_bf, E4M3, 2 * P, PACK * P)
             else:
-                interleave_permuted(nc.vector.tensor_copy, x_bf, x_raw[g], 0, PACK)
-                quantize(x_mx[g], x_bf, E4M3, 0, K_PASS)
+                interleave_x(nc.vector.tensor_copy, x_bf, u, 0, PACK)
+                quantize(x_mx[u], x_bf, E4M3, 0, K_PASS)
             for j in range(PACK):
-                cols = slice(j * P, (j + 1) * P)
+                words = slice(j * P, (j + 1) * P)
                 logits = ps_a.tile([P, N], F32, name="logits")
                 nc.tensor.matmul_mx(
                     out=logits[:],
-                    lhsT=x_mx[g][0][:, cols].bitcast(E4M3), lhsT_scale=x_mx[g][1][:, cols],
+                    lhsT=x_mx[u][0][:, words].bitcast(E4M3), lhsT_scale=x_mx[u][1][:, words],
                     rhs=w_mx[0][:].bitcast(E4M3), rhs_scale=w_mx[1][:],
                     start=True, stop=True)
-                nc.scalar.activation(err[g][:, j, :], logits[:], ACT.Sigmoid)
+                nc.scalar.activation(err[u][:, j, :], logits[:], ACT.Sigmoid)
 
-        def grad_matmul(g, t):
-            c0 = (2 * g + t % 2) * P
-            cols = slice(c0, c0 + P)
+        def interleave_xm(dst, u, pair, m0, m1):
+            nc.scalar.copy(
+                dst[:].rearrange("p (u e m j) -> p u m j e", u=GROUPS, e=2, j=PACK)[:, u, m0:m1],
+                xm_raw[u][:].rearrange("p j (m t) -> p m j t", t=PACK)[:, m0:m1, :, 2 * pair:2 * pair + 2])
+
+        def gradient_matmul(u, t):
+            word0 = (2 * u + t % 2) * P
+            words = slice(word0, word0 + P)
             nc.tensor.matmul_mx(
                 out=dw[t][:],
-                lhsT=m_mx[t // 2][0][:, cols].bitcast(E4M3), lhsT_scale=m_mx[t // 2][1][:, cols],
-                rhs=g_mx[g][0][:].bitcast(E5M2), rhs_scale=g_mx[g][1][:],
-                start=(g == 0), stop=(g == PASSES - 1))
+                lhsT=xm_mx[t // 2][0][:, words].bitcast(E4M3), lhsT_scale=xm_mx[t // 2][1][:, words],
+                rhs=g_mx[u][0][:].bitcast(E5M2), rhs_scale=g_mx[u][1][:],
+                start=(u == 0), stop=(u == GROUPS - 1))
 
-        for g in range(PASSES):
-            g4 = g_bf[g][:].rearrange("p (c i j) -> p c j i", i=4, j=PACK)
-            e4 = err[g][:].rearrange("p j (c i) -> p c j i", i=4)
-            if FUSED[g]:
-                for h in range(4):
-                    js = slice(h, h + 1)
-                    nc.vector.tensor_tensor(err[g][:, js, :], err[g][:, js, :], y_raw[g][:, js, :], ALU.subtract)
-                nc.vector.tensor_tensor(
-                    g4, e4, wt_sb[:, g, :].unsqueeze(1).unsqueeze(3).to_broadcast([P, N // 4, PACK, 4]), ALU.mult)
-            else:
-                for j in range(PACK):
-                    nc.scalar.activation(err[g][:, j, :], err[g][:, j, :], ACT.Copy, scale=wt_sb[:, g, j:j + 1])
-                    nc.vector.tensor_scalar(y_raw[g][:, j, :], y_raw[g][:, j, :], wt_sb[:, g, j:j + 1], None, ALU.mult)
-                nc.vector.tensor_tensor(g4, e4, y_raw[g][:].rearrange("p j (c i) -> p c j i", i=4), ALU.subtract)
-            for h in range(2):
-                interleave_xm(m_lo, g, 0, 64 * h, 64 * h + 64)
-            quantize(m_mx[0], m_lo, E4M3, 2 * P * g, 2 * P * (g + 1))
-            quantize(g_mx[g], g_bf[g], E5M2, 0, N)
+        for u in range(GROUPS):
+            for j in range(PACK):
+                nc.vector.tensor_tensor(err[u][:, j:j + 1, :], err[u][:, j:j + 1, :], y_raw[u][:, j:j + 1, :],
+                                        ALU.subtract)
+            nc.vector.tensor_tensor(
+                g_bf[u][:].rearrange("p (c i j) -> p c j i", i=RUN, j=PACK),
+                err[u][:].rearrange("p j (c i) -> p c j i", i=RUN),
+                wt_sb[:, u, :].unsqueeze(1).unsqueeze(3).to_broadcast([P, N // RUN, PACK, RUN]),
+                ALU.mult)
+            for m0 in (0, P // 2):
+                interleave_xm(xm_bf_first, u, 0, m0, m0 + P // 2)
+            quantize(xm_mx[0], xm_bf_first, E4M3, 2 * P * u, 2 * P * (u + 1))
+            quantize(g_mx[u], g_bf[u], E5M2, 0, N)
             for t in range(2):
-                grad_matmul(g, t)
+                gradient_matmul(u, t)
 
-        step = [f32_tile("step%d" % t, [P, N]) for t in range(PACK)]
+        step = {t: f32_tile("step%d" % t, [P, N]) for t in range(1, PACK)}
         new_cols = [f32_tile("new_cols%d" % t, [P, N]) for t in range(PACK)]
 
+        xm_bf_second = bf16_tile("xm_bf_second")
+        for u in range(GROUPS):
+            interleave_xm(xm_bf_second, u, 1, 0, P)
+        quantize(xm_mx[1], xm_bf_second, E4M3, 0, PACK * P)
+        for t in range(2, PACK):
+            for u in range(GROUPS):
+                gradient_matmul(u, t)
+
+        w_decayed.append(f32_tile("w_decayed%d" % LAST, [P, N], "x_raw1"))
+        result.append(f32_tile("result%d" % LAST, [P, T], "y_raw1"))
+        nc.scalar.activation(w_decayed[LAST][:], w_picked[:, LAST, :], ACT.Copy, scale=1.0 - LR * WD)
+        piece = T // LATE_COPY_PIECES
+        for c0 in range(0, T, piece):
+            nc.scalar.activation(result[LAST][:, c0:c0 + piece], table[LAST][:, c0:c0 + piece], ACT.Copy)
+
         def update(t):
-            if t in POOL_ADD:
+            if t == 0:
+                nc.vector.scalar_tensor_tensor(new_cols[t][:], dw[t][:], -LR, w_decayed[t][:], ALU.mult, ALU.add)
+            else:
                 nc.scalar.activation(step[t][:], dw[t][:], ACT.Copy, scale=-LR)
                 nc.gpsimd.tensor_tensor(new_cols[t][:], step[t][:], w_decayed[t][:], ALU.add)
-            else:
-                nc.vector.scalar_tensor_tensor(new_cols[t][:], dw[t][:], -LR, w_decayed[t][:], ALU.mult, ALU.add)
 
-        def scatter(t):
-            nc.vector.tensor_copy(result[t][:].indirect(offsets[:]), new_cols[t][:])
-            nc.sync.dma_start(out_rows[:, t, :], result[t][:])
-
-        m_hi = bf_tile("m_hi", None)
-        for g in range(PASSES):
-            interleave_xm(m_hi, g, 1, 0, P)
-        quantize(m_mx[1], m_hi, E4M3, 0, 4 * P)
-        for t in range(2, PACK):
-            for g in range(PASSES):
-                grad_matmul(g, t)
-        last = PACK - 1
-        w_decayed.append(f32_tile("w_decayed3", [P, N], "x_raw1"))
-        result.append(f32_tile("result3", [P, T], "y_raw1"))
-        nc.scalar.activation(w_decayed[last][:], w_picked[:, last, :], ACT.Copy, scale=1.0 - LR * WD)
-        for q in range(4):
-            nc.scalar.activation(result[last][:, q * 512:(q + 1) * 512], table[last][:, q * 512:(q + 1) * 512], ACT.Copy)
         update(0)
         for t in range(PACK):
-            if t + 1 < PACK:
+            if t < LAST:
                 update(t + 1)
-            scatter(t)
+            nc.vector.tensor_copy(result[t][:].indirect(offsets[:]), new_cols[t][:])
+            nc.sync.dma_start(out_hbm[:, t, :], result[t][:])

@@ -25,6 +25,7 @@ RUN = 4
 LIST_COLS = N // 16
 LOGIT_BANKS = 4
 LATE_COPY_PIECES = 4
+FUSED_SLOTS = 384
 
 
 def tile_attend_gnce_sgd_kernel(tc, xT, wT, y, wt, xm, offs, out):
@@ -37,8 +38,8 @@ def tile_attend_gnce_sgd_kernel(tc, xT, wT, y, wt, xm, offs, out):
         def f32_tile(name, shape, tag=None):
             return sb.tile(shape, F32, name=name, tag=tag or name, align_bytes=64)
 
-        def bf16_tile(name):
-            return sb.tile([P, K_PASS * PACK], BF16, name=name, align_bytes=64)
+        def bf16_tile(name, tag=None, words=K_PASS):
+            return sb.tile([P, words * PACK], BF16, name=name, tag=tag or name, align_bytes=64)
 
         def mx_tiles(name):
             return (sb.tile([P, K_PASS], U32, name=name + "_codes", align_bytes=64),
@@ -64,11 +65,11 @@ def tile_attend_gnce_sgd_kernel(tc, xT, wT, y, wt, xm, offs, out):
 
         nc.sync.dma_start(table[0][:], table_hbm[:, 0, :])
         nc.sync.dma_start(offsets[:], offs)
-        nc.sync.dma_start(wt_sb[:], wt[0].rearrange("(u p j) one -> p u (j one)", u=GROUPS, j=PACK))
         for t in range(1, PACK):
             nc.sync.dma_start(table[t][:], table_hbm[:, t, :])
         for u in range(GROUPS):
             nc.sync.dma_start(x_raw[u][:], x_hbm[:, :, u * K_PASS:(u + 1) * K_PASS])
+        nc.sync.dma_start(wt_sb[:], wt[0].rearrange("(u p j) one -> p u (j one)", u=GROUPS, j=PACK))
         for u in range(GROUPS):
             for j0 in (0, 2):
                 nc.sync.dma_start(y_raw[u][:, j0:j0 + 2, :], y_hbm[u][:, j0:j0 + 2, :])
@@ -96,10 +97,12 @@ def tile_attend_gnce_sgd_kernel(tc, xT, wT, y, wt, xm, offs, out):
         quantize(w_mx, w_bf, E4M3, 0, N)
 
         x_mx = [mx_tiles("x%d" % u) for u in range(GROUPS)]
+        sig = [[f32_tile("sig%d%d" % (u, j), [P, N]) for j in range(PACK)] for u in range(GROUPS)]
         err = [f32_tile("err%d" % u, [P, PACK, N]) for u in range(GROUPS)]
-        g_bf = [bf16_tile("g_bf%d" % u) for u in range(GROUPS)]
+        g_bf = [bf16_tile("g_bf0", "sig12"), bf16_tile("g_bf1")]
         g_mx = [mx_tiles("g%d" % u) for u in range(GROUPS)]
-        xm_bf_first = bf16_tile("xm_bf_first")
+        xm_bf_first = bf16_tile("xm_bf_first", "y_raw0")
+        xm_bf_second = [bf16_tile("xm_bf_second0", "y_raw0", 2 * P), bf16_tile("xm_bf_second1", None, 2 * P)]
         xm_mx = [mx_tiles("xm_pair%d" % pair) for pair in range(2)]
         dw = [ps_dw.tile([P, N], F32, name="dw%d" % t) for t in range(PACK)]
 
@@ -115,8 +118,10 @@ def tile_attend_gnce_sgd_kernel(tc, xT, wT, y, wt, xm, offs, out):
                 quantize(x_mx[u], x_bf, E4M3, 0, 2 * P)
                 quantize(x_mx[u], x_bf, E4M3, 2 * P, PACK * P)
             else:
-                interleave_x(nc.vector.tensor_copy, x_bf, u, 0, PACK)
-                quantize(x_mx[u], x_bf, E4M3, 0, K_PASS)
+                interleave_x(nc.vector.tensor_copy, x_bf, u, 0, 2)
+                interleave_x(nc.vector.tensor_copy, x_bf, u, 2, PACK)
+                quantize(x_mx[u], x_bf, E4M3, 0, 2 * P)
+                quantize(x_mx[u], x_bf, E4M3, 2 * P, PACK * P)
             for j in range(PACK):
                 words = slice(j * P, (j + 1) * P)
                 logits = ps_a.tile([P, N], F32, name="logits")
@@ -125,66 +130,78 @@ def tile_attend_gnce_sgd_kernel(tc, xT, wT, y, wt, xm, offs, out):
                     lhsT=x_mx[u][0][:, words].bitcast(E4M3), lhsT_scale=x_mx[u][1][:, words],
                     rhs=w_mx[0][:].bitcast(E4M3), rhs_scale=w_mx[1][:],
                     start=True, stop=True)
-                nc.scalar.activation(err[u][:, j, :], logits[:], ACT.Sigmoid)
+                nc.scalar.activation(sig[u][j][:], logits[:], ACT.Sigmoid)
 
-        def interleave_xm(dst, u, pair, m0, m1):
-            nc.scalar.copy(
-                dst[:].rearrange("p (u e m j) -> p u m j e", u=GROUPS, e=2, j=PACK)[:, u, m0:m1],
-                xm_raw[u][:].rearrange("p j (m t) -> p m j t", t=PACK)[:, m0:m1, :, 2 * pair:2 * pair + 2])
+        def xm_rows(u, pair):
+            return xm_raw[u][:].rearrange("p j (m t) -> p m j t", t=PACK)[:, :, :, 2 * pair:2 * pair + 2]
+
+        def xm_words(u, t):
+            word0 = (2 * (t % 2) + u) * P if t < 2 else (2 * u + t % 2) * P
+            return slice(word0, word0 + P)
 
         def gradient_matmul(u, t):
-            word0 = (2 * u + t % 2) * P
-            words = slice(word0, word0 + P)
+            words = xm_words(u, t)
             nc.tensor.matmul_mx(
                 out=dw[t][:],
                 lhsT=xm_mx[t // 2][0][:, words].bitcast(E4M3), lhsT_scale=xm_mx[t // 2][1][:, words],
                 rhs=g_mx[u][0][:].bitcast(E5M2), rhs_scale=g_mx[u][1][:],
                 start=(u == 0), stop=(u == GROUPS - 1))
 
+        def g_words(u, slots):
+            return g_bf[u][:, PACK * slots.start:PACK * slots.stop].rearrange("p (c i j) -> p c j i", i=RUN, j=PACK)
+
+        def in_runs(src):
+            return src.rearrange("p j (c i) -> p c j i", i=RUN)
+
         for u in range(GROUPS):
             for j in range(PACK):
-                nc.vector.tensor_tensor(err[u][:, j:j + 1, :], err[u][:, j:j + 1, :], y_raw[u][:, j:j + 1, :],
-                                        ALU.subtract)
-            nc.vector.tensor_tensor(
-                g_bf[u][:].rearrange("p (c i j) -> p c j i", i=RUN, j=PACK),
-                err[u][:].rearrange("p j (c i) -> p c j i", i=RUN),
-                wt_sb[:, u, :].unsqueeze(1).unsqueeze(3).to_broadcast([P, N // RUN, PACK, RUN]),
-                ALU.mult)
-            for m0 in (0, P // 2):
-                interleave_xm(xm_bf_first, u, 0, m0, m0 + P // 2)
-            quantize(xm_mx[0], xm_bf_first, E4M3, 2 * P * u, 2 * P * (u + 1))
-            quantize(g_mx[u], g_bf[u], E5M2, 0, N)
-            for t in range(2):
-                gradient_matmul(u, t)
+                nc.vector.tensor_tensor(err[u][:, j, :], sig[u][j][:], y_raw[u][:, j, :], ALU.subtract)
 
-        step = {t: f32_tile("step%d" % t, [P, N]) for t in range(1, PACK)}
-        new_cols = [f32_tile("new_cols%d" % t, [P, N]) for t in range(PACK)]
-
-        xm_bf_second = bf16_tile("xm_bf_second")
+        fused, apart = slice(0, FUSED_SLOTS), slice(FUSED_SLOTS, N)
+        weighted = [f32_tile("weighted0", [P, PACK, N - FUSED_SLOTS]), f32_tile("weighted1", [P, PACK, N])]
+        for u, slots in ((0, apart), (1, slice(0, N))):
+            for j in range(PACK):
+                nc.scalar.activation(weighted[u][:, j, :], err[u][:, j, slots], ACT.Copy, scale=wt_sb[:, u, j:j + 1])
+        first_dst = xm_bf_first[:].rearrange("p (e u m j) -> p u m j e", u=GROUPS, e=2, j=PACK)
         for u in range(GROUPS):
-            interleave_xm(xm_bf_second, u, 1, 0, P)
-        quantize(xm_mx[1], xm_bf_second, E4M3, 0, PACK * P)
+            nc.scalar.copy(first_dst[:, u], xm_rows(u, 0))
+
+        nc.vector.tensor_copy(g_words(0, apart), in_runs(weighted[0][:]))
+        nc.vector.tensor_tensor(
+            g_words(0, fused), in_runs(err[0][:, :, fused]),
+            wt_sb[:, 0, :].unsqueeze(1).unsqueeze(3).to_broadcast([P, FUSED_SLOTS // RUN, PACK, RUN]),
+            ALU.mult)
+        nc.vector.tensor_copy(g_words(1, slice(0, N)), in_runs(weighted[1][:]))
+        for u in range(GROUPS):
+            quantize(g_mx[u], g_bf[u], E5M2, 0, N)
+            quantize(xm_mx[0], xm_bf_first, E4M3, u * P, (u + 1) * P)
+            gradient_matmul(u, 0)
+        quantize(xm_mx[0], xm_bf_first, E4M3, 2 * P, 4 * P)
+        for u in range(GROUPS):
+            gradient_matmul(u, 1)
+
+        for u, copy in ((1, nc.scalar.copy), (0, nc.vector.tensor_copy)):
+            copy(xm_bf_second[u][:].rearrange("p (e m j) -> p m j e", e=2, j=PACK), xm_rows(u, 1))
+        for u in reversed(range(GROUPS)):
+            words = slice(2 * P * u, 2 * P * (u + 1))
+            nc.vector.quantize_mx(out=xm_mx[1][0][:, words].bitcast(E4M3), scales=xm_mx[1][1][:, words],
+                                  in_=xm_bf_second[u][:])
         for t in range(2, PACK):
             for u in range(GROUPS):
                 gradient_matmul(u, t)
 
-        w_decayed.append(f32_tile("w_decayed%d" % LAST, [P, N], "x_raw1"))
-        result.append(f32_tile("result%d" % LAST, [P, T], "y_raw1"))
+        def update(t):
+            step = f32_tile("step%d" % t, [P, N])
+            nc.scalar.activation(step[:], dw[t][:], ACT.Copy, scale=-LR)
+            nc.vector.tensor_tensor(result[t][:].indirect(offsets[:]), step[:], w_decayed[t][:], ALU.add)
+            nc.sync.dma_start(out_hbm[:, t, :], result[t][:])
+
+        for t in range(LAST):
+            update(t)
+        w_decayed.append(f32_tile("w_decayed%d" % LAST, [P, N], "xm_raw1"))
         nc.scalar.activation(w_decayed[LAST][:], w_picked[:, LAST, :], ACT.Copy, scale=1.0 - LR * WD)
+        result.append(f32_tile("result%d" % LAST, [P, T], "xm_raw0"))
         piece = T // LATE_COPY_PIECES
         for c0 in range(0, T, piece):
             nc.scalar.activation(result[LAST][:, c0:c0 + piece], table[LAST][:, c0:c0 + piece], ACT.Copy)
-
-        def update(t):
-            if t == 0:
-                nc.vector.scalar_tensor_tensor(new_cols[t][:], dw[t][:], -LR, w_decayed[t][:], ALU.mult, ALU.add)
-            else:
-                nc.scalar.activation(step[t][:], dw[t][:], ACT.Copy, scale=-LR)
-                nc.gpsimd.tensor_tensor(new_cols[t][:], step[t][:], w_decayed[t][:], ALU.add)
-
-        update(0)
-        for t in range(PACK):
-            if t < LAST:
-                update(t + 1)
-            nc.vector.tensor_copy(result[t][:].indirect(offsets[:]), new_cols[t][:])
-            nc.sync.dma_start(out_hbm[:, t, :], result[t][:])
+        update(LAST)

@@ -53,7 +53,7 @@ def tile_attend_gnce_sgd_kernel(tc, xT, wT, y, wt, xm, offs, out):
         wt_sb = f32_tile("wt_sb", [P, GROUPS, PACK])
         table = [f32_tile("table%d" % t, [P, T]) for t in range(PACK)]
         result = [f32_tile("result%d" % t, [P, T]) for t in range(LAST)]
-        x_raw = [f32_tile("x_raw%d" % u, [P, PACK, K_PASS]) for u in range(GROUPS)]
+        x_raw = [[f32_tile("x_raw%d%d" % (u, h), [P, PACK, K_PASS // 2]) for h in range(2)] for u in range(GROUPS)]
         y_raw = [f32_tile("y_raw%d" % u, [P, PACK, N]) for u in range(GROUPS)]
         xm_raw = [f32_tile("xm_raw%d" % u, [P, PACK, D]) for u in range(GROUPS)]
 
@@ -68,7 +68,9 @@ def tile_attend_gnce_sgd_kernel(tc, xT, wT, y, wt, xm, offs, out):
         for t in range(1, PACK):
             nc.sync.dma_start(table[t][:], table_hbm[:, t, :])
         for u in range(GROUPS):
-            nc.sync.dma_start(x_raw[u][:], x_hbm[:, :, u * K_PASS:(u + 1) * K_PASS])
+            for h in range(2):
+                row0 = u * K_PASS + h * K_PASS // 2
+                nc.sync.dma_start(x_raw[u][h][:], x_hbm[:, :, row0:row0 + K_PASS // 2])
         nc.sync.dma_start(wt_sb[:], wt[0].rearrange("(u p j) one -> p u (j one)", u=GROUPS, j=PACK))
         for u in range(GROUPS):
             for j0 in (0, 2):
@@ -91,10 +93,11 @@ def tile_attend_gnce_sgd_kernel(tc, xT, wT, y, wt, xm, offs, out):
         w_dst = w_bf[:].rearrange("p (c i t) -> p c t i", i=RUN, t=PACK)
         w_src = w_picked[:].rearrange("p t (c i) -> p c t i", i=RUN)
         half_runs = N // RUN // 2
-        nc.scalar.copy(w_dst[:, :half_runs], w_src[:, :half_runs])
+        nc.vector.tensor_copy(w_dst[:, :half_runs], w_src[:, :half_runs])
         nc.vector.tensor_copy(w_dst[:, half_runs:], w_src[:, half_runs:])
         w_mx = mx_tiles("w")
-        quantize(w_mx, w_bf, E4M3, 0, N)
+        quantize(w_mx, w_bf, E4M3, 0, N // 2)
+        quantize(w_mx, w_bf, E4M3, N // 2, N)
 
         x_mx = [mx_tiles("x%d" % u) for u in range(GROUPS)]
         sig = [[f32_tile("sig%d%d" % (u, j), [P, N]) for j in range(PACK)] for u in range(GROUPS)]
@@ -106,22 +109,18 @@ def tile_attend_gnce_sgd_kernel(tc, xT, wT, y, wt, xm, offs, out):
         xm_mx = [mx_tiles("xm_pair%d" % pair) for pair in range(2)]
         dw = [ps_dw.tile([P, N], F32, name="dw%d" % t) for t in range(PACK)]
 
-        def interleave_x(copy, dst, u, j0, j1):
-            copy(dst[:].rearrange("p (j m t) -> p m t j", j=PACK, t=PACK)[:, :, :, j0:j1],
-                 x_raw[u][:].rearrange("p t (m j) -> p m t j", j=PACK)[:, :, :, j0:j1])
+        def interleave_x(copy, dst, u, h, j0, j1):
+            copy(dst[:].rearrange("p (j h m t) -> p h m t j", j=PACK, h=2, t=PACK)[:, h, :, :, j0:j1],
+                 x_raw[u][h][:].rearrange("p t (m j) -> p m t j", j=PACK)[:, :, :, j0:j1])
 
         for u in range(GROUPS):
-            x_bf = bf16_tile("x_bf")
-            if u == 0:
-                interleave_x(nc.vector.tensor_copy, x_bf, u, 0, 2)
-                interleave_x(nc.scalar.copy, x_bf, u, 2, PACK)
-                quantize(x_mx[u], x_bf, E4M3, 0, 2 * P)
-                quantize(x_mx[u], x_bf, E4M3, 2 * P, PACK * P)
-            else:
-                interleave_x(nc.vector.tensor_copy, x_bf, u, 0, 2)
-                interleave_x(nc.vector.tensor_copy, x_bf, u, 2, PACK)
-                quantize(x_mx[u], x_bf, E4M3, 0, 2 * P)
-                quantize(x_mx[u], x_bf, E4M3, 2 * P, PACK * P)
+            x_bf = bf16_tile("x_bf%d" % u)
+            interleave_x(nc.scalar.copy, x_bf, u, 0, 0, PACK)
+            late_copy = nc.scalar.copy if u == 0 else nc.vector.tensor_copy
+            interleave_x(late_copy, x_bf, u, 1, 0, 2)
+            interleave_x(late_copy, x_bf, u, 1, 2, PACK)
+            quantize(x_mx[u], x_bf, E4M3, 0, 2 * P)
+            quantize(x_mx[u], x_bf, E4M3, 2 * P, PACK * P)
             for j in range(PACK):
                 words = slice(j * P, (j + 1) * P)
                 logits = ps_a.tile([P, N], F32, name="logits")

@@ -78,6 +78,10 @@ def tile_attend_gnce_sgd_kernel(tc, xT, wT, y, wt, xm, offs, out):
         for u in range(GROUPS):
             nc.sync.dma_start(xm_raw[u][:], xm_hbm[u])
 
+        warm = f32_tile("warm", [P, 2])
+        nc.vector.memset(warm[:, 0:1], 0.0)
+        nc.scalar.activation(warm[:, 1:2], warm[:, 0:1], ACT.Sigmoid)
+
         w_picked = f32_tile("w_picked", [P, PACK, N])
         w_decayed = [f32_tile("w_decayed%d" % t, [P, N]) for t in range(LAST)]
         for t in range(LAST):

@@ -25,7 +25,7 @@ RUN = 4
 LIST_COLS = N // 16
 LOGIT_BANKS = 4
 LATE_COPY_PIECES = 4
-FUSED_SLOTS = 384
+FUSED_SLOTS = 352
 
 
 def tile_attend_gnce_sgd_kernel(tc, xT, wT, y, wt, xm, offs, out):
@@ -55,7 +55,8 @@ def tile_attend_gnce_sgd_kernel(tc, xT, wT, y, wt, xm, offs, out):
         result = [f32_tile("result%d" % t, [P, T]) for t in range(LAST)]
         x_raw = [[f32_tile("x_raw%d%d" % (u, h), [P, PACK, K_PASS // 2]) for h in range(2)] for u in range(GROUPS)]
         y_raw = [f32_tile("y_raw%d" % u, [P, PACK, N]) for u in range(GROUPS)]
-        xm_raw = [f32_tile("xm_raw%d" % u, [P, PACK, D]) for u in range(GROUPS)]
+        xm_raw = [[f32_tile("xm_raw0", [P, PACK, D])],
+                  [f32_tile("xm_raw1%d" % h, [P, PACK, D // 2]) for h in range(2)]]
 
         table_hbm = wT.rearrange("(p t) c -> p t c", t=PACK)
         out_hbm = out.rearrange("(p t) c -> p t c", t=PACK)
@@ -75,8 +76,9 @@ def tile_attend_gnce_sgd_kernel(tc, xT, wT, y, wt, xm, offs, out):
         for u in range(GROUPS):
             for j0 in (0, 2):
                 nc.sync.dma_start(y_raw[u][:, j0:j0 + 2, :], y_hbm[u][:, j0:j0 + 2, :])
-        for u in range(GROUPS):
-            nc.sync.dma_start(xm_raw[u][:], xm_hbm[u])
+        nc.sync.dma_start(xm_raw[0][0][:], xm_hbm[0])
+        for h in range(2):
+            nc.sync.dma_start(xm_raw[1][h][:], xm_hbm[1][:, :, h * D // 2:(h + 1) * D // 2])
 
         warm = f32_tile("warm", [P, 2])
         nc.vector.memset(warm[:, 0:1], 0.0)
@@ -109,7 +111,7 @@ def tile_attend_gnce_sgd_kernel(tc, xT, wT, y, wt, xm, offs, out):
         g_bf = [bf16_tile("g_bf0", "sig12"), bf16_tile("g_bf1")]
         g_mx = [mx_tiles("g%d" % u) for u in range(GROUPS)]
         xm_bf_first = bf16_tile("xm_bf_first", "y_raw0")
-        xm_bf_second = [bf16_tile("xm_bf_second0", "y_raw0", 2 * P), bf16_tile("xm_bf_second1", None, 2 * P)]
+        xm_bf_second = [bf16_tile("xm_bf_second0", "y_raw0", 2 * P), bf16_tile("xm_bf_second1", "g_bf1", 2 * P)]
         xm_mx = [mx_tiles("xm_pair%d" % pair) for pair in range(2)]
         dw = [ps_dw.tile([P, N], F32, name="dw%d" % t) for t in range(PACK)]
 
@@ -135,8 +137,11 @@ def tile_attend_gnce_sgd_kernel(tc, xT, wT, y, wt, xm, offs, out):
                     start=True, stop=True)
                 nc.scalar.activation(sig[u][j][:], logits[:], ACT.Sigmoid)
 
-        def xm_rows(u, pair):
-            return xm_raw[u][:].rearrange("p j (m t) -> p m j t", t=PACK)[:, :, :, 2 * pair:2 * pair + 2]
+        def interleave_xm(copy, dst, u, pair):
+            share = P // len(xm_raw[u])
+            for h, raw in enumerate(xm_raw[u]):
+                copy(dst[:, h * share:(h + 1) * share],
+                     raw[:].rearrange("p j (m t) -> p m j t", t=PACK)[:, :, :, 2 * pair:2 * pair + 2])
 
         def xm_words(u, t):
             word0 = (2 * (t % 2) + u) * P if t < 2 else (2 * u + t % 2) * P
@@ -167,7 +172,7 @@ def tile_attend_gnce_sgd_kernel(tc, xT, wT, y, wt, xm, offs, out):
                 nc.scalar.activation(weighted[u][:, j, :], err[u][:, j, slots], ACT.Copy, scale=wt_sb[:, u, j:j + 1])
         first_dst = xm_bf_first[:].rearrange("p (e u m j) -> p u m j e", u=GROUPS, e=2, j=PACK)
         for u in range(GROUPS):
-            nc.scalar.copy(first_dst[:, u], xm_rows(u, 0))
+            interleave_xm(nc.scalar.copy, first_dst[:, u], u, 0)
 
         nc.vector.tensor_copy(g_words(0, apart), in_runs(weighted[0][:]))
         nc.vector.tensor_tensor(
@@ -184,8 +189,8 @@ def tile_attend_gnce_sgd_kernel(tc, xT, wT, y, wt, xm, offs, out):
             gradient_matmul(u, 1)
 
         for u, copy in ((1, nc.scalar.copy), (0, nc.vector.tensor_copy)):
-            copy(xm_bf_second[u][:].rearrange("p (e m j) -> p m j e", e=2, j=PACK), xm_rows(u, 1))
-        for u in reversed(range(GROUPS)):
+            interleave_xm(copy, xm_bf_second[u][:].rearrange("p (e m j) -> p m j e", e=2, j=PACK), u, 1)
+        for u in range(GROUPS):
             words = slice(2 * P * u, 2 * P * (u + 1))
             nc.vector.quantize_mx(out=xm_mx[1][0][:, words].bitcast(E4M3), scales=xm_mx[1][1][:, words],
                                   in_=xm_bf_second[u][:])
@@ -201,7 +206,7 @@ def tile_attend_gnce_sgd_kernel(tc, xT, wT, y, wt, xm, offs, out):
 
         for t in range(LAST):
             update(t)
-        w_decayed.append(f32_tile("w_decayed%d" % LAST, [P, N], "xm_raw1"))
+        w_decayed.append(f32_tile("w_decayed%d" % LAST, [P, N], "xm_raw11"))
         nc.scalar.activation(w_decayed[LAST][:], w_picked[:, LAST, :], ACT.Copy, scale=1.0 - LR * WD)
         result.append(f32_tile("result%d" % LAST, [P, T], "xm_raw0"))
         piece = T // LATE_COPY_PIECES

@@ -121,11 +121,18 @@ def tile_attend_gnce_sgd_kernel(tc, xT, wT, y, wt, xm, offs, out):
 
         for u in range(GROUPS):
             x_bf = bf16_tile("x_bf%d" % u)
-            interleave_x(nc.scalar.copy, x_bf, u, 0, 0, PACK)
-            late_copy = nc.scalar.copy if u == 0 else nc.vector.tensor_copy
-            interleave_x(late_copy, x_bf, u, 1, 0, 2)
-            interleave_x(late_copy, x_bf, u, 1, 2, PACK)
-            quantize(x_mx[u], x_bf, E4M3, 0, 2 * P)
+            if u == 0:
+                interleave_x(nc.scalar.copy, x_bf, u, 0, 0, PACK)
+                interleave_x(nc.scalar.copy, x_bf, u, 1, 0, 2)
+                interleave_x(nc.scalar.copy, x_bf, u, 1, 2, PACK)
+                quantize(x_mx[u], x_bf, E4M3, 0, P)
+                quantize(x_mx[u], x_bf, E4M3, P, 2 * P)
+            else:
+                interleave_x(nc.scalar.copy, x_bf, u, 0, 0, 2)
+                interleave_x(nc.vector.tensor_copy, x_bf, u, 0, 2, PACK)
+                interleave_x(nc.vector.tensor_copy, x_bf, u, 1, 0, 2)
+                interleave_x(nc.vector.tensor_copy, x_bf, u, 1, 2, PACK)
+                quantize(x_mx[u], x_bf, E4M3, 0, 2 * P)
             quantize(x_mx[u], x_bf, E4M3, 2 * P, PACK * P)
             for j in range(PACK):
                 words = slice(j * P, (j + 1) * P)

@@ -25,6 +25,7 @@ RUN = 4
 LIST_COLS = N // 16
 LOGIT_BANKS = 4
 LATE_COPY_PIECES = 4
+HALF = N // 2
 FUSED_SLOTS = 352
 
 
@@ -52,9 +53,10 @@ def tile_attend_gnce_sgd_kernel(tc, xT, wT, y, wt, xm, offs, out):
         offsets = sb.tile([P, LIST_COLS], U16, name="offsets")
         wt_sb = f32_tile("wt_sb", [P, GROUPS, PACK])
         table = [f32_tile("table%d" % t, [P, T]) for t in range(PACK)]
-        result = [f32_tile("result%d" % t, [P, T]) for t in range(LAST)]
+        result = [f32_tile("result%d" % t, [P, T]) for t in range(PACK)]
         x_raw = [[f32_tile("x_raw%d%d" % (u, h), [P, PACK, K_PASS // 2]) for h in range(2)] for u in range(GROUPS)]
-        y_raw = [f32_tile("y_raw%d" % u, [P, PACK, N]) for u in range(GROUPS)]
+        y_raw0 = f32_tile("y_raw0", [P, PACK, N])
+        y_raw1 = [f32_tile("y_raw1%d" % h, [P, PACK, HALF]) for h in range(2)]
         xm_raw = [[f32_tile("xm_raw0", [P, PACK, D])],
                   [f32_tile("xm_raw1%d" % h, [P, PACK, D // 2]) for h in range(2)]]
 
@@ -73,12 +75,15 @@ def tile_attend_gnce_sgd_kernel(tc, xT, wT, y, wt, xm, offs, out):
                 row0 = u * K_PASS + h * K_PASS // 2
                 nc.sync.dma_start(x_raw[u][h][:], x_hbm[:, :, row0:row0 + K_PASS // 2])
         nc.sync.dma_start(wt_sb[:], wt[0].rearrange("(u p j) one -> p u (j one)", u=GROUPS, j=PACK))
-        for u in range(GROUPS):
-            for j0 in (0, 2):
-                nc.sync.dma_start(y_raw[u][:, j0:j0 + 2, :], y_hbm[u][:, j0:j0 + 2, :])
+        for j0 in (0, 2):
+            nc.sync.dma_start(y_raw0[:, j0:j0 + 2, :], y_hbm[0][:, j0:j0 + 2, :])
+        nc.sync.dma_start(y_raw1[0][:], y_hbm[1][:, :, 0:HALF])
         nc.sync.dma_start(xm_raw[0][0][:], xm_hbm[0])
         for h in range(2):
             nc.sync.dma_start(xm_raw[1][h][:], xm_hbm[1][:, :, h * D // 2:(h + 1) * D // 2])
+        for j0 in (0, 2):
+            nc.sync.dma_start(y_raw1[1][:, j0:j0 + 2, :], y_hbm[1][:, j0:j0 + 2, HALF:N])
+        nc.sync.dma_start(result[LAST][:], table_hbm[:, LAST, :])
 
         warm = f32_tile("warm", [P, 2])
         nc.vector.memset(warm[:, 0:1], 0.0)
@@ -106,117 +111,177 @@ def tile_attend_gnce_sgd_kernel(tc, xT, wT, y, wt, xm, offs, out):
         quantize(w_mx, w_bf, E4M3, N // 2, N)
 
         x_mx = [mx_tiles("x%d" % u) for u in range(GROUPS)]
-        sig = [[f32_tile("sig%d%d" % (u, j), [P, N]) for j in range(PACK)] for u in range(GROUPS)]
-        err = [f32_tile("err%d" % u, [P, PACK, N]) for u in range(GROUPS)]
-        g_bf = [bf16_tile("g_bf0", "sig12"), bf16_tile("g_bf1")]
+        sig0 = [f32_tile("sig0%d" % j, [P, N]) for j in range(PACK)]
+        sig1 = [f32_tile("sig1%d" % h, [P, PACK, HALF]) for h in range(2)]
+        err0 = f32_tile("err0", [P, PACK, N])
+        g_bf0 = bf16_tile("g_bf0")
+        g_bf1 = [bf16_tile("g_bf1%d" % h, words=HALF) for h in range(2)]
         g_mx = [mx_tiles("g%d" % u) for u in range(GROUPS)]
         xm_bf_first = bf16_tile("xm_bf_first", "y_raw0")
-        xm_bf_second = [bf16_tile("xm_bf_second0", "y_raw0", 2 * P), bf16_tile("xm_bf_second1", "g_bf1", 2 * P)]
         xm_mx = [mx_tiles("xm_pair%d" % pair) for pair in range(2)]
-        dw = [ps_dw.tile([P, N], F32, name="dw%d" % t) for t in range(PACK)]
+        nc.vector.memset(g_mx[1][0][:, HALF:N], 0)
+        nc.vector.memset(g_mx[1][1][:, HALF:N], 0)
 
         def interleave_x(copy, dst, u, h, j0, j1):
             copy(dst[:].rearrange("p (j h m t) -> p h m t j", j=PACK, h=2, t=PACK)[:, h, :, :, j0:j1],
                  x_raw[u][h][:].rearrange("p t (m j) -> p m t j", j=PACK)[:, :, :, j0:j1])
 
-        for u in range(GROUPS):
-            x_bf = bf16_tile("x_bf%d" % u)
-            if u == 0:
-                interleave_x(nc.scalar.copy, x_bf, u, 0, 0, PACK)
-                interleave_x(nc.scalar.copy, x_bf, u, 1, 0, 2)
-                interleave_x(nc.scalar.copy, x_bf, u, 1, 2, PACK)
-                quantize(x_mx[u], x_bf, E4M3, 0, P)
-                quantize(x_mx[u], x_bf, E4M3, P, 2 * P)
-            else:
-                interleave_x(nc.scalar.copy, x_bf, u, 0, 0, 2)
-                interleave_x(nc.vector.tensor_copy, x_bf, u, 0, 2, PACK)
-                interleave_x(nc.vector.tensor_copy, x_bf, u, 1, 0, 2)
-                interleave_x(nc.vector.tensor_copy, x_bf, u, 1, 2, PACK)
-                quantize(x_mx[u], x_bf, E4M3, 0, 2 * P)
-            quantize(x_mx[u], x_bf, E4M3, 2 * P, PACK * P)
-            for j in range(PACK):
-                words = slice(j * P, (j + 1) * P)
-                logits = ps_a.tile([P, N], F32, name="logits")
-                nc.tensor.matmul_mx(
-                    out=logits[:],
-                    lhsT=x_mx[u][0][:, words].bitcast(E4M3), lhsT_scale=x_mx[u][1][:, words],
-                    rhs=w_mx[0][:].bitcast(E4M3), rhs_scale=w_mx[1][:],
-                    start=True, stop=True)
-                nc.scalar.activation(sig[u][j][:], logits[:], ACT.Sigmoid)
+        def logits_matmul(dst, u, j, slots):
+            words = slice(j * P, (j + 1) * P)
+            nc.tensor.matmul_mx(
+                out=dst,
+                lhsT=x_mx[u][0][:, words].bitcast(E4M3), lhsT_scale=x_mx[u][1][:, words],
+                rhs=w_mx[0][:, slots].bitcast(E4M3), rhs_scale=w_mx[1][:, slots],
+                start=True, stop=True)
 
-        def interleave_xm(copy, dst, u, pair):
+        x_bf = [bf16_tile("x_bf%d" % u) for u in range(GROUPS)]
+        interleave_x(nc.scalar.copy, x_bf[0], 0, 0, 0, PACK)
+        interleave_x(nc.scalar.copy, x_bf[0], 0, 1, 0, 2)
+        interleave_x(nc.scalar.copy, x_bf[0], 0, 1, 2, PACK)
+        quantize(x_mx[0], x_bf[0], E4M3, 0, P)
+        quantize(x_mx[0], x_bf[0], E4M3, P, 2 * P)
+        quantize(x_mx[0], x_bf[0], E4M3, 2 * P, PACK * P)
+        interleave_x(nc.scalar.copy, x_bf[1], 1, 0, 0, 2)
+        for j in range(PACK):
+            logits = ps_a.tile([P, N], F32, name="logits")
+            logits_matmul(logits[:], 0, j, slice(0, N))
+            nc.scalar.activation(sig0[j][:], logits[:], ACT.Sigmoid)
+        interleave_x(nc.vector.tensor_copy, x_bf[1], 1, 0, 2, PACK)
+        interleave_x(nc.vector.tensor_copy, x_bf[1], 1, 1, 0, 2)
+        interleave_x(nc.vector.tensor_copy, x_bf[1], 1, 1, 2, PACK)
+        quantize(x_mx[1], x_bf[1], E4M3, 0, 2 * P)
+        quantize(x_mx[1], x_bf[1], E4M3, 2 * P, PACK * P)
+
+        def sigmoids1(h):
+            for j0 in (0, 2):
+                logits = ps_a.tile([P, N], F32, name="logits")
+                for e in range(2):
+                    logits_matmul(logits[:, e * HALF:(e + 1) * HALF], 1, j0 + e, slice(h * HALF, (h + 1) * HALF))
+                nc.scalar.activation(sig1[h][:, j0:j0 + 2, :].rearrange("p j i -> p (j i)"), logits[:], ACT.Sigmoid)
+
+        y_wt = [f32_tile("y_wt%d" % h, [P, PACK, HALF]) for h in range(2)]
+        g1 = [f32_tile("g1%d" % h, [P, PACK, HALF]) for h in range(2)]
+
+        def weigh_labels(h):
+            for j in range(PACK):
+                nc.scalar.activation(y_wt[h][:, j, :], y_raw1[h][:, j, :], ACT.Copy, scale=wt_sb[:, 1, j:j + 1])
+
+        def gradient1(h):
+            for j in range(PACK):
+                nc.vector.scalar_tensor_tensor(g1[h][:, j, :], sig1[h][:, j, :], wt_sb[:, 1, j:j + 1],
+                                               y_wt[h][:, j, :], ALU.mult, ALU.subtract)
+
+        def interleave_xm(copy, dst, u, h, pair):
             share = P // len(xm_raw[u])
-            for h, raw in enumerate(xm_raw[u]):
-                copy(dst[:, h * share:(h + 1) * share],
-                     raw[:].rearrange("p j (m t) -> p m j t", t=PACK)[:, :, :, 2 * pair:2 * pair + 2])
+            copy(dst[:, h * share:(h + 1) * share],
+                 xm_raw[u][h][:].rearrange("p j (m t) -> p m j t", t=PACK)[:, :, :, 2 * pair:2 * pair + 2])
 
         def xm_words(u, t):
             word0 = (2 * (t % 2) + u) * P if t < 2 else (2 * u + t % 2) * P
             return slice(word0, word0 + P)
 
-        def gradient_matmul(u, t):
+        def gradient_matmul(dst, u, t, first):
             words = xm_words(u, t)
             nc.tensor.matmul_mx(
-                out=dw[t][:],
+                out=dst[:],
                 lhsT=xm_mx[t // 2][0][:, words].bitcast(E4M3), lhsT_scale=xm_mx[t // 2][1][:, words],
                 rhs=g_mx[u][0][:].bitcast(E5M2), rhs_scale=g_mx[u][1][:],
-                start=(u == 0), stop=(u == GROUPS - 1))
+                start=first, stop=not first)
 
-        def g_words(u, slots):
-            return g_bf[u][:, PACK * slots.start:PACK * slots.stop].rearrange("p (c i j) -> p c j i", i=RUN, j=PACK)
+        def g_words(dst, slots):
+            return dst[:, PACK * slots.start:PACK * slots.stop].rearrange("p (c i j) -> p c j i", i=RUN, j=PACK)
 
         def in_runs(src):
             return src.rearrange("p j (c i) -> p c j i", i=RUN)
 
-        for u in range(GROUPS):
-            for j in range(PACK):
-                nc.vector.tensor_tensor(err[u][:, j, :], sig[u][j][:], y_raw[u][:, j, :], ALU.subtract)
+        def quantize_g1(h):
+            words = slice(h * HALF, (h + 1) * HALF)
+            nc.vector.quantize_mx(out=g_mx[1][0][:, words].bitcast(E5M2), scales=g_mx[1][1][:, words],
+                                  in_=g_bf1[h][:])
 
+        def scale_step(name, dw, slots, tag=None):
+            step = f32_tile(name, [P, slots.stop - slots.start], tag)
+            nc.scalar.activation(step[:], dw[:, slots], ACT.Copy, scale=-LR)
+            return step
+
+        def scatter(t, step, slots):
+            list_cols = slice(slots.start // 16, slots.stop // 16)
+            nc.vector.tensor_tensor(result[t][:].indirect(offsets[:, list_cols]), step[:], w_decayed[t][:, slots],
+                                    ALU.add)
+
+        early, late, whole = slice(0, HALF), slice(HALF, N), slice(0, N)
+        for j in range(PACK):
+            nc.vector.tensor_tensor(err0[:, j, :], sig0[j][:], y_raw0[:, j, :], ALU.subtract)
+        sigmoids1(0)
+        weigh_labels(0)
         fused, apart = slice(0, FUSED_SLOTS), slice(FUSED_SLOTS, N)
-        weighted = [f32_tile("weighted0", [P, PACK, N - FUSED_SLOTS]), f32_tile("weighted1", [P, PACK, N])]
-        for u, slots in ((0, apart), (1, slice(0, N))):
-            for j in range(PACK):
-                nc.scalar.activation(weighted[u][:, j, :], err[u][:, j, slots], ACT.Copy, scale=wt_sb[:, u, j:j + 1])
-        first_dst = xm_bf_first[:].rearrange("p (e u m j) -> p u m j e", u=GROUPS, e=2, j=PACK)
-        for u in range(GROUPS):
-            interleave_xm(nc.scalar.copy, first_dst[:, u], u, 0)
-
-        nc.vector.tensor_copy(g_words(0, apart), in_runs(weighted[0][:]))
+        weighted0 = f32_tile("weighted0", [P, PACK, N - FUSED_SLOTS])
+        for j in range(PACK):
+            nc.scalar.activation(weighted0[:, j, :], err0[:, j, apart], ACT.Copy, scale=wt_sb[:, 0, j:j + 1])
         nc.vector.tensor_tensor(
-            g_words(0, fused), in_runs(err[0][:, :, fused]),
+            g_words(g_bf0, fused), in_runs(err0[:, :, fused]),
             wt_sb[:, 0, :].unsqueeze(1).unsqueeze(3).to_broadcast([P, FUSED_SLOTS // RUN, PACK, RUN]),
             ALU.mult)
-        nc.vector.tensor_copy(g_words(1, slice(0, N)), in_runs(weighted[1][:]))
-        for u in range(GROUPS):
-            quantize(g_mx[u], g_bf[u], E5M2, 0, N)
-            quantize(xm_mx[0], xm_bf_first, E4M3, u * P, (u + 1) * P)
-            gradient_matmul(u, 0)
+        gradient1(0)
+        nc.vector.tensor_copy(g_words(g_bf0, apart), in_runs(weighted0[:]))
+        first_dst = xm_bf_first[:].rearrange("p (e u m j) -> p u m j e", u=GROUPS, e=2, j=PACK)
+        interleave_xm(nc.scalar.copy, first_dst[:, 0], 0, 0, 0)
+        dw_early = [ps_dw.tile([P, N], F32, name="dw_early%d" % t, tag="dw%d" % t) for t in range(2)]
+        quantize(g_mx[0], g_bf0, E5M2, 0, N)
+        nc.vector.tensor_copy(g_words(g_bf1[0], early), in_runs(g1[0][:]))
+        quantize(xm_mx[0], xm_bf_first, E4M3, 0, P)
+        gradient_matmul(dw_early[0], 0, 0, True)
+        quantize_g1(0)
+        sigmoids1(1)
+        for h in range(2):
+            interleave_xm(nc.scalar.copy, first_dst[:, 1], 1, h, 0)
+        weigh_labels(1)
+
+        quantize(xm_mx[0], xm_bf_first, E4M3, P, 2 * P)
+        gradient_matmul(dw_early[0], 1, 0, False)
         quantize(xm_mx[0], xm_bf_first, E4M3, 2 * P, 4 * P)
         for u in range(GROUPS):
-            gradient_matmul(u, 1)
+            gradient_matmul(dw_early[1], u, 1, u == 0)
+        gradient1(1)
 
-        for u, copy in ((1, nc.scalar.copy), (0, nc.vector.tensor_copy)):
-            interleave_xm(copy, xm_bf_second[u][:].rearrange("p (e m j) -> p m j e", e=2, j=PACK), u, 1)
-        for u in range(GROUPS):
-            words = slice(2 * P * u, 2 * P * (u + 1))
-            nc.vector.quantize_mx(out=xm_mx[1][0][:, words].bitcast(E4M3), scales=xm_mx[1][1][:, words],
-                                  in_=xm_bf_second[u][:])
-        for t in range(2, PACK):
+        step = scale_step("step_early0", dw_early[0], early)
+        nc.scalar.copy(g_words(g_bf1[1], early), in_runs(g1[1][:]))
+        scatter(0, step, early)
+        step = scale_step("step_early1", dw_early[1], early, "g11")
+        quantize_g1(1)
+        scatter(1, step, early)
+        dw_late = [ps_dw.tile([P, N], F32, name="dw_late%d" % t, tag="dw%d" % t) for t in range(2)]
+        for t in range(2):
             for u in range(GROUPS):
-                gradient_matmul(u, t)
+                gradient_matmul(dw_late[t], u, t, u == 0)
 
-        def update(t):
-            step = f32_tile("step%d" % t, [P, N])
-            nc.scalar.activation(step[:], dw[t][:], ACT.Copy, scale=-LR)
-            nc.vector.tensor_tensor(result[t][:].indirect(offsets[:]), step[:], w_decayed[t][:], ALU.add)
-            nc.sync.dma_start(out_hbm[:, t, :], result[t][:])
+        dw_rest = [ps_dw.tile([P, N], F32, name="dw_rest%d" % t) for t in range(2)]
 
-        for t in range(LAST):
-            update(t)
+        def second_pair(u, tag):
+            xm_bf = bf16_tile("xm_bf_second%d" % u, tag, 2 * P)
+            for h in range(len(xm_raw[u])):
+                interleave_xm(nc.scalar.copy, xm_bf[:].rearrange("p (e m j) -> p m j e", e=2, j=PACK), u, h, 1)
+            return xm_bf
+
+        def second_matmuls(u, xm_bf):
+            words = slice(2 * P * u, 2 * P * (u + 1))
+            nc.vector.quantize_mx(out=xm_mx[1][0][:, words].bitcast(E4M3), scales=xm_mx[1][1][:, words], in_=xm_bf[:])
+            for t in range(2, PACK):
+                gradient_matmul(dw_rest[t - 2], u, t, u == 1)
+
+        xm_bf = second_pair(1, "g_bf11")
+        second_matmuls(1, xm_bf)
+        step = scale_step("step_late0", dw_late[0], late)
+        scatter(0, step, late)
+        nc.sync.dma_start(out_hbm[:, 0, :], result[0][:])
+        xm_bf = second_pair(0, "g11")
+        second_matmuls(0, xm_bf)
+        step = scale_step("step_late1", dw_late[1], late)
+        scatter(1, step, late)
+        nc.sync.dma_start(out_hbm[:, 1, :], result[1][:])
         w_decayed.append(f32_tile("w_decayed%d" % LAST, [P, N], "xm_raw11"))
         nc.scalar.activation(w_decayed[LAST][:], w_picked[:, LAST, :], ACT.Copy, scale=1.0 - LR * WD)
-        result.append(f32_tile("result%d" % LAST, [P, T], "xm_raw0"))
-        piece = T // LATE_COPY_PIECES
-        for c0 in range(0, T, piece):
-            nc.scalar.activation(result[LAST][:, c0:c0 + piece], table[LAST][:, c0:c0 + piece], ACT.Copy)
-        update(LAST)
+        for t in range(2, PACK):
+            step = scale_step("step%d" % t, dw_rest[t - 2], whole)
+            scatter(t, step, whole)
+            nc.sync.dma_start(out_hbm[:, t, :], result[t][:])

@@ -114,7 +114,7 @@ def tile_attend_gnce_sgd_kernel(tc, xT, wT, y, wt, xm, offs, out):
         sig0 = [f32_tile("sig0%d" % j, [P, N]) for j in range(PACK)]
         sig1 = [f32_tile("sig1%d" % h, [P, PACK, HALF]) for h in range(2)]
         err0 = f32_tile("err0", [P, PACK, N])
-        g_bf0 = bf16_tile("g_bf0")
+        g_bf0 = bf16_tile("g_bf0", "y_raw10")
         g_bf1 = [bf16_tile("g_bf1%d" % h, words=HALF) for h in range(2)]
         g_mx = [mx_tiles("g%d" % u) for u in range(GROUPS)]
         xm_bf_first = bf16_tile("xm_bf_first", "y_raw0")
@@ -141,12 +141,11 @@ def tile_attend_gnce_sgd_kernel(tc, xT, wT, y, wt, xm, offs, out):
         quantize(x_mx[0], x_bf[0], E4M3, 0, P)
         quantize(x_mx[0], x_bf[0], E4M3, P, 2 * P)
         quantize(x_mx[0], x_bf[0], E4M3, 2 * P, PACK * P)
-        interleave_x(nc.scalar.copy, x_bf[1], 1, 0, 0, 2)
         for j in range(PACK):
             logits = ps_a.tile([P, N], F32, name="logits")
             logits_matmul(logits[:], 0, j, slice(0, N))
             nc.scalar.activation(sig0[j][:], logits[:], ACT.Sigmoid)
-        interleave_x(nc.vector.tensor_copy, x_bf[1], 1, 0, 2, PACK)
+        interleave_x(nc.vector.tensor_copy, x_bf[1], 1, 0, 0, PACK)
         interleave_x(nc.vector.tensor_copy, x_bf[1], 1, 1, 0, 2)
         interleave_x(nc.vector.tensor_copy, x_bf[1], 1, 1, 2, PACK)
         quantize(x_mx[1], x_bf[1], E4M3, 0, 2 * P)
@@ -213,22 +212,19 @@ def tile_attend_gnce_sgd_kernel(tc, xT, wT, y, wt, xm, offs, out):
         for j in range(PACK):
             nc.vector.tensor_tensor(err0[:, j, :], sig0[j][:], y_raw0[:, j, :], ALU.subtract)
         sigmoids1(0)
-        weigh_labels(0)
-        fused, apart = slice(0, FUSED_SLOTS), slice(FUSED_SLOTS, N)
-        weighted0 = f32_tile("weighted0", [P, PACK, N - FUSED_SLOTS])
+        err1 = f32_tile("err1", [P, PACK, HALF])
+        nc.vector.tensor_tensor(err1[:], sig1[0][:], y_raw1[0][:], ALU.subtract)
         for j in range(PACK):
-            nc.scalar.activation(weighted0[:, j, :], err0[:, j, apart], ACT.Copy, scale=wt_sb[:, 0, j:j + 1])
+            nc.scalar.activation(g1[0][:, j, :], err1[:, j, :], ACT.Copy, scale=wt_sb[:, 1, j:j + 1])
         nc.vector.tensor_tensor(
-            g_words(g_bf0, fused), in_runs(err0[:, :, fused]),
-            wt_sb[:, 0, :].unsqueeze(1).unsqueeze(3).to_broadcast([P, FUSED_SLOTS // RUN, PACK, RUN]),
+            g_words(g_bf0, whole), in_runs(err0[:]),
+            wt_sb[:, 0, :].unsqueeze(1).unsqueeze(3).to_broadcast([P, N // RUN, PACK, RUN]),
             ALU.mult)
-        gradient1(0)
-        nc.vector.tensor_copy(g_words(g_bf0, apart), in_runs(weighted0[:]))
         first_dst = xm_bf_first[:].rearrange("p (e u m j) -> p u m j e", u=GROUPS, e=2, j=PACK)
         interleave_xm(nc.scalar.copy, first_dst[:, 0], 0, 0, 0)
         dw_early = [ps_dw.tile([P, N], F32, name="dw_early%d" % t, tag="dw%d" % t) for t in range(2)]
-        quantize(g_mx[0], g_bf0, E5M2, 0, N)
         nc.vector.tensor_copy(g_words(g_bf1[0], early), in_runs(g1[0][:]))
+        quantize(g_mx[0], g_bf0, E5M2, 0, N)
         quantize(xm_mx[0], xm_bf_first, E4M3, 0, P)
         gradient_matmul(dw_early[0], 0, 0, True)
         quantize_g1(0)

@@ -26,7 +26,8 @@ LIST_COLS = N // 16
 LOGIT_BANKS = 4
 LATE_COPY_PIECES = 4
 HALF = N // 2
-FUSED_SLOTS = 352
+SCALAR_XM_WORDS = 64
+FUSED_SLOTS = 320
 
 
 def tile_attend_gnce_sgd_kernel(tc, xT, wT, y, wt, xm, offs, out):
@@ -58,7 +59,7 @@ def tile_attend_gnce_sgd_kernel(tc, xT, wT, y, wt, xm, offs, out):
         y_raw0 = f32_tile("y_raw0", [P, PACK, N])
         y_raw1 = [f32_tile("y_raw1%d" % h, [P, PACK, HALF]) for h in range(2)]
         xm_raw = [[f32_tile("xm_raw0", [P, PACK, D])],
-                  [f32_tile("xm_raw1%d" % h, [P, PACK, D // 2]) for h in range(2)]]
+                  [f32_tile("xm_raw10", [P, PACK, D])]]
 
         table_hbm = wT.rearrange("(p t) c -> p t c", t=PACK)
         out_hbm = out.rearrange("(p t) c -> p t c", t=PACK)
@@ -79,8 +80,7 @@ def tile_attend_gnce_sgd_kernel(tc, xT, wT, y, wt, xm, offs, out):
             nc.sync.dma_start(y_raw0[:, j0:j0 + 2, :], y_hbm[0][:, j0:j0 + 2, :])
         nc.sync.dma_start(y_raw1[0][:], y_hbm[1][:, :, 0:HALF])
         nc.sync.dma_start(xm_raw[0][0][:], xm_hbm[0])
-        for h in range(2):
-            nc.sync.dma_start(xm_raw[1][h][:], xm_hbm[1][:, :, h * D // 2:(h + 1) * D // 2])
+        nc.sync.dma_start(xm_raw[1][0][:], xm_hbm[1])
         for j0 in (0, 2):
             nc.sync.dma_start(y_raw1[1][:, j0:j0 + 2, :], y_hbm[1][:, j0:j0 + 2, HALF:N])
         nc.sync.dma_start(result[LAST][:], table_hbm[:, LAST, :])
@@ -170,10 +170,9 @@ def tile_attend_gnce_sgd_kernel(tc, xT, wT, y, wt, xm, offs, out):
                 nc.vector.scalar_tensor_tensor(g1[h][:, j, :], sig1[h][:, j, :], wt_sb[:, 1, j:j + 1],
                                                y_wt[h][:, j, :], ALU.mult, ALU.subtract)
 
-        def interleave_xm(copy, dst, u, h, pair):
-            share = P // len(xm_raw[u])
-            copy(dst[:, h * share:(h + 1) * share],
-                 xm_raw[u][h][:].rearrange("p j (m t) -> p m j t", t=PACK)[:, :, :, 2 * pair:2 * pair + 2])
+        def interleave_xm(copy, dst, u, h, pair, m0=0, m1=P):
+            copy(dst[:, m0:m1],
+                 xm_raw[u][h][:].rearrange("p j (m t) -> p m j t", t=PACK)[:, m0:m1, :, 2 * pair:2 * pair + 2])
 
         def xm_words(u, t):
             word0 = (2 * (t % 2) + u) * P if t < 2 else (2 * u + t % 2) * P
@@ -214,12 +213,17 @@ def tile_attend_gnce_sgd_kernel(tc, xT, wT, y, wt, xm, offs, out):
         sigmoids1(0)
         err1 = f32_tile("err1", [P, PACK, HALF])
         nc.vector.tensor_tensor(err1[:], sig1[0][:], y_raw1[0][:], ALU.subtract)
+        fused, apart = slice(0, FUSED_SLOTS), slice(FUSED_SLOTS, N)
+        weighted0 = f32_tile("weighted0", [P, PACK, N - FUSED_SLOTS])
+        for j in range(PACK):
+            nc.scalar.activation(weighted0[:, j, :], err0[:, j, apart], ACT.Copy, scale=wt_sb[:, 0, j:j + 1])
         for j in range(PACK):
             nc.scalar.activation(g1[0][:, j, :], err1[:, j, :], ACT.Copy, scale=wt_sb[:, 1, j:j + 1])
         nc.vector.tensor_tensor(
-            g_words(g_bf0, whole), in_runs(err0[:]),
-            wt_sb[:, 0, :].unsqueeze(1).unsqueeze(3).to_broadcast([P, N // RUN, PACK, RUN]),
+            g_words(g_bf0, fused), in_runs(err0[:, :, fused]),
+            wt_sb[:, 0, :].unsqueeze(1).unsqueeze(3).to_broadcast([P, FUSED_SLOTS // RUN, PACK, RUN]),
             ALU.mult)
+        nc.vector.tensor_copy(g_words(g_bf0, apart), in_runs(weighted0[:]))
         first_dst = xm_bf_first[:].rearrange("p (e u m j) -> p u m j e", u=GROUPS, e=2, j=PACK)
         interleave_xm(nc.scalar.copy, first_dst[:, 0], 0, 0, 0)
         dw_early = [ps_dw.tile([P, N], F32, name="dw_early%d" % t, tag="dw%d" % t) for t in range(2)]
@@ -229,8 +233,8 @@ def tile_attend_gnce_sgd_kernel(tc, xT, wT, y, wt, xm, offs, out):
         gradient_matmul(dw_early[0], 0, 0, True)
         quantize_g1(0)
         sigmoids1(1)
-        for h in range(2):
-            interleave_xm(nc.scalar.copy, first_dst[:, 1], 1, h, 0)
+        interleave_xm(nc.scalar.copy, first_dst[:, 1], 1, 0, 0, 0, SCALAR_XM_WORDS)
+        interleave_xm(nc.vector.tensor_copy, first_dst[:, 1], 1, 0, 0, SCALAR_XM_WORDS, P)
         weigh_labels(1)
 
         quantize(xm_mx[0], xm_bf_first, E4M3, P, 2 * P)
@@ -275,7 +279,7 @@ def tile_attend_gnce_sgd_kernel(tc, xT, wT, y, wt, xm, offs, out):
         step = scale_step("step_late1", dw_late[1], late)
         scatter(1, step, late)
         nc.sync.dma_start(out_hbm[:, 1, :], result[1][:])
-        w_decayed.append(f32_tile("w_decayed%d" % LAST, [P, N], "xm_raw11"))
+        w_decayed.append(f32_tile("w_decayed%d" % LAST, [P, N], "xm_raw10"))
         nc.scalar.activation(w_decayed[LAST][:], w_picked[:, LAST, :], ACT.Copy, scale=1.0 - LR * WD)
         for t in range(2, PACK):
             step = scale_step("step%d" % t, dw_rest[t - 2], whole)

@@ -22,16 +22,17 @@ K_PASS = P * PACK
 GROUPS = R // K_PASS
 LAST = PACK - 1
 RUN = 4
-LIST_COLS = N // 16
-LOGIT_BANKS = 4
-LATE_COPY_PIECES = 4
+SLOTS_PER_COL = 16
 HALF = N // 2
-SCALAR_XM_WORDS = 64
+LOGIT_BANKS = 4
 FUSED_SLOTS = 320
+SCALAR_XM_WORDS = 64
 
 
 def tile_attend_gnce_sgd_kernel(tc, xT, wT, y, wt, xm, offs, out):
     nc = tc.nc
+    early, late, whole = slice(0, HALF), slice(HALF, N), slice(0, N)
+    halves = (early, late)
     with ExitStack() as ctx:
         sb = ctx.enter_context(tc.tile_pool(name="sb", bufs=1))
         ps_a = ctx.enter_context(tc.psum_pool(name="ps_a", bufs=LOGIT_BANKS))
@@ -47,19 +48,23 @@ def tile_attend_gnce_sgd_kernel(tc, xT, wT, y, wt, xm, offs, out):
             return (sb.tile([P, K_PASS], U32, name=name + "_codes", align_bytes=64),
                     sb.tile([P, K_PASS], U8, name=name + "_scales", align_bytes=64))
 
-        def quantize(mx, src, fmt, word0, word1):
-            nc.vector.quantize_mx(out=mx[0][:, word0:word1].bitcast(fmt), scales=mx[1][:, word0:word1],
-                                  in_=src[:, PACK * word0:PACK * word1])
+        def quantize(mx, words, fmt, src):
+            nc.vector.quantize_mx(out=mx[0][:, words].bitcast(fmt), scales=mx[1][:, words], in_=src)
 
-        offsets = sb.tile([P, LIST_COLS], U16, name="offsets")
+        def quantize_part(mx, src_tile, fmt, word0, word1):
+            quantize(mx, slice(word0, word1), fmt, src_tile[:, PACK * word0:PACK * word1])
+
+        def list_part(slots):
+            return offsets[:, slots.start // SLOTS_PER_COL:slots.stop // SLOTS_PER_COL]
+
+        offsets = sb.tile([P, N // SLOTS_PER_COL], U16, name="offsets")
         wt_sb = f32_tile("wt_sb", [P, GROUPS, PACK])
         table = [f32_tile("table%d" % t, [P, T]) for t in range(PACK)]
         result = [f32_tile("result%d" % t, [P, T]) for t in range(PACK)]
         x_raw = [[f32_tile("x_raw%d%d" % (u, h), [P, PACK, K_PASS // 2]) for h in range(2)] for u in range(GROUPS)]
         y_raw0 = f32_tile("y_raw0", [P, PACK, N])
-        y_raw1 = [f32_tile("y_raw1%d" % h, [P, PACK, HALF]) for h in range(2)]
-        xm_raw = [[f32_tile("xm_raw0", [P, PACK, D])],
-                  [f32_tile("xm_raw10", [P, PACK, D])]]
+        y_early1, y_late1 = [f32_tile(name, [P, PACK, HALF]) for name in ("y_early1", "y_late1")]
+        xm_raw = [f32_tile("xm_raw%d" % u, [P, PACK, D]) for u in range(GROUPS)]
 
         table_hbm = wT.rearrange("(p t) c -> p t c", t=PACK)
         out_hbm = out.rearrange("(p t) c -> p t c", t=PACK)
@@ -78,11 +83,11 @@ def tile_attend_gnce_sgd_kernel(tc, xT, wT, y, wt, xm, offs, out):
         nc.sync.dma_start(wt_sb[:], wt[0].rearrange("(u p j) one -> p u (j one)", u=GROUPS, j=PACK))
         for j0 in (0, 2):
             nc.sync.dma_start(y_raw0[:, j0:j0 + 2, :], y_hbm[0][:, j0:j0 + 2, :])
-        nc.sync.dma_start(y_raw1[0][:], y_hbm[1][:, :, 0:HALF])
-        nc.sync.dma_start(xm_raw[0][0][:], xm_hbm[0])
-        nc.sync.dma_start(xm_raw[1][0][:], xm_hbm[1])
+        nc.sync.dma_start(y_early1[:], y_hbm[1][:, :, early])
+        for u in range(GROUPS):
+            nc.sync.dma_start(xm_raw[u][:], xm_hbm[u])
         for j0 in (0, 2):
-            nc.sync.dma_start(y_raw1[1][:, j0:j0 + 2, :], y_hbm[1][:, j0:j0 + 2, HALF:N])
+            nc.sync.dma_start(y_late1[:, j0:j0 + 2, :], y_hbm[1][:, j0:j0 + 2, late])
         nc.sync.dma_start(result[LAST][:], table_hbm[:, LAST, :])
 
         warm = f32_tile("warm", [P, 2])
@@ -95,35 +100,35 @@ def tile_attend_gnce_sgd_kernel(tc, xT, wT, y, wt, xm, offs, out):
             nc.vector.tensor_copy(w_picked[:, t, :], table[t][:].indirect(offsets[:]))
             nc.scalar.activation(result[t][:], table[t][:], ACT.Copy)
             nc.vector.tensor_scalar(w_decayed[t][:], w_picked[:, t, :], 1.0 - LR * WD, None, ALU.mult)
-        for h in range(2):
-            entries = slice(h * N // 2, (h + 1) * N // 2)
-            list_cols = slice(h * LIST_COLS // 2, (h + 1) * LIST_COLS // 2)
-            nc.vector.tensor_copy(w_picked[:, LAST, entries], table[LAST][:].indirect(offsets[:, list_cols]))
 
+        for slots in halves:
+            nc.vector.tensor_copy(w_picked[:, LAST, slots], table[LAST][:].indirect(list_part(slots)))
         w_bf = bf16_tile("w_bf")
         w_dst = w_bf[:].rearrange("p (c i t) -> p c t i", i=RUN, t=PACK)
         w_src = w_picked[:].rearrange("p t (c i) -> p c t i", i=RUN)
-        half_runs = N // RUN // 2
-        nc.vector.tensor_copy(w_dst[:, :half_runs], w_src[:, :half_runs])
-        nc.vector.tensor_copy(w_dst[:, half_runs:], w_src[:, half_runs:])
+        for slots in halves:
+            runs = slice(slots.start // RUN, slots.stop // RUN)
+            nc.vector.tensor_copy(w_dst[:, runs], w_src[:, runs])
         w_mx = mx_tiles("w")
-        quantize(w_mx, w_bf, E4M3, 0, N // 2)
-        quantize(w_mx, w_bf, E4M3, N // 2, N)
+        for slots in halves:
+            quantize_part(w_mx, w_bf, E4M3, slots.start, slots.stop)
 
         x_mx = [mx_tiles("x%d" % u) for u in range(GROUPS)]
         sig0 = [f32_tile("sig0%d" % j, [P, N]) for j in range(PACK)]
-        sig1 = [f32_tile("sig1%d" % h, [P, PACK, HALF]) for h in range(2)]
+        sig_early1, sig_late1 = [f32_tile(name, [P, PACK, HALF]) for name in ("sig_early1", "sig_late1")]
         err0 = f32_tile("err0", [P, PACK, N])
-        g_bf0 = bf16_tile("g_bf0", "y_raw10")
-        g_bf1 = [bf16_tile("g_bf1%d" % h, words=HALF) for h in range(2)]
+        g_bf0 = bf16_tile("g_bf0", "y_early1")
+        g_bf_early1, g_bf_late1 = [bf16_tile(name, words=HALF) for name in ("g_bf_early1", "g_bf_late1")]
         g_mx = [mx_tiles("g%d" % u) for u in range(GROUPS)]
-        xm_bf_first = bf16_tile("xm_bf_first", "y_raw0")
+        xm_bf_pair0 = bf16_tile("xm_bf_pair0", "y_raw0")
         xm_mx = [mx_tiles("xm_pair%d" % pair) for pair in range(2)]
-        nc.vector.memset(g_mx[1][0][:, HALF:N], 0)
-        nc.vector.memset(g_mx[1][1][:, HALF:N], 0)
+        nc.vector.memset(g_mx[1][0][:, late], 0)
+        nc.vector.memset(g_mx[1][1][:, late], 0)
 
-        def interleave_x(copy, dst, u, h, j0, j1):
-            copy(dst[:].rearrange("p (j h m t) -> p h m t j", j=PACK, h=2, t=PACK)[:, h, :, :, j0:j1],
+        x_bf = [bf16_tile("x_bf%d" % u) for u in range(GROUPS)]
+
+        def interleave_x(copy, u, h, j0, j1):
+            copy(x_bf[u][:].rearrange("p (j h m t) -> p h m t j", j=PACK, h=2, t=PACK)[:, h, :, :, j0:j1],
                  x_raw[u][h][:].rearrange("p t (m j) -> p m t j", j=PACK)[:, :, :, j0:j1])
 
         def logits_matmul(dst, u, j, slots):
@@ -134,68 +139,92 @@ def tile_attend_gnce_sgd_kernel(tc, xT, wT, y, wt, xm, offs, out):
                 rhs=w_mx[0][:, slots].bitcast(E4M3), rhs_scale=w_mx[1][:, slots],
                 start=True, stop=True)
 
-        x_bf = [bf16_tile("x_bf%d" % u) for u in range(GROUPS)]
-        interleave_x(nc.scalar.copy, x_bf[0], 0, 0, 0, PACK)
-        interleave_x(nc.scalar.copy, x_bf[0], 0, 1, 0, 2)
-        interleave_x(nc.scalar.copy, x_bf[0], 0, 1, 2, PACK)
-        quantize(x_mx[0], x_bf[0], E4M3, 0, P)
-        quantize(x_mx[0], x_bf[0], E4M3, P, 2 * P)
-        quantize(x_mx[0], x_bf[0], E4M3, 2 * P, PACK * P)
+        def interleave_x_group(copy, u):
+            interleave_x(copy, u, 0, 0, PACK)
+            for j0 in (0, 2):
+                interleave_x(copy, u, 1, j0, j0 + 2)
+
+        interleave_x_group(nc.scalar.copy, 0)
+        for j0, j1 in ((0, 1), (1, 2), (2, PACK)):
+            quantize_part(x_mx[0], x_bf[0], E4M3, j0 * P, j1 * P)
         for j in range(PACK):
             logits = ps_a.tile([P, N], F32, name="logits")
-            logits_matmul(logits[:], 0, j, slice(0, N))
+            logits_matmul(logits[:], 0, j, whole)
             nc.scalar.activation(sig0[j][:], logits[:], ACT.Sigmoid)
-        interleave_x(nc.vector.tensor_copy, x_bf[1], 1, 0, 0, PACK)
-        interleave_x(nc.vector.tensor_copy, x_bf[1], 1, 1, 0, 2)
-        interleave_x(nc.vector.tensor_copy, x_bf[1], 1, 1, 2, PACK)
-        quantize(x_mx[1], x_bf[1], E4M3, 0, 2 * P)
-        quantize(x_mx[1], x_bf[1], E4M3, 2 * P, PACK * P)
+        interleave_x_group(nc.vector.tensor_copy, 1)
+        for j0 in (0, 2):
+            quantize_part(x_mx[1], x_bf[1], E4M3, j0 * P, (j0 + 2) * P)
 
-        def sigmoids1(h):
+        def sigmoids_group1(sig, slots):
             for j0 in (0, 2):
                 logits = ps_a.tile([P, N], F32, name="logits")
                 for e in range(2):
-                    logits_matmul(logits[:, e * HALF:(e + 1) * HALF], 1, j0 + e, slice(h * HALF, (h + 1) * HALF))
-                nc.scalar.activation(sig1[h][:, j0:j0 + 2, :].rearrange("p j i -> p (j i)"), logits[:], ACT.Sigmoid)
+                    logits_matmul(logits[:, e * HALF:(e + 1) * HALF], 1, j0 + e, slots)
+                nc.scalar.activation(sig[:, j0:j0 + 2, :].rearrange("p j i -> p (j i)"), logits[:], ACT.Sigmoid)
 
-        y_wt = [f32_tile("y_wt%d" % h, [P, PACK, HALF]) for h in range(2)]
-        g1 = [f32_tile("g1%d" % h, [P, PACK, HALF]) for h in range(2)]
+        y_wt_late1 = f32_tile("y_wt_late1", [P, PACK, HALF])
+        g_early1, g_late1 = [f32_tile(name, [P, PACK, HALF]) for name in ("g_early1", "g_late1")]
 
-        def weigh_labels(h):
-            for j in range(PACK):
-                nc.scalar.activation(y_wt[h][:, j, :], y_raw1[h][:, j, :], ACT.Copy, scale=wt_sb[:, 1, j:j + 1])
-
-        def gradient1(h):
-            for j in range(PACK):
-                nc.vector.scalar_tensor_tensor(g1[h][:, j, :], sig1[h][:, j, :], wt_sb[:, 1, j:j + 1],
-                                               y_wt[h][:, j, :], ALU.mult, ALU.subtract)
-
-        def interleave_xm(copy, dst, u, h, pair, m0=0, m1=P):
-            copy(dst[:, m0:m1],
-                 xm_raw[u][h][:].rearrange("p j (m t) -> p m j t", t=PACK)[:, m0:m1, :, 2 * pair:2 * pair + 2])
-
-        def xm_words(u, t):
-            word0 = (2 * (t % 2) + u) * P if t < 2 else (2 * u + t % 2) * P
-            return slice(word0, word0 + P)
-
-        def gradient_matmul(dst, u, t, first):
-            words = xm_words(u, t)
-            nc.tensor.matmul_mx(
-                out=dst[:],
-                lhsT=xm_mx[t // 2][0][:, words].bitcast(E4M3), lhsT_scale=xm_mx[t // 2][1][:, words],
-                rhs=g_mx[u][0][:].bitcast(E5M2), rhs_scale=g_mx[u][1][:],
-                start=first, stop=not first)
-
-        def g_words(dst, slots):
-            return dst[:, PACK * slots.start:PACK * slots.stop].rearrange("p (c i j) -> p c j i", i=RUN, j=PACK)
+        def g_words(g_bf, slots):
+            return g_bf[:, PACK * slots.start:PACK * slots.stop].rearrange("p (c i j) -> p c j i", i=RUN, j=PACK)
 
         def in_runs(src):
             return src.rearrange("p j (c i) -> p c j i", i=RUN)
 
-        def quantize_g1(h):
-            words = slice(h * HALF, (h + 1) * HALF)
-            nc.vector.quantize_mx(out=g_mx[1][0][:, words].bitcast(E5M2), scales=g_mx[1][1][:, words],
-                                  in_=g_bf1[h][:])
+        def weigh(dst, src, u):
+            for j in range(PACK):
+                nc.scalar.activation(dst[:, j, :], src[:, j, :], ACT.Copy, scale=wt_sb[:, u, j:j + 1])
+
+        for j in range(PACK):
+            nc.vector.tensor_tensor(err0[:, j, :], sig0[j][:], y_raw0[:, j, :], ALU.subtract)
+        sigmoids_group1(sig_early1, early)
+        err_early1 = f32_tile("err_early1", [P, PACK, HALF])
+        nc.vector.tensor_tensor(err_early1[:], sig_early1[:], y_early1[:], ALU.subtract)
+        fused, apart = slice(0, FUSED_SLOTS), slice(FUSED_SLOTS, N)
+        g_apart0 = f32_tile("g_apart0", [P, PACK, N - FUSED_SLOTS])
+        weigh(g_apart0, err0[:, :, apart], 0)
+        weigh(g_early1, err_early1, 1)
+        nc.vector.tensor_tensor(
+            g_words(g_bf0, fused), in_runs(err0[:, :, fused]),
+            wt_sb[:, 0, :].unsqueeze(1).unsqueeze(3).to_broadcast([P, FUSED_SLOTS // RUN, PACK, RUN]),
+            ALU.mult)
+        nc.vector.tensor_copy(g_words(g_bf0, apart), in_runs(g_apart0[:]))
+
+        def interleave_xm(copy, dst, u, pair, m0=0, m1=P):
+            copy(dst[:, m0:m1],
+                 xm_raw[u][:].rearrange("p j (m t) -> p m j t", t=PACK)[:, m0:m1, :, 2 * pair:2 * pair + 2])
+
+        def gradient_matmul(dw, u, t, first):
+            pair, e = divmod(t, 2)
+            word0 = (2 * e + u) * P if pair == 0 else (2 * u + e) * P
+            words = slice(word0, word0 + P)
+            nc.tensor.matmul_mx(
+                out=dw[:],
+                lhsT=xm_mx[pair][0][:, words].bitcast(E4M3), lhsT_scale=xm_mx[pair][1][:, words],
+                rhs=g_mx[u][0][:].bitcast(E5M2), rhs_scale=g_mx[u][1][:],
+                start=first, stop=not first)
+
+        pair0_dst = xm_bf_pair0[:].rearrange("p (e u m j) -> p u m j e", u=GROUPS, e=2, j=PACK)
+        interleave_xm(nc.scalar.copy, pair0_dst[:, 0], 0, 0)
+        dw_early = [ps_dw.tile([P, N], F32, name="dw_early%d" % t, tag="dw%d" % t) for t in range(2)]
+        nc.vector.tensor_copy(g_words(g_bf_early1, early), in_runs(g_early1[:]))
+        quantize_part(g_mx[0], g_bf0, E5M2, 0, N)
+        quantize_part(xm_mx[0], xm_bf_pair0, E4M3, 0, P)
+        gradient_matmul(dw_early[0], 0, 0, True)
+        quantize(g_mx[1], early, E5M2, g_bf_early1[:])
+        sigmoids_group1(sig_late1, late)
+        interleave_xm(nc.scalar.copy, pair0_dst[:, 1], 1, 0, 0, SCALAR_XM_WORDS)
+        interleave_xm(nc.vector.tensor_copy, pair0_dst[:, 1], 1, 0, SCALAR_XM_WORDS, P)
+        weigh(y_wt_late1, y_late1, 1)
+
+        quantize_part(xm_mx[0], xm_bf_pair0, E4M3, P, 2 * P)
+        gradient_matmul(dw_early[0], 1, 0, False)
+        quantize_part(xm_mx[0], xm_bf_pair0, E4M3, 2 * P, 4 * P)
+        for u in range(GROUPS):
+            gradient_matmul(dw_early[1], u, 1, u == 0)
+        for j in range(PACK):
+            nc.vector.scalar_tensor_tensor(g_late1[:, j, :], sig_late1[:, j, :], wt_sb[:, 1, j:j + 1],
+                                           y_wt_late1[:, j, :], ALU.mult, ALU.subtract)
 
         def scale_step(name, dw, slots, tag=None):
             step = f32_tile(name, [P, slots.stop - slots.start], tag)
@@ -203,85 +232,32 @@ def tile_attend_gnce_sgd_kernel(tc, xT, wT, y, wt, xm, offs, out):
             return step
 
         def scatter(t, step, slots):
-            list_cols = slice(slots.start // 16, slots.stop // 16)
-            nc.vector.tensor_tensor(result[t][:].indirect(offsets[:, list_cols]), step[:], w_decayed[t][:, slots],
-                                    ALU.add)
+            nc.vector.tensor_tensor(result[t][:].indirect(list_part(slots)), step[:], w_decayed[t][:, slots], ALU.add)
 
-        early, late, whole = slice(0, HALF), slice(HALF, N), slice(0, N)
-        for j in range(PACK):
-            nc.vector.tensor_tensor(err0[:, j, :], sig0[j][:], y_raw0[:, j, :], ALU.subtract)
-        sigmoids1(0)
-        err1 = f32_tile("err1", [P, PACK, HALF])
-        nc.vector.tensor_tensor(err1[:], sig1[0][:], y_raw1[0][:], ALU.subtract)
-        fused, apart = slice(0, FUSED_SLOTS), slice(FUSED_SLOTS, N)
-        weighted0 = f32_tile("weighted0", [P, PACK, N - FUSED_SLOTS])
-        for j in range(PACK):
-            nc.scalar.activation(weighted0[:, j, :], err0[:, j, apart], ACT.Copy, scale=wt_sb[:, 0, j:j + 1])
-        for j in range(PACK):
-            nc.scalar.activation(g1[0][:, j, :], err1[:, j, :], ACT.Copy, scale=wt_sb[:, 1, j:j + 1])
-        nc.vector.tensor_tensor(
-            g_words(g_bf0, fused), in_runs(err0[:, :, fused]),
-            wt_sb[:, 0, :].unsqueeze(1).unsqueeze(3).to_broadcast([P, FUSED_SLOTS // RUN, PACK, RUN]),
-            ALU.mult)
-        nc.vector.tensor_copy(g_words(g_bf0, apart), in_runs(weighted0[:]))
-        first_dst = xm_bf_first[:].rearrange("p (e u m j) -> p u m j e", u=GROUPS, e=2, j=PACK)
-        interleave_xm(nc.scalar.copy, first_dst[:, 0], 0, 0, 0)
-        dw_early = [ps_dw.tile([P, N], F32, name="dw_early%d" % t, tag="dw%d" % t) for t in range(2)]
-        nc.vector.tensor_copy(g_words(g_bf1[0], early), in_runs(g1[0][:]))
-        quantize(g_mx[0], g_bf0, E5M2, 0, N)
-        quantize(xm_mx[0], xm_bf_first, E4M3, 0, P)
-        gradient_matmul(dw_early[0], 0, 0, True)
-        quantize_g1(0)
-        sigmoids1(1)
-        interleave_xm(nc.scalar.copy, first_dst[:, 1], 1, 0, 0, 0, SCALAR_XM_WORDS)
-        interleave_xm(nc.vector.tensor_copy, first_dst[:, 1], 1, 0, 0, SCALAR_XM_WORDS, P)
-        weigh_labels(1)
-
-        quantize(xm_mx[0], xm_bf_first, E4M3, P, 2 * P)
-        gradient_matmul(dw_early[0], 1, 0, False)
-        quantize(xm_mx[0], xm_bf_first, E4M3, 2 * P, 4 * P)
-        for u in range(GROUPS):
-            gradient_matmul(dw_early[1], u, 1, u == 0)
-        gradient1(1)
-
-        step = scale_step("step_early0", dw_early[0], early)
-        nc.scalar.copy(g_words(g_bf1[1], early), in_runs(g1[1][:]))
-        scatter(0, step, early)
-        step = scale_step("step_early1", dw_early[1], early, "g11")
-        quantize_g1(1)
-        scatter(1, step, early)
+        step_early0 = scale_step("step_early0", dw_early[0], early)
+        nc.scalar.copy(g_words(g_bf_late1, slice(0, HALF)), in_runs(g_late1[:]))
+        scatter(0, step_early0, early)
+        step_early1 = scale_step("step_early1", dw_early[1], early, "g_late1")
+        quantize(g_mx[1], late, E5M2, g_bf_late1[:])
+        scatter(1, step_early1, early)
         dw_late = [ps_dw.tile([P, N], F32, name="dw_late%d" % t, tag="dw%d" % t) for t in range(2)]
         for t in range(2):
             for u in range(GROUPS):
                 gradient_matmul(dw_late[t], u, t, u == 0)
 
-        dw_rest = [ps_dw.tile([P, N], F32, name="dw_rest%d" % t) for t in range(2)]
+        dw_pair1 = [ps_dw.tile([P, N], F32, name="dw_pair1%d" % e) for e in range(2)]
+        for t, u, tag in ((0, 1, "g_bf_late1"), (1, 0, "g_late1")):
+            xm_bf_pair1 = bf16_tile("xm_bf_pair1%d" % u, tag, 2 * P)
+            interleave_xm(nc.scalar.copy, xm_bf_pair1[:].rearrange("p (e m j) -> p m j e", e=2, j=PACK), u, 1)
+            quantize(xm_mx[1], slice(2 * P * u, 2 * P * (u + 1)), E4M3, xm_bf_pair1[:])
+            for e in range(2):
+                gradient_matmul(dw_pair1[e], u, 2 + e, u == 1)
+            scatter(t, scale_step("step_late%d" % t, dw_late[t], late), late)
+            nc.sync.dma_start(out_hbm[:, t, :], result[t][:])
 
-        def second_pair(u, tag):
-            xm_bf = bf16_tile("xm_bf_second%d" % u, tag, 2 * P)
-            for h in range(len(xm_raw[u])):
-                interleave_xm(nc.scalar.copy, xm_bf[:].rearrange("p (e m j) -> p m j e", e=2, j=PACK), u, h, 1)
-            return xm_bf
-
-        def second_matmuls(u, xm_bf):
-            words = slice(2 * P * u, 2 * P * (u + 1))
-            nc.vector.quantize_mx(out=xm_mx[1][0][:, words].bitcast(E4M3), scales=xm_mx[1][1][:, words], in_=xm_bf[:])
-            for t in range(2, PACK):
-                gradient_matmul(dw_rest[t - 2], u, t, u == 1)
-
-        xm_bf = second_pair(1, "g_bf11")
-        second_matmuls(1, xm_bf)
-        step = scale_step("step_late0", dw_late[0], late)
-        scatter(0, step, late)
-        nc.sync.dma_start(out_hbm[:, 0, :], result[0][:])
-        xm_bf = second_pair(0, "g11")
-        second_matmuls(0, xm_bf)
-        step = scale_step("step_late1", dw_late[1], late)
-        scatter(1, step, late)
-        nc.sync.dma_start(out_hbm[:, 1, :], result[1][:])
-        w_decayed.append(f32_tile("w_decayed%d" % LAST, [P, N], "xm_raw10"))
+        w_decayed.append(f32_tile("w_decayed%d" % LAST, [P, N], "xm_raw1"))
         nc.scalar.activation(w_decayed[LAST][:], w_picked[:, LAST, :], ACT.Copy, scale=1.0 - LR * WD)
-        for t in range(2, PACK):
-            step = scale_step("step%d" % t, dw_rest[t - 2], whole)
-            scatter(t, step, whole)
+        for e in range(2):
+            t = 2 + e
+            scatter(t, scale_step("step%d" % t, dw_pair1[e], whole), whole)
             nc.sync.dma_start(out_hbm[:, t, :], result[t][:])

@@ -24,6 +24,9 @@ LAST = PACK - 1
 RUN = 4
 SLOTS_PER_COL = 16
 HALF = N // 2
+EARLY = 384
+LATE = N - EARLY
+SCALAR_SLOTS = (352, 352, 320, EARLY)
 LOGIT_BANKS = 4
 FUSED_SLOTS = 320
 SCALAR_XM_WORDS = 64
@@ -31,8 +34,9 @@ SCALAR_XM_WORDS = 64
 
 def tile_attend_gnce_sgd_kernel(tc, xT, wT, y, wt, xm, offs, out):
     nc = tc.nc
-    early, late, whole = slice(0, HALF), slice(HALF, N), slice(0, N)
-    halves = (early, late)
+    early, late, whole = slice(0, EARLY), slice(EARLY, N), slice(0, N)
+    halves = (slice(0, HALF), slice(HALF, N))
+    early_parts = (slice(0, HALF), slice(HALF, EARLY))
     with ExitStack() as ctx:
         sb = ctx.enter_context(tc.tile_pool(name="sb", bufs=1))
         ps_a = ctx.enter_context(tc.psum_pool(name="ps_a", bufs=LOGIT_BANKS))
@@ -44,9 +48,9 @@ def tile_attend_gnce_sgd_kernel(tc, xT, wT, y, wt, xm, offs, out):
         def bf16_tile(name, tag=None, words=K_PASS):
             return sb.tile([P, words * PACK], BF16, name=name, tag=tag or name, align_bytes=64)
 
-        def mx_tiles(name):
-            return (sb.tile([P, K_PASS], U32, name=name + "_codes", align_bytes=64),
-                    sb.tile([P, K_PASS], U8, name=name + "_scales", align_bytes=64))
+        def mx_tiles(name, words=K_PASS, tag=None):
+            return (sb.tile([P, words], U32, name=name + "_codes", tag=tag or name + "_codes", align_bytes=64),
+                    sb.tile([P, words], U8, name=name + "_scales", align_bytes=64))
 
         def quantize(mx, words, fmt, src):
             nc.vector.quantize_mx(out=mx[0][:, words].bitcast(fmt), scales=mx[1][:, words], in_=src)
@@ -63,8 +67,9 @@ def tile_attend_gnce_sgd_kernel(tc, xT, wT, y, wt, xm, offs, out):
         result = [f32_tile("result%d" % t, [P, T]) for t in range(PACK)]
         x_raw = [[f32_tile("x_raw%d%d" % (u, h), [P, PACK, K_PASS // 2]) for h in range(2)] for u in range(GROUPS)]
         y_raw0 = f32_tile("y_raw0", [P, PACK, N])
-        y_early1, y_late1 = [f32_tile(name, [P, PACK, HALF]) for name in ("y_early1", "y_late1")]
-        xm_raw = [f32_tile("xm_raw%d" % u, [P, PACK, D]) for u in range(GROUPS)]
+        y_early1 = f32_tile("y_early1", [P, PACK, EARLY])
+        y_late1 = f32_tile("y_late1", [P, PACK, LATE])
+        xm_raw = f32_tile("xm_raw", [P, GROUPS, PACK, D])
 
         table_hbm = wT.rearrange("(p t) c -> p t c", t=PACK)
         out_hbm = out.rearrange("(p t) c -> p t c", t=PACK)
@@ -85,9 +90,8 @@ def tile_attend_gnce_sgd_kernel(tc, xT, wT, y, wt, xm, offs, out):
             nc.sync.dma_start(y_raw0[:, j0:j0 + 2, :], y_hbm[0][:, j0:j0 + 2, :])
         nc.sync.dma_start(y_early1[:], y_hbm[1][:, :, early])
         for u in range(GROUPS):
-            nc.sync.dma_start(xm_raw[u][:], xm_hbm[u])
-        for j0 in (0, 2):
-            nc.sync.dma_start(y_late1[:, j0:j0 + 2, :], y_hbm[1][:, j0:j0 + 2, late])
+            nc.sync.dma_start(xm_raw[:, u], xm_hbm[u])
+        nc.sync.dma_start(y_late1[:], y_hbm[1][:, :, late])
         nc.sync.dma_start(result[LAST][:], table_hbm[:, LAST, :])
 
         warm = f32_tile("warm", [P, 2])
@@ -95,49 +99,52 @@ def tile_attend_gnce_sgd_kernel(tc, xT, wT, y, wt, xm, offs, out):
         nc.scalar.activation(warm[:, 1:2], warm[:, 0:1], ACT.Sigmoid)
 
         w_picked = f32_tile("w_picked", [P, PACK, N])
-        w_decayed = [f32_tile("w_decayed%d" % t, [P, N]) for t in range(LAST)]
+        scalar_part = [slice(0, n) for n in SCALAR_SLOTS]
+        vector_part = [slice(n, N) for n in SCALAR_SLOTS]
+        w_decayed = [f32_tile("w_decayed%d" % t, [P, N - SCALAR_SLOTS[t]]) for t in range(PACK)]
+
+        def decay_late(t):
+            nc.vector.tensor_scalar(w_decayed[t][:], w_picked[:, t, vector_part[t]], 1.0 - LR * WD, None, ALU.mult)
+
+        def in_runs(src):
+            return src.rearrange("p j (c i) -> p c j i", i=RUN)
+
+        def words_in_runs(dst):
+            return dst.rearrange("p (c i j) -> p c j i", i=RUN, j=PACK)
+
         for t in range(LAST):
             nc.vector.tensor_copy(w_picked[:, t, :], table[t][:].indirect(offsets[:]))
             nc.scalar.activation(result[t][:], table[t][:], ACT.Copy)
-            nc.vector.tensor_scalar(w_decayed[t][:], w_picked[:, t, :], 1.0 - LR * WD, None, ALU.mult)
+            decay_late(t)
 
         for slots in halves:
             nc.vector.tensor_copy(w_picked[:, LAST, slots], table[LAST][:].indirect(list_part(slots)))
         w_bf = bf16_tile("w_bf")
-        w_dst = w_bf[:].rearrange("p (c i t) -> p c t i", i=RUN, t=PACK)
-        w_src = w_picked[:].rearrange("p t (c i) -> p c t i", i=RUN)
         for slots in halves:
-            runs = slice(slots.start // RUN, slots.stop // RUN)
-            nc.vector.tensor_copy(w_dst[:, runs], w_src[:, runs])
+            nc.vector.tensor_copy(words_in_runs(w_bf[:, PACK * slots.start:PACK * slots.stop]),
+                                  in_runs(w_picked[:, :, slots]))
         w_mx = mx_tiles("w")
         for slots in halves:
             quantize_part(w_mx, w_bf, E4M3, slots.start, slots.stop)
 
         x_mx = [mx_tiles("x%d" % u) for u in range(GROUPS)]
-        sig0 = [f32_tile("sig0%d" % j, [P, N]) for j in range(PACK)]
-        sig_early1, sig_late1 = [f32_tile(name, [P, PACK, HALF]) for name in ("sig_early1", "sig_late1")]
-        err0 = f32_tile("err0", [P, PACK, N])
-        g_bf0 = bf16_tile("g_bf0", "y_early1")
-        g_bf_early1, g_bf_late1 = [bf16_tile(name, words=HALF) for name in ("g_bf_early1", "g_bf_late1")]
-        g_mx = [mx_tiles("g%d" % u) for u in range(GROUPS)]
-        xm_bf_pair0 = bf16_tile("xm_bf_pair0", "y_raw0")
-        xm_mx = [mx_tiles("xm_pair%d" % pair) for pair in range(2)]
-        nc.vector.memset(g_mx[1][0][:, late], 0)
-        nc.vector.memset(g_mx[1][1][:, late], 0)
-
         x_bf = [bf16_tile("x_bf%d" % u) for u in range(GROUPS)]
+        sig = [f32_tile("sig%d" % u, [P, PACK, N]) for u in range(GROUPS)]
 
         def interleave_x(copy, u, h, j0, j1):
             copy(x_bf[u][:].rearrange("p (j h m t) -> p h m t j", j=PACK, h=2, t=PACK)[:, h, :, :, j0:j1],
                  x_raw[u][h][:].rearrange("p t (m j) -> p m t j", j=PACK)[:, :, :, j0:j1])
 
-        def logits_matmul(dst, u, j, slots):
-            words = slice(j * P, (j + 1) * P)
-            nc.tensor.matmul_mx(
-                out=dst,
-                lhsT=x_mx[u][0][:, words].bitcast(E4M3), lhsT_scale=x_mx[u][1][:, words],
-                rhs=w_mx[0][:, slots].bitcast(E4M3), rhs_scale=w_mx[1][:, slots],
-                start=True, stop=True)
+        def sigmoids(u):
+            for j in range(PACK):
+                words = slice(j * P, (j + 1) * P)
+                logits = ps_a.tile([P, N], F32, name="logits")
+                nc.tensor.matmul_mx(
+                    out=logits[:],
+                    lhsT=x_mx[u][0][:, words].bitcast(E4M3), lhsT_scale=x_mx[u][1][:, words],
+                    rhs=w_mx[0][:].bitcast(E4M3), rhs_scale=w_mx[1][:],
+                    start=True, stop=True)
+                nc.scalar.activation(sig[u][:, j, :], logits[:], ACT.Sigmoid)
 
         def interleave_x_group(copy, u):
             interleave_x(copy, u, 0, 0, PACK)
@@ -147,117 +154,144 @@ def tile_attend_gnce_sgd_kernel(tc, xT, wT, y, wt, xm, offs, out):
         interleave_x_group(nc.scalar.copy, 0)
         for j0, j1 in ((0, 1), (1, 2), (2, PACK)):
             quantize_part(x_mx[0], x_bf[0], E4M3, j0 * P, j1 * P)
-        for j in range(PACK):
-            logits = ps_a.tile([P, N], F32, name="logits")
-            logits_matmul(logits[:], 0, j, whole)
-            nc.scalar.activation(sig0[j][:], logits[:], ACT.Sigmoid)
+        sigmoids(0)
         interleave_x_group(nc.vector.tensor_copy, 1)
         for j0 in (0, 2):
             quantize_part(x_mx[1], x_bf[1], E4M3, j0 * P, (j0 + 2) * P)
+        sigmoids(1)
 
-        def sigmoids_group1(sig, slots):
-            for j0 in (0, 2):
-                logits = ps_a.tile([P, N], F32, name="logits")
-                for e in range(2):
-                    logits_matmul(logits[:, e * HALF:(e + 1) * HALF], 1, j0 + e, slots)
-                nc.scalar.activation(sig[:, j0:j0 + 2, :].rearrange("p j i -> p (j i)"), logits[:], ACT.Sigmoid)
+        g_mx = [mx_tiles("g%d" % u) for u in range(GROUPS)]
 
-        y_wt_late1 = f32_tile("y_wt_late1", [P, PACK, HALF])
-        g_early1, g_late1 = [f32_tile(name, [P, PACK, HALF]) for name in ("g_early1", "g_late1")]
+        g_bf = [bf16_tile("g_bf%d" % u) for u in range(GROUPS)]
 
-        def g_words(g_bf, slots):
-            return g_bf[:, PACK * slots.start:PACK * slots.stop].rearrange("p (c i j) -> p c j i", i=RUN, j=PACK)
+        def g_words(u, slots):
+            return words_in_runs(g_bf[u][:, PACK * slots.start:PACK * slots.stop])
 
-        def in_runs(src):
-            return src.rearrange("p j (c i) -> p c j i", i=RUN)
+        def weigh_fused(u, slots, err):
+            runs = (slots.stop - slots.start) // RUN
+            nc.vector.tensor_tensor(
+                g_words(u, slots), in_runs(err),
+                wt_sb[:, u, :].unsqueeze(1).unsqueeze(3).to_broadcast([P, runs, PACK, RUN]), ALU.mult)
 
-        def weigh(dst, src, u):
+        def weigh_apart(u, dst, src):
             for j in range(PACK):
                 nc.scalar.activation(dst[:, j, :], src[:, j, :], ACT.Copy, scale=wt_sb[:, u, j:j + 1])
 
-        for j in range(PACK):
-            nc.vector.tensor_tensor(err0[:, j, :], sig0[j][:], y_raw0[:, j, :], ALU.subtract)
-        sigmoids_group1(sig_early1, early)
-        err_early1 = f32_tile("err_early1", [P, PACK, HALF])
-        nc.vector.tensor_tensor(err_early1[:], sig_early1[:], y_early1[:], ALU.subtract)
-        fused, apart = slice(0, FUSED_SLOTS), slice(FUSED_SLOTS, N)
-        g_apart0 = f32_tile("g_apart0", [P, PACK, N - FUSED_SLOTS])
-        weigh(g_apart0, err0[:, :, apart], 0)
-        weigh(g_early1, err_early1, 1)
-        nc.vector.tensor_tensor(
-            g_words(g_bf0, fused), in_runs(err0[:, :, fused]),
-            wt_sb[:, 0, :].unsqueeze(1).unsqueeze(3).to_broadcast([P, FUSED_SLOTS // RUN, PACK, RUN]),
-            ALU.mult)
-        nc.vector.tensor_copy(g_words(g_bf0, apart), in_runs(g_apart0[:]))
+        def quantize_g(u, slots):
+            quantize_part(g_mx[u], g_bf[u], E5M2, slots.start, slots.stop)
 
-        def interleave_xm(copy, dst, u, pair, m0=0, m1=P):
-            copy(dst[:, m0:m1],
-                 xm_raw[u][:].rearrange("p j (m t) -> p m j t", t=PACK)[:, m0:m1, :, 2 * pair:2 * pair + 2])
+        apart, fused = slice(0, N - FUSED_SLOTS), slice(N - FUSED_SLOTS, N)
+        err0 = f32_tile("err0", [P, PACK, N])
+        y_wt_early1 = f32_tile("y_wt_early1", [P, PACK, EARLY])
+        g_early1 = f32_tile("g_early1", [P, PACK, EARLY])
 
-        def gradient_matmul(dw, u, t, first):
+        xm_bf = [bf16_tile("xm_bf%d" % pair) for pair in range(2)]
+        xm_mx = [mx_tiles("xm_pair0")]
+
+        def interleave_xm(copy, groups, pair, words=slice(0, P)):
+            copy(xm_bf[pair][:].rearrange("p (e u m j) -> p u m j e", u=GROUPS, e=2, j=PACK)[:, groups, words],
+                 xm_raw[:].rearrange("p u j (m t) -> p u m j t", t=PACK)[:, groups, words, :, 2 * pair:2 * pair + 2])
+
+        def gradient_matmul(dst, u, t, slots, start, stop):
             pair, e = divmod(t, 2)
-            word0 = (2 * e + u) * P if pair == 0 else (2 * u + e) * P
-            words = slice(word0, word0 + P)
+            words = slice((2 * e + u) * P, (2 * e + u + 1) * P)
             nc.tensor.matmul_mx(
-                out=dw[:],
+                out=dst,
                 lhsT=xm_mx[pair][0][:, words].bitcast(E4M3), lhsT_scale=xm_mx[pair][1][:, words],
-                rhs=g_mx[u][0][:].bitcast(E5M2), rhs_scale=g_mx[u][1][:],
-                start=first, stop=not first)
+                rhs=g_mx[u][0][:, slots].bitcast(E5M2), rhs_scale=g_mx[u][1][:, slots],
+                start=start, stop=stop)
 
-        pair0_dst = xm_bf_pair0[:].rearrange("p (e u m j) -> p u m j e", u=GROUPS, e=2, j=PACK)
-        interleave_xm(nc.scalar.copy, pair0_dst[:, 0], 0, 0)
-        dw_early = [ps_dw.tile([P, N], F32, name="dw_early%d" % t, tag="dw%d" % t) for t in range(2)]
-        nc.vector.tensor_copy(g_words(g_bf_early1, early), in_runs(g_early1[:]))
-        quantize_part(g_mx[0], g_bf0, E5M2, 0, N)
-        quantize_part(xm_mx[0], xm_bf_pair0, E4M3, 0, P)
-        gradient_matmul(dw_early[0], 0, 0, True)
-        quantize(g_mx[1], early, E5M2, g_bf_early1[:])
-        sigmoids_group1(sig_late1, late)
-        interleave_xm(nc.scalar.copy, pair0_dst[:, 1], 1, 0, 0, SCALAR_XM_WORDS)
-        interleave_xm(nc.vector.tensor_copy, pair0_dst[:, 1], 1, 0, SCALAR_XM_WORDS, P)
-        weigh(y_wt_late1, y_late1, 1)
+        def early_gradient(dw, t):
+            passes = [(u, slots) for u in range(GROUPS) for slots in early_parts]
+            for k, (u, slots) in enumerate(passes):
+                gradient_matmul(dw[:, slots], u, t, slots, k == 0, k == len(passes) - 1)
 
-        quantize_part(xm_mx[0], xm_bf_pair0, E4M3, P, 2 * P)
-        gradient_matmul(dw_early[0], 1, 0, False)
-        quantize_part(xm_mx[0], xm_bf_pair0, E4M3, 2 * P, 4 * P)
-        for u in range(GROUPS):
-            gradient_matmul(dw_early[1], u, 1, u == 0)
-        for j in range(PACK):
-            nc.vector.scalar_tensor_tensor(g_late1[:, j, :], sig_late1[:, j, :], wt_sb[:, 1, j:j + 1],
-                                           y_wt_late1[:, j, :], ALU.mult, ALU.subtract)
+        def late_gradient(dst, t, slots):
+            for u in range(GROUPS):
+                gradient_matmul(dst, u, t, slots, u == 0, u == GROUPS - 1)
 
-        def scale_step(name, dw, slots, tag=None):
-            step = f32_tile(name, [P, slots.stop - slots.start], tag)
-            nc.scalar.activation(step[:], dw[:, slots], ACT.Copy, scale=-LR)
+        for j0, slots in ((0, whole), (2, fused), (2, apart)):
+            nc.vector.tensor_tensor(err0[:, j0:j0 + 2, slots], sig[0][:, j0:j0 + 2, slots],
+                                    y_raw0[:, j0:j0 + 2, slots], ALU.subtract)
+        weigh_fused(0, fused, err0[:, :, fused])
+        weigh_apart(1, y_wt_early1, y_early1)
+        for j, slots in ((0, early), (1, early), (2, early), (3, early_parts[0]), (3, early_parts[1])):
+            nc.vector.scalar_tensor_tensor(g_early1[:, j, slots], sig[1][:, j, slots], wt_sb[:, 1, j:j + 1],
+                                           y_wt_early1[:, j, slots], ALU.mult, ALU.subtract)
+        g_apart0 = y_early1[:, :, apart]
+        weigh_apart(0, g_apart0, err0[:, :, apart])
+        for pair in range(2):
+            interleave_xm(nc.scalar.copy, 0, pair)
+        for slots in early_parts:
+            nc.vector.tensor_copy(g_words(1, slots), in_runs(g_early1[:, :, slots]))
+        nc.vector.tensor_copy(g_words(0, apart), in_runs(g_apart0))
+        for slots in early_parts:
+            quantize_g(1, slots)
+        quantize_g(0, whole)
+        quantize_part(xm_mx[0], xm_bf[0], E4M3, 0, P)
+        interleave_xm(nc.scalar.copy, 1, 0, slice(0, SCALAR_XM_WORDS))
+        interleave_xm(nc.vector.tensor_copy, 1, 0, slice(SCALAR_XM_WORDS, P))
+        interleave_xm(nc.scalar.copy, 1, 1)
+        quantize_part(xm_mx[0], xm_bf[0], E4M3, P, 2 * P)
+        quantize_part(xm_mx[0], xm_bf[0], E4M3, 2 * P, 4 * P)
+        dw_early = [ps_dw.tile([P, EARLY], F32, name="dw_early%d" % t, tag="dw%d" % t) for t in range(PACK)]
+        for t in range(2):
+            early_gradient(dw_early[t], t)
+
+        total = [f32_tile("total%d" % t, [P, SCALAR_SLOTS[t]]) for t in range(PACK)]
+
+        def update_early(t):
+            nc.vector.scalar_tensor_tensor(total[t][:], w_picked[:, t, scalar_part[t]], -(1.0 - LR * WD) / LR,
+                                           dw_early[t][:, scalar_part[t]], ALU.mult, ALU.add)
+
+        def scatter_early(t):
+            nc.scalar.activation(result[t][:].indirect(list_part(scalar_part[t])), total[t][:], ACT.Copy, scale=-LR)
+
+        def scatter_late(t, step):
+            nc.vector.tensor_tensor(result[t][:].indirect(list_part(vector_part[t])), step, w_decayed[t][:], ALU.add)
+
+        def store(t):
+            nc.sync.dma_start(out_hbm[:, t, :], result[t][:])
+
+        err_late1 = xm_bf[0][:, :2 * PACK * LATE].bitcast(F32).rearrange("p (j i) -> p j i", j=PACK)
+        nc.vector.tensor_tensor(err_late1, sig[1][:, :, late], y_late1[:], ALU.subtract)
+        update_early(0)
+        scatter_early(0)
+        weigh_fused(1, late, err_late1)
+        decay_late(LAST)
+        quantize_g(1, late)
+        dw_late0 = ps_dw.tile([P, HALF], F32, name="dw_late0", tag="dw0")
+        late_gradient(dw_late0[:], 0, halves[1])
+
+        xm_mx.append(mx_tiles("xm_pair1", K_PASS, "xm_bf0"))
+        quantize_part(xm_mx[1], xm_bf[1], E4M3, 0, K_PASS)
+
+        def scale_step(t, dw):
+            step = f32_tile("step%d" % t, [P, N - SCALAR_SLOTS[t]])
+            nc.vector.tensor_scalar(step[:], dw, -LR, None, ALU.mult)
             return step
 
-        def scatter(t, step, slots):
-            nc.vector.tensor_tensor(result[t][:].indirect(list_part(slots)), step[:], w_decayed[t][:, slots], ALU.add)
-
-        step_early0 = scale_step("step_early0", dw_early[0], early)
-        nc.scalar.copy(g_words(g_bf_late1, slice(0, HALF)), in_runs(g_late1[:]))
-        scatter(0, step_early0, early)
-        step_early1 = scale_step("step_early1", dw_early[1], early, "g_late1")
-        quantize(g_mx[1], late, E5M2, g_bf_late1[:])
-        scatter(1, step_early1, early)
-        dw_late = [ps_dw.tile([P, N], F32, name="dw_late%d" % t, tag="dw%d" % t) for t in range(2)]
-        for t in range(2):
-            for u in range(GROUPS):
-                gradient_matmul(dw_late[t], u, t, u == 0)
-
-        dw_pair1 = [ps_dw.tile([P, N], F32, name="dw_pair1%d" % e) for e in range(2)]
-        for t, u, tag in ((0, 1, "g_bf_late1"), (1, 0, "g_late1")):
-            xm_bf_pair1 = bf16_tile("xm_bf_pair1%d" % u, tag, 2 * P)
-            interleave_xm(nc.scalar.copy, xm_bf_pair1[:].rearrange("p (e m j) -> p m j e", e=2, j=PACK), u, 1)
-            quantize(xm_mx[1], slice(2 * P * u, 2 * P * (u + 1)), E4M3, xm_bf_pair1[:])
-            for e in range(2):
-                gradient_matmul(dw_pair1[e], u, 2 + e, u == 1)
-            scatter(t, scale_step("step_late%d" % t, dw_late[t], late), late)
-            nc.sync.dma_start(out_hbm[:, t, :], result[t][:])
-
-        w_decayed.append(f32_tile("w_decayed%d" % LAST, [P, N], "xm_raw1"))
-        nc.scalar.activation(w_decayed[LAST][:], w_picked[:, LAST, :], ACT.Copy, scale=1.0 - LR * WD)
-        for e in range(2):
-            t = 2 + e
-            scatter(t, scale_step("step%d" % t, dw_pair1[e], whole), whole)
-            nc.sync.dma_start(out_hbm[:, t, :], result[t][:])
+        step0 = scale_step(0, dw_late0[:, SCALAR_SLOTS[0] - HALF:])
+        update_early(1)
+        scatter_early(1)
+        early_gradient(dw_early[2], 2)
+        dw_late12 = ps_dw.tile([P, 2, HALF], F32, name="dw_late12", tag="dw1")
+        for t in (1, 2):
+            late_gradient(dw_late12[:, t - 1, :], t, halves[1])
+        early_gradient(dw_early[LAST], LAST)
+        dw_late3 = ps_a.tile([P, N], F32, name="logits")
+        late_gradient(dw_late3[:, :LATE], LAST, late)
+        scatter_late(0, step0[:])
+        store(0)
+        update_early(2)
+        scatter_early(2)
+        step1, step2 = [scale_step(t, dw_late12[:, t - 1, SCALAR_SLOTS[t] - HALF:]) for t in (1, 2)]
+        scatter_late(1, step1[:])
+        store(1)
+        update_early(LAST)
+        scatter_early(LAST)
+        step3 = scale_step(LAST, dw_late3[:, :LATE])
+        scatter_late(2, step2[:])
+        store(2)
+        scatter_late(LAST, step3[:])
+        store(LAST)

@@ -65,7 +65,8 @@ def tile_attend_gnce_sgd_kernel(tc, xT, wT, y, wt, xm, offs, out):
         wt_sb = f32_tile("wt_sb", [P, GROUPS, PACK])
         table = [f32_tile("table%d" % t, [P, T]) for t in range(PACK)]
         result = [f32_tile("result%d" % t, [P, T]) for t in range(PACK)]
-        x_raw = [[f32_tile("x_raw%d%d" % (u, h), [P, PACK, K_PASS // 2]) for h in range(2)] for u in range(GROUPS)]
+        x_raw0 = f32_tile("x_raw0", [P, PACK, K_PASS])
+        x_raw1 = [f32_tile("x_raw1%d" % h, [P, PACK, K_PASS // 2]) for h in range(2)]
         y_raw0 = f32_tile("y_raw0", [P, PACK, N])
         y_early1 = f32_tile("y_early1", [P, PACK, EARLY])
         y_late1 = f32_tile("y_late1", [P, PACK, LATE])
@@ -81,10 +82,10 @@ def tile_attend_gnce_sgd_kernel(tc, xT, wT, y, wt, xm, offs, out):
         nc.sync.dma_start(offsets[:], offs)
         for t in range(1, PACK):
             nc.sync.dma_start(table[t][:], table_hbm[:, t, :])
-        for u in range(GROUPS):
-            for h in range(2):
-                row0 = u * K_PASS + h * K_PASS // 2
-                nc.sync.dma_start(x_raw[u][h][:], x_hbm[:, :, row0:row0 + K_PASS // 2])
+        nc.sync.dma_start(x_raw0[:], x_hbm[:, :, :K_PASS])
+        for h in range(2):
+            row0 = K_PASS + h * K_PASS // 2
+            nc.sync.dma_start(x_raw1[h][:], x_hbm[:, :, row0:row0 + K_PASS // 2])
         nc.sync.dma_start(wt_sb[:], wt[0].rearrange("(u p j) one -> p u (j one)", u=GROUPS, j=PACK))
         for j0 in (0, 2):
             nc.sync.dma_start(y_raw0[:, j0:j0 + 2, :], y_hbm[0][:, j0:j0 + 2, :])
@@ -117,8 +118,8 @@ def tile_attend_gnce_sgd_kernel(tc, xT, wT, y, wt, xm, offs, out):
             nc.scalar.activation(result[t][:], table[t][:], ACT.Copy)
             decay_late(t)
 
-        for slots in halves:
-            nc.vector.tensor_copy(w_picked[:, LAST, slots], table[LAST][:].indirect(list_part(slots)))
+        nc.vector.tensor_copy(w_picked[:, LAST, halves[0]], table[LAST][:].indirect(list_part(halves[0])))
+        nc.scalar.activation(w_picked[:, LAST, halves[1]], table[LAST][:].indirect(list_part(halves[1])), ACT.Copy)
         w_bf = bf16_tile("w_bf")
         for slots in halves:
             nc.vector.tensor_copy(words_in_runs(w_bf[:, PACK * slots.start:PACK * slots.stop]),
@@ -131,9 +132,10 @@ def tile_attend_gnce_sgd_kernel(tc, xT, wT, y, wt, xm, offs, out):
         x_bf = [bf16_tile("x_bf%d" % u) for u in range(GROUPS)]
         sig = [f32_tile("sig%d" % u, [P, PACK, N]) for u in range(GROUPS)]
 
-        def interleave_x(copy, u, h, j0, j1):
-            copy(x_bf[u][:].rearrange("p (j h m t) -> p h m t j", j=PACK, h=2, t=PACK)[:, h, :, :, j0:j1],
-                 x_raw[u][h][:].rearrange("p t (m j) -> p m t j", j=PACK)[:, :, :, j0:j1])
+        def interleave_x(copy, u, src, m0, j0, j1):
+            words = slice(m0, m0 + src.shape[2] // PACK)
+            copy(x_bf[u][:].rearrange("p (j m t) -> p m t j", j=PACK, t=PACK)[:, words, :, j0:j1],
+                 src[:].rearrange("p t (m j) -> p m t j", j=PACK)[:, :, :, j0:j1])
 
         def sigmoids(u):
             for j in range(PACK):
@@ -146,16 +148,14 @@ def tile_attend_gnce_sgd_kernel(tc, xT, wT, y, wt, xm, offs, out):
                     start=True, stop=True)
                 nc.scalar.activation(sig[u][:, j, :], logits[:], ACT.Sigmoid)
 
-        def interleave_x_group(copy, u):
-            interleave_x(copy, u, 0, 0, PACK)
-            for j0 in (0, 2):
-                interleave_x(copy, u, 1, j0, j0 + 2)
-
-        interleave_x_group(nc.scalar.copy, 0)
+        interleave_x(nc.vector.tensor_copy, 0, x_raw0, 0, 0, 2)
+        interleave_x(nc.scalar.copy, 0, x_raw0, 0, 2, PACK)
         for j0, j1 in ((0, 1), (1, 2), (2, PACK)):
             quantize_part(x_mx[0], x_bf[0], E4M3, j0 * P, j1 * P)
         sigmoids(0)
-        interleave_x_group(nc.vector.tensor_copy, 1)
+        interleave_x(nc.vector.tensor_copy, 1, x_raw1[0], 0, 0, PACK)
+        for j0 in (0, 2):
+            interleave_x(nc.vector.tensor_copy, 1, x_raw1[1], P // 2, j0, j0 + 2)
         for j0 in (0, 2):
             quantize_part(x_mx[1], x_bf[1], E4M3, j0 * P, (j0 + 2) * P)
         sigmoids(1)
@@ -192,6 +192,8 @@ def tile_attend_gnce_sgd_kernel(tc, xT, wT, y, wt, xm, offs, out):
             copy(xm_bf[pair][:].rearrange("p (e u m j) -> p u m j e", u=GROUPS, e=2, j=PACK)[:, groups, words],
                  xm_raw[:].rearrange("p u j (m t) -> p u m j t", t=PACK)[:, groups, words, :, 2 * pair:2 * pair + 2])
 
+        low_words, high_words = slice(0, P // 2), slice(P // 2, P)
+
         def gradient_matmul(dst, u, t, slots, start, stop):
             pair, e = divmod(t, 2)
             words = slice((2 * e + u) * P, (2 * e + u + 1) * P)
@@ -220,8 +222,8 @@ def tile_attend_gnce_sgd_kernel(tc, xT, wT, y, wt, xm, offs, out):
                                            y_wt_early1[:, j, slots], ALU.mult, ALU.subtract)
         g_apart0 = y_early1[:, :, apart]
         weigh_apart(0, g_apart0, err0[:, :, apart])
-        for pair in range(2):
-            interleave_xm(nc.scalar.copy, 0, pair)
+        interleave_xm(nc.scalar.copy, 0, 0)
+        interleave_xm(nc.scalar.copy, 0, 1, low_words)
         for slots in early_parts:
             nc.vector.tensor_copy(g_words(1, slots), in_runs(g_early1[:, :, slots]))
         nc.vector.tensor_copy(g_words(0, apart), in_runs(g_apart0))
@@ -231,7 +233,8 @@ def tile_attend_gnce_sgd_kernel(tc, xT, wT, y, wt, xm, offs, out):
         quantize_part(xm_mx[0], xm_bf[0], E4M3, 0, P)
         interleave_xm(nc.scalar.copy, 1, 0, slice(0, SCALAR_XM_WORDS))
         interleave_xm(nc.vector.tensor_copy, 1, 0, slice(SCALAR_XM_WORDS, P))
-        interleave_xm(nc.scalar.copy, 1, 1)
+        interleave_xm(nc.scalar.copy, slice(0, GROUPS), 1, high_words)
+        interleave_xm(nc.scalar.copy, 1, 1, low_words)
         quantize_part(xm_mx[0], xm_bf[0], E4M3, P, 2 * P)
         quantize_part(xm_mx[0], xm_bf[0], E4M3, 2 * P, 4 * P)
         dw_early = [ps_dw.tile([P, EARLY], F32, name="dw_early%d" % t, tag="dw%d" % t) for t in range(PACK)]

@@ -1,6 +1,7 @@
 from contextlib import ExitStack
 
 import concourse.mybir as mybir
+from concourse.masks import make_identity
 
 N, T, D, R = 512, 2048, 512, 1024
 LR, WD = 0.1, 0.5
@@ -27,20 +28,23 @@ HALF = N // 2
 EARLY = 384
 LATE = N - EARLY
 SCALAR_SLOTS = (352, 352, 320, EARLY)
-LOGIT_BANKS = 4
-FUSED_SLOTS = 320
-SCALAR_XM_WORDS = 64
+LOGIT_BANKS = ((0, 1, 2, 3), (0, 1, 4, 5))
+BLOCKS = 2
+VECTOR_X_ROWS = 336
+SCALAR_XM_WORDS = 48
 
 
 def tile_attend_gnce_sgd_kernel(tc, xT, wT, y, wt, xm, offs, out):
     nc = tc.nc
-    early, late, whole = slice(0, EARLY), slice(EARLY, N), slice(0, N)
+    early, late = slice(0, EARLY), slice(EARLY, N)
     halves = (slice(0, HALF), slice(HALF, N))
     early_parts = (slice(0, HALF), slice(HALF, EARLY))
     with ExitStack() as ctx:
         sb = ctx.enter_context(tc.tile_pool(name="sb", bufs=1))
-        ps_a = ctx.enter_context(tc.psum_pool(name="ps_a", bufs=LOGIT_BANKS))
-        ps_dw = ctx.enter_context(tc.psum_pool(name="ps_dw", bufs=1))
+        ps = ctx.enter_context(tc.psum_pool(name="ps", bufs=1))
+
+        def bank(b, name, shape):
+            return ps.tile(shape, F32, name=name, tag="bank%d" % b)
 
         def f32_tile(name, shape, tag=None):
             return sb.tile(shape, F32, name=name, tag=tag or name, align_bytes=64)
@@ -80,13 +84,14 @@ def tile_attend_gnce_sgd_kernel(tc, xT, wT, y, wt, xm, offs, out):
 
         nc.sync.dma_start(table[0][:], table_hbm[:, 0, :])
         nc.sync.dma_start(offsets[:], offs)
-        for t in range(1, PACK):
+        for t in range(1, LAST):
             nc.sync.dma_start(table[t][:], table_hbm[:, t, :])
+        nc.sync.dma_start(wt_sb[:], wt[0].rearrange("(u p j) one -> p u (j one)", u=GROUPS, j=PACK))
+        nc.sync.dma_start(table[LAST][:], table_hbm[:, LAST, :])
         nc.sync.dma_start(x_raw0[:], x_hbm[:, :, :K_PASS])
         for h in range(2):
             row0 = K_PASS + h * K_PASS // 2
             nc.sync.dma_start(x_raw1[h][:], x_hbm[:, :, row0:row0 + K_PASS // 2])
-        nc.sync.dma_start(wt_sb[:], wt[0].rearrange("(u p j) one -> p u (j one)", u=GROUPS, j=PACK))
         for j0 in (0, 2):
             nc.sync.dma_start(y_raw0[:, j0:j0 + 2, :], y_hbm[0][:, j0:j0 + 2, :])
         nc.sync.dma_start(y_early1[:], y_hbm[1][:, :, early])
@@ -98,6 +103,9 @@ def tile_attend_gnce_sgd_kernel(tc, xT, wT, y, wt, xm, offs, out):
         warm = f32_tile("warm", [P, 2])
         nc.vector.memset(warm[:, 0:1], 0.0)
         nc.scalar.activation(warm[:, 1:2], warm[:, 0:1], ACT.Sigmoid)
+
+        identity = f32_tile("identity", [P, P])
+        make_identity(nc, identity[:])
 
         w_picked = f32_tile("w_picked", [P, PACK, N])
         scalar_part = [slice(0, n) for n in SCALAR_SLOTS]
@@ -117,6 +125,14 @@ def tile_attend_gnce_sgd_kernel(tc, xT, wT, y, wt, xm, offs, out):
             nc.vector.tensor_copy(w_picked[:, t, :], table[t][:].indirect(offsets[:]))
             nc.scalar.activation(result[t][:], table[t][:], ACT.Copy)
             decay_late(t)
+
+        wt_turned = bank(7, "wt_turned", [P, PACK, P])
+        for j in range(PACK):
+            nc.tensor.transpose(wt_turned[:, j, :], wt_sb[:, 0, j:j + 1].to_broadcast([P, P]), identity[:])
+        wt_neg = f32_tile("wt_neg", [P, PACK])
+        nc.vector.tensor_scalar(wt_neg[:], wt_sb[:, 0, :], -1.0, None, ALU.mult)
+        wt_row = f32_tile("wt_row", [P, P, PACK])
+        nc.vector.tensor_scalar(wt_row[:], wt_turned[:].rearrange("s j p -> s p j"), -1.0, None, ALU.mult)
 
         nc.vector.tensor_copy(w_picked[:, LAST, halves[0]], table[LAST][:].indirect(list_part(halves[0])))
         nc.scalar.activation(w_picked[:, LAST, halves[1]], table[LAST][:].indirect(list_part(halves[1])), ACT.Copy)
@@ -140,25 +156,32 @@ def tile_attend_gnce_sgd_kernel(tc, xT, wT, y, wt, xm, offs, out):
         def sigmoids(u):
             for j in range(PACK):
                 words = slice(j * P, (j + 1) * P)
-                logits = ps_a.tile([P, N], F32, name="logits")
+                logits = bank(LOGIT_BANKS[u][j], "logits%d%d" % (u, j), [P, N])
                 nc.tensor.matmul_mx(
                     out=logits[:],
                     lhsT=x_mx[u][0][:, words].bitcast(E4M3), lhsT_scale=x_mx[u][1][:, words],
                     rhs=w_mx[0][:].bitcast(E4M3), rhs_scale=w_mx[1][:],
                     start=True, stop=True)
-                nc.scalar.activation(sig[u][:, j, :], logits[:], ACT.Sigmoid)
+                nc.scalar.activation(sig[u][:, j, :], logits[:], ACT.Sigmoid, scale=1.0 if u else -1.0)
 
-        interleave_x(nc.vector.tensor_copy, 0, x_raw0, 0, 0, 2)
+        interleave_x(nc.vector.tensor_copy, 0, x_raw0[:, :, :VECTOR_X_ROWS], 0, 0, 2)
+        interleave_x(nc.scalar.copy, 0, x_raw0[:, :, VECTOR_X_ROWS:], VECTOR_X_ROWS // PACK, 0, 2)
         interleave_x(nc.scalar.copy, 0, x_raw0, 0, 2, PACK)
         for j0, j1 in ((0, 1), (1, 2), (2, PACK)):
             quantize_part(x_mx[0], x_bf[0], E4M3, j0 * P, j1 * P)
         sigmoids(0)
+        sums = [bank(2 + b, "sums%d" % b, [P, PACK, P]) for b in range(BLOCKS)]
         interleave_x(nc.vector.tensor_copy, 1, x_raw1[0], 0, 0, PACK)
         for j0 in (0, 2):
             interleave_x(nc.vector.tensor_copy, 1, x_raw1[1], P // 2, j0, j0 + 2)
         for j0 in (0, 2):
             quantize_part(x_mx[1], x_bf[1], E4M3, j0 * P, (j0 + 2) * P)
         sigmoids(1)
+        for b in range(BLOCKS):
+            terms = [(src, j) for j in range(PACK) for src in (y_raw0, sig[0])]
+            for k, (src, j) in enumerate(terms):
+                nc.tensor.matmul(sums[b][:, j, :], src[:, j, HALF + b * P:HALF + (b + 1) * P], identity[:],
+                                 is_transpose=True, start=k == 0, stop=k == len(terms) - 1)
 
         g_mx = [mx_tiles("g%d" % u) for u in range(GROUPS)]
 
@@ -180,17 +203,19 @@ def tile_attend_gnce_sgd_kernel(tc, xT, wT, y, wt, xm, offs, out):
         def quantize_g(u, slots):
             quantize_part(g_mx[u], g_bf[u], E5M2, slots.start, slots.stop)
 
-        apart, fused = slice(0, N - FUSED_SLOTS), slice(N - FUSED_SLOTS, N)
-        err0 = f32_tile("err0", [P, PACK, N])
+        err0 = [f32_tile("err0%d" % b, [P, PACK, P]) for b in range(BLOCKS)]
+        g_turned_back = bf16_tile("g_turned_back", None, HALF)
         y_wt_early1 = f32_tile("y_wt_early1", [P, PACK, EARLY])
         g_early1 = f32_tile("g_early1", [P, PACK, EARLY])
 
-        xm_bf = [bf16_tile("xm_bf%d" % pair) for pair in range(2)]
+        xm_bf_all = bf16_tile("xm_bf", None, 2 * K_PASS)
+        xm_bf = [xm_bf_all[:, pair * PACK * K_PASS:(pair + 1) * PACK * K_PASS] for pair in range(2)]
         xm_mx = [mx_tiles("xm_pair0")]
 
         def interleave_xm(copy, groups, pair, words=slice(0, P)):
             copy(xm_bf[pair][:].rearrange("p (e u m j) -> p u m j e", u=GROUPS, e=2, j=PACK)[:, groups, words],
                  xm_raw[:].rearrange("p u j (m t) -> p u m j t", t=PACK)[:, groups, words, :, 2 * pair:2 * pair + 2])
+
 
         low_words, high_words = slice(0, P // 2), slice(P // 2, P)
 
@@ -212,24 +237,37 @@ def tile_attend_gnce_sgd_kernel(tc, xT, wT, y, wt, xm, offs, out):
             for u in range(GROUPS):
                 gradient_matmul(dst, u, t, slots, u == 0, u == GROUPS - 1)
 
-        for j0, slots in ((0, whole), (2, fused), (2, apart)):
-            nc.vector.tensor_tensor(err0[:, j0:j0 + 2, slots], sig[0][:, j0:j0 + 2, slots],
-                                    y_raw0[:, j0:j0 + 2, slots], ALU.subtract)
-        weigh_fused(0, fused, err0[:, :, fused])
+        for j0 in (0, 2):
+            for b in range(BLOCKS):
+                slots = slice(b * P, (b + 1) * P)
+                nc.vector.scalar_tensor_tensor(err0[b][:, j0:j0 + 2, :], sig[0][:, j0:j0 + 2, slots], 1.0,
+                                               y_raw0[:, j0:j0 + 2, slots], ALU.subtract, ALU.add)
+        for b in range(BLOCKS):
+            nc.vector.tensor_tensor(
+                g_words(0, slice(b * P, (b + 1) * P)), in_runs(err0[b][:]),
+                wt_neg[:].unsqueeze(1).unsqueeze(3).to_broadcast([P, P // RUN, PACK, RUN]), ALU.mult)
+        turned_words = err0[0][:].rearrange("s (b j) i -> s b (j i)", b=BLOCKS)
+        pairs = bank(7, "pairs", [P, BLOCKS, 2, P])
+        for b in range(BLOCKS):
+            nc.vector.scalar_tensor_tensor(turned_words[:, b, :].bitcast(BF16).rearrange("s (p j) -> s p j", j=PACK),
+                                           sums[b][:].rearrange("s j p -> s p j"), 1.0, wt_row[:],
+                                           ALU.subtract, ALU.mult)
+            for e in range(2):
+                nc.tensor.transpose(pairs[:, b, e, :], turned_words[:, b, e::2], identity[:])
         weigh_apart(1, y_wt_early1, y_early1)
         for j, slots in ((0, early), (1, early), (2, early), (3, early_parts[0]), (3, early_parts[1])):
             nc.vector.scalar_tensor_tensor(g_early1[:, j, slots], sig[1][:, j, slots], wt_sb[:, 1, j:j + 1],
                                            y_wt_early1[:, j, slots], ALU.mult, ALU.subtract)
-        g_apart0 = y_early1[:, :, apart]
-        weigh_apart(0, g_apart0, err0[:, :, apart])
+        nc.scalar.copy(g_turned_back[:].bitcast(F32).rearrange("p (b n e) -> p b n e", b=BLOCKS, e=2),
+                       pairs[:].rearrange("p b e n -> p b n e"))
         interleave_xm(nc.scalar.copy, 0, 0)
         interleave_xm(nc.scalar.copy, 0, 1, low_words)
         for slots in early_parts:
             nc.vector.tensor_copy(g_words(1, slots), in_runs(g_early1[:, :, slots]))
-        nc.vector.tensor_copy(g_words(0, apart), in_runs(g_apart0))
         for slots in early_parts:
             quantize_g(1, slots)
-        quantize_g(0, whole)
+        quantize_g(0, halves[0])
+        quantize(g_mx[0], halves[1], E5M2, g_turned_back[:])
         quantize_part(xm_mx[0], xm_bf[0], E4M3, 0, P)
         interleave_xm(nc.scalar.copy, 1, 0, slice(0, SCALAR_XM_WORDS))
         interleave_xm(nc.vector.tensor_copy, 1, 0, slice(SCALAR_XM_WORDS, P))
@@ -237,7 +275,7 @@ def tile_attend_gnce_sgd_kernel(tc, xT, wT, y, wt, xm, offs, out):
         interleave_xm(nc.scalar.copy, 1, 1, low_words)
         quantize_part(xm_mx[0], xm_bf[0], E4M3, P, 2 * P)
         quantize_part(xm_mx[0], xm_bf[0], E4M3, 2 * P, 4 * P)
-        dw_early = [ps_dw.tile([P, EARLY], F32, name="dw_early%d" % t, tag="dw%d" % t) for t in range(PACK)]
+        dw_early = [bank(t, "dw_early%d" % t, [P, EARLY]) for t in range(PACK)]
         for t in range(2):
             early_gradient(dw_early[t], t)
 
@@ -261,12 +299,11 @@ def tile_attend_gnce_sgd_kernel(tc, xT, wT, y, wt, xm, offs, out):
         update_early(0)
         scatter_early(0)
         weigh_fused(1, late, err_late1)
-        decay_late(LAST)
         quantize_g(1, late)
-        dw_late0 = ps_dw.tile([P, HALF], F32, name="dw_late0", tag="dw0")
+        dw_late0 = bank(0, "dw_late0", [P, HALF])
         late_gradient(dw_late0[:], 0, halves[1])
 
-        xm_mx.append(mx_tiles("xm_pair1", K_PASS, "xm_bf0"))
+        xm_mx.append(mx_tiles("xm_pair1", K_PASS, "wt_sb"))
         quantize_part(xm_mx[1], xm_bf[1], E4M3, 0, K_PASS)
 
         def scale_step(t, dw):
@@ -278,11 +315,11 @@ def tile_attend_gnce_sgd_kernel(tc, xT, wT, y, wt, xm, offs, out):
         update_early(1)
         scatter_early(1)
         early_gradient(dw_early[2], 2)
-        dw_late12 = ps_dw.tile([P, 2, HALF], F32, name="dw_late12", tag="dw1")
+        dw_late12 = bank(1, "dw_late12", [P, 2, HALF])
         for t in (1, 2):
             late_gradient(dw_late12[:, t - 1, :], t, halves[1])
         early_gradient(dw_early[LAST], LAST)
-        dw_late3 = ps_a.tile([P, N], F32, name="logits")
+        dw_late3 = bank(6, "dw_late3", [P, N])
         late_gradient(dw_late3[:, :LATE], LAST, late)
         scatter_late(0, step0[:])
         store(0)
@@ -291,6 +328,7 @@ def tile_attend_gnce_sgd_kernel(tc, xT, wT, y, wt, xm, offs, out):
         step1, step2 = [scale_step(t, dw_late12[:, t - 1, SCALAR_SLOTS[t] - HALF:]) for t in (1, 2)]
         scatter_late(1, step1[:])
         store(1)
+        decay_late(LAST)
         update_early(LAST)
         scatter_early(LAST)
         step3 = scale_step(LAST, dw_late3[:, :LATE])

@@ -84,10 +84,12 @@ def tile_attend_gnce_sgd_kernel(tc, xT, wT, y, wt, xm, offs, out):
 
         nc.sync.dma_start(table[0][:], table_hbm[:, 0, :])
         nc.sync.dma_start(offsets[:], offs)
-        for t in range(1, LAST):
+        nc.sync.dma_start(table[1][:], table_hbm[:, 1, :])
+        wt_rows = f32_tile("wt_rows", [P, K_PASS])
+        nc.gpsimd.memset(wt_rows[:], 0.0)
+        nc.sync.dma_start(wt_rows[:GROUPS, :], wt[0].rearrange("(u r) one -> u (r one)", u=GROUPS))
+        for t in range(2, PACK):
             nc.sync.dma_start(table[t][:], table_hbm[:, t, :])
-        nc.sync.dma_start(wt_sb[:], wt[0].rearrange("(u p j) one -> p u (j one)", u=GROUPS, j=PACK))
-        nc.sync.dma_start(table[LAST][:], table_hbm[:, LAST, :])
         nc.sync.dma_start(x_raw0[:], x_hbm[:, :, :K_PASS])
         for h in range(2):
             row0 = K_PASS + h * K_PASS // 2
@@ -126,6 +128,10 @@ def tile_attend_gnce_sgd_kernel(tc, xT, wT, y, wt, xm, offs, out):
             nc.scalar.activation(result[t][:], table[t][:], ACT.Copy)
             decay_late(t)
 
+        wt_dealt = bank(6, "wt_dealt", [P, PACK, P])
+        for j in range(PACK):
+            nc.tensor.transpose(wt_dealt[:, j, :], wt_rows[:, j::PACK], identity[:])
+        nc.vector.tensor_copy(wt_sb[:], wt_dealt[:, :, :GROUPS].rearrange("p j u -> p u j"))
         wt_turned = bank(7, "wt_turned", [P, PACK, P])
         for j in range(PACK):
             nc.tensor.transpose(wt_turned[:, j, :], wt_sb[:, 0, j:j + 1].to_broadcast([P, P]), identity[:])

@@ -27,11 +27,11 @@ SLOTS_PER_COL = 16
 HALF = N // 2
 EARLY = 384
 LATE = N - EARLY
-SCALAR_SLOTS = (352, 352, 320, EARLY)
+SCALAR_SLOTS = (352, 320, 320, EARLY)
 LOGIT_BANKS = ((0, 1, 2, 3), (0, 1, 4, 5))
 BLOCKS = 2
 VECTOR_X_ROWS = 336
-SCALAR_XM_WORDS = 48
+SCALAR_XM_WORDS = 72
 
 
 def tile_attend_gnce_sgd_kernel(tc, xT, wT, y, wt, xm, offs, out):

@@ -27,7 +27,7 @@ SLOTS_PER_COL = 16
 HALF = N // 2
 EARLY = 384
 LATE = N - EARLY
-SCALAR_SLOTS = (352, 320, 320, EARLY)
+SCALAR_SLOTS = (352, 352, HALF, EARLY)
 LOGIT_BANKS = ((0, 1, 2, 3), (0, 1, 4, 5))
 BLOCKS = 2
 VECTOR_X_ROWS = 336
@@ -320,24 +320,24 @@ def tile_attend_gnce_sgd_kernel(tc, xT, wT, y, wt, xm, offs, out):
         step0 = scale_step(0, dw_late0[:, SCALAR_SLOTS[0] - HALF:])
         update_early(1)
         scatter_early(1)
-        early_gradient(dw_early[2], 2)
+        for t in (2, LAST):
+            early_gradient(dw_early[t], t)
         dw_late12 = bank(1, "dw_late12", [P, 2, HALF])
         for t in (1, 2):
             late_gradient(dw_late12[:, t - 1, :], t, halves[1])
-        early_gradient(dw_early[LAST], LAST)
         dw_late3 = bank(6, "dw_late3", [P, N])
         late_gradient(dw_late3[:, :LATE], LAST, late)
         scatter_late(0, step0[:])
         store(0)
-        update_early(2)
-        scatter_early(2)
-        step1, step2 = [scale_step(t, dw_late12[:, t - 1, SCALAR_SLOTS[t] - HALF:]) for t in (1, 2)]
+        step1 = scale_step(1, dw_late12[:, 0, SCALAR_SLOTS[1] - HALF:])
+        for t in (2, LAST):
+            update_early(t)
+            scatter_early(t)
         scatter_late(1, step1[:])
         store(1)
-        decay_late(LAST)
-        update_early(LAST)
-        scatter_early(LAST)
+        step2 = scale_step(2, dw_late12[:, 1, SCALAR_SLOTS[2] - HALF:])
         step3 = scale_step(LAST, dw_late3[:, :LATE])
+        decay_late(LAST)
         scatter_late(2, step2[:])
         store(2)
         scatter_late(LAST, step3[:])

@@ -30,7 +30,6 @@ LATE = N - EARLY
 SCALAR_SLOTS = (352, 352, HALF, EARLY)
 LOGIT_BANKS = ((0, 1, 2, 3), (0, 1, 4, 5))
 BLOCKS = 2
-VECTOR_X_ROWS = 336
 SCALAR_XM_WORDS = 72
 
 
@@ -69,7 +68,7 @@ def tile_attend_gnce_sgd_kernel(tc, xT, wT, y, wt, xm, offs, out):
         wt_sb = f32_tile("wt_sb", [P, GROUPS, PACK])
         table = [f32_tile("table%d" % t, [P, T]) for t in range(PACK)]
         result = [f32_tile("result%d" % t, [P, T]) for t in range(PACK)]
-        x_raw0 = f32_tile("x_raw0", [P, PACK, K_PASS])
+        x_raw0 = [f32_tile("x_raw0%d" % h, [P, PACK, K_PASS // 2]) for h in range(2)]
         x_raw1 = [f32_tile("x_raw1%d" % h, [P, PACK, K_PASS // 2]) for h in range(2)]
         y_raw0 = f32_tile("y_raw0", [P, PACK, N])
         y_early1 = f32_tile("y_early1", [P, PACK, EARLY])
@@ -90,7 +89,8 @@ def tile_attend_gnce_sgd_kernel(tc, xT, wT, y, wt, xm, offs, out):
         nc.sync.dma_start(wt_rows[:GROUPS, :], wt[0].rearrange("(u r) one -> u (r one)", u=GROUPS))
         for t in range(2, PACK):
             nc.sync.dma_start(table[t][:], table_hbm[:, t, :])
-        nc.sync.dma_start(x_raw0[:], x_hbm[:, :, :K_PASS])
+        for h in range(2):
+            nc.sync.dma_start(x_raw0[h][:], x_hbm[:, :, h * K_PASS // 2:(h + 1) * K_PASS // 2])
         for h in range(2):
             row0 = K_PASS + h * K_PASS // 2
             nc.sync.dma_start(x_raw1[h][:], x_hbm[:, :, row0:row0 + K_PASS // 2])
@@ -170,9 +170,9 @@ def tile_attend_gnce_sgd_kernel(tc, xT, wT, y, wt, xm, offs, out):
                     start=True, stop=True)
                 nc.scalar.activation(sig[u][:, j, :], logits[:], ACT.Sigmoid, scale=1.0 if u else -1.0)
 
-        interleave_x(nc.vector.tensor_copy, 0, x_raw0[:, :, :VECTOR_X_ROWS], 0, 0, 2)
-        interleave_x(nc.scalar.copy, 0, x_raw0[:, :, VECTOR_X_ROWS:], VECTOR_X_ROWS // PACK, 0, 2)
-        interleave_x(nc.scalar.copy, 0, x_raw0, 0, 2, PACK)
+        interleave_x(nc.scalar.copy, 0, x_raw0[0], 0, 0, PACK)
+        interleave_x(nc.scalar.copy, 0, x_raw0[1], P // 2, 0, 2)
+        interleave_x(nc.scalar.copy, 0, x_raw0[1], P // 2, 2, PACK)
         for j0, j1 in ((0, 1), (1, 2), (2, PACK)):
             quantize_part(x_mx[0], x_bf[0], E4M3, j0 * P, j1 * P)
         sigmoids(0)

@@ -30,6 +30,7 @@ LATE = N - EARLY
 SCALAR_SLOTS = (352, 352, HALF, EARLY)
 LOGIT_BANKS = ((0, 1, 2, 3), (0, 1, 4, 5))
 BLOCKS = 2
+VECTOR_PAIR1_WORDS = 24
 SCALAR_XM_WORDS = 72
 
 
@@ -223,7 +224,8 @@ def tile_attend_gnce_sgd_kernel(tc, xT, wT, y, wt, xm, offs, out):
                  xm_raw[:].rearrange("p u j (m t) -> p u m j t", t=PACK)[:, groups, words, :, 2 * pair:2 * pair + 2])
 
 
-        low_words, high_words = slice(0, P // 2), slice(P // 2, P)
+        low_words = slice(VECTOR_PAIR1_WORDS, VECTOR_PAIR1_WORDS + P // 2)
+        high_words = slice(low_words.stop, P)
 
         def gradient_matmul(dst, u, t, slots, start, stop):
             pair, e = divmod(t, 2)
@@ -300,11 +302,13 @@ def tile_attend_gnce_sgd_kernel(tc, xT, wT, y, wt, xm, offs, out):
         def store(t):
             nc.sync.dma_start(out_hbm[:, t, :], result[t][:])
 
-        err_late1 = xm_bf[0][:, :2 * PACK * LATE].bitcast(F32).rearrange("p (j i) -> p j i", j=PACK)
+        err_end = PACK * (K_PASS + 16)
+        err_late1 = xm_bf_all[:, err_end - 2 * PACK * LATE:err_end].bitcast(F32).rearrange("p (j i) -> p j i", j=PACK)
         nc.vector.tensor_tensor(err_late1, sig[1][:, :, late], y_late1[:], ALU.subtract)
         update_early(0)
         scatter_early(0)
         weigh_fused(1, late, err_late1)
+        interleave_xm(nc.vector.tensor_copy, slice(0, GROUPS), 1, slice(0, VECTOR_PAIR1_WORDS))
         quantize_g(1, late)
         dw_late0 = bank(0, "dw_late0", [P, HALF])
         late_gradient(dw_late0[:], 0, halves[1])

from contextlib import ExitStack

import concourse.mybir as mybir
from concourse.masks import make_identity

N, T, D, R = 512, 2048, 512, 1024
LR, WD = 0.1, 0.5
FLOPS = 2 * 2 * R * D * N

F32 = mybir.dt.float32
BF16 = mybir.dt.bfloat16
U32 = mybir.dt.uint32
U16 = mybir.dt.uint16
U8 = mybir.dt.uint8
E4M3 = mybir.dt.float8_e4m3fn_x4
E5M2 = mybir.dt.float8_e5m2_x4
ALU = mybir.AluOpType
ACT = mybir.ActivationFunctionType

P = 128
PACK = 4
K_PASS = P * PACK
GROUPS = R // K_PASS
LAST = PACK - 1
RUN = 4
SLOTS_PER_COL = 16
HALF = N // 2
EARLY = 384
LATE = N - EARLY
SCALAR_SLOTS = (352, 352, HALF, EARLY)
LOGIT_BANKS = ((0, 1, 2, 3), (0, 1, 4, 5))
BLOCKS = 2
VECTOR_PAIR1_WORDS = 24
SCALAR_XM_WORDS = 72


def tile_attend_gnce_sgd_kernel(tc, xT, wT, y, wt, xm, offs, out):
    nc = tc.nc
    early, late = slice(0, EARLY), slice(EARLY, N)
    halves = (slice(0, HALF), slice(HALF, N))
    early_parts = (slice(0, HALF), slice(HALF, EARLY))
    with ExitStack() as ctx:
        sb = ctx.enter_context(tc.tile_pool(name="sb", bufs=1))
        ps = ctx.enter_context(tc.psum_pool(name="ps", bufs=1))

        def bank(b, name, shape):
            return ps.tile(shape, F32, name=name, tag="bank%d" % b)

        def f32_tile(name, shape, tag=None):
            return sb.tile(shape, F32, name=name, tag=tag or name, align_bytes=64)

        def bf16_tile(name, tag=None, words=K_PASS):
            return sb.tile([P, words * PACK], BF16, name=name, tag=tag or name, align_bytes=64)

        def mx_tiles(name, words=K_PASS, tag=None):
            return (sb.tile([P, words], U32, name=name + "_codes", tag=tag or name + "_codes", align_bytes=64),
                    sb.tile([P, words], U8, name=name + "_scales", align_bytes=64))

        def quantize(mx, words, fmt, src):
            nc.vector.quantize_mx(out=mx[0][:, words].bitcast(fmt), scales=mx[1][:, words], in_=src)

        def quantize_part(mx, src_tile, fmt, word0, word1):
            quantize(mx, slice(word0, word1), fmt, src_tile[:, PACK * word0:PACK * word1])

        def list_part(slots):
            return offsets[:, slots.start // SLOTS_PER_COL:slots.stop // SLOTS_PER_COL]

        offsets = sb.tile([P, N // SLOTS_PER_COL], U16, name="offsets")
        wt_sb = f32_tile("wt_sb", [P, GROUPS, PACK])
        table = [f32_tile("table%d" % t, [P, T]) for t in range(PACK)]
        result = [f32_tile("result%d" % t, [P, T]) for t in range(PACK)]
        x_raw0 = [f32_tile("x_raw0%d" % h, [P, PACK, K_PASS // 2]) for h in range(2)]
        x_raw1 = [f32_tile("x_raw1%d" % h, [P, PACK, K_PASS // 2]) for h in range(2)]
        y_raw0 = f32_tile("y_raw0", [P, PACK, N])
        y_early1 = f32_tile("y_early1", [P, PACK, EARLY])
        y_late1 = f32_tile("y_late1", [P, PACK, LATE])
        xm_raw = f32_tile("xm_raw", [P, GROUPS, PACK, D])

        table_hbm = wT.rearrange("(p t) c -> p t c", t=PACK)
        out_hbm = out.rearrange("(p t) c -> p t c", t=PACK)
        x_hbm = xT[0].rearrange("(p t) r -> p t r", t=PACK)
        y_hbm = y[0].rearrange("(u p j) i -> u p j i", u=GROUPS, j=PACK)
        xm_hbm = xm[0].rearrange("(u p j) d -> u p j d", u=GROUPS, j=PACK)

        nc.sync.dma_start(table[0][:], table_hbm[:, 0, :])
        nc.sync.dma_start(offsets[:], offs)
        nc.sync.dma_start(table[1][:], table_hbm[:, 1, :])
        wt_rows = f32_tile("wt_rows", [P, K_PASS])
        nc.gpsimd.memset(wt_rows[:], 0.0)
        nc.sync.dma_start(wt_rows[:GROUPS, :], wt[0].rearrange("(u r) one -> u (r one)", u=GROUPS))
        for t in range(2, PACK):
            nc.sync.dma_start(table[t][:], table_hbm[:, t, :])
        for h in range(2):
            nc.sync.dma_start(x_raw0[h][:], x_hbm[:, :, h * K_PASS // 2:(h + 1) * K_PASS // 2])
        for h in range(2):
            row0 = K_PASS + h * K_PASS // 2
            nc.sync.dma_start(x_raw1[h][:], x_hbm[:, :, row0:row0 + K_PASS // 2])
        for j0 in (0, 2):
            nc.sync.dma_start(y_raw0[:, j0:j0 + 2, :], y_hbm[0][:, j0:j0 + 2, :])
        nc.sync.dma_start(y_early1[:], y_hbm[1][:, :, early])
        for u in range(GROUPS):
            nc.sync.dma_start(xm_raw[:, u], xm_hbm[u])
        nc.sync.dma_start(y_late1[:], y_hbm[1][:, :, late])
        nc.sync.dma_start(result[LAST][:], table_hbm[:, LAST, :])

        warm = f32_tile("warm", [P, 2])
        nc.vector.memset(warm[:, 0:1], 0.0)
        nc.scalar.activation(warm[:, 1:2], warm[:, 0:1], ACT.Sigmoid)

        identity = f32_tile("identity", [P, P])
        make_identity(nc, identity[:])

        w_picked = f32_tile("w_picked", [P, PACK, N])
        scalar_part = [slice(0, n) for n in SCALAR_SLOTS]
        vector_part = [slice(n, N) for n in SCALAR_SLOTS]
        w_decayed = [f32_tile("w_decayed%d" % t, [P, N - SCALAR_SLOTS[t]]) for t in range(PACK)]

        def decay_late(t):
            nc.vector.tensor_scalar(w_decayed[t][:], w_picked[:, t, vector_part[t]], 1.0 - LR * WD, None, ALU.mult)

        def in_runs(src):
            return src.rearrange("p j (c i) -> p c j i", i=RUN)

        def words_in_runs(dst):
            return dst.rearrange("p (c i j) -> p c j i", i=RUN, j=PACK)

        for t in range(LAST):
            nc.vector.tensor_copy(w_picked[:, t, :], table[t][:].indirect(offsets[:]))
            nc.scalar.activation(result[t][:], table[t][:], ACT.Copy)
            decay_late(t)

        wt_dealt = bank(6, "wt_dealt", [P, PACK, P])
        for j in range(PACK):
            nc.tensor.transpose(wt_dealt[:, j, :], wt_rows[:, j::PACK], identity[:])
        nc.vector.tensor_copy(wt_sb[:], wt_dealt[:, :, :GROUPS].rearrange("p j u -> p u j"))
        wt_turned = bank(7, "wt_turned", [P, PACK, P])
        for j in range(PACK):
            nc.tensor.transpose(wt_turned[:, j, :], wt_sb[:, 0, j:j + 1].to_broadcast([P, P]), identity[:])
        wt_neg = f32_tile("wt_neg", [P, PACK])
        nc.vector.tensor_scalar(wt_neg[:], wt_sb[:, 0, :], -1.0, None, ALU.mult)
        wt_row = f32_tile("wt_row", [P, P, PACK])
        nc.vector.tensor_scalar(wt_row[:], wt_turned[:].rearrange("s j p -> s p j"), -1.0, None, ALU.mult)

        nc.vector.tensor_copy(w_picked[:, LAST, halves[0]], table[LAST][:].indirect(list_part(halves[0])))
        nc.scalar.activation(w_picked[:, LAST, halves[1]], table[LAST][:].indirect(list_part(halves[1])), ACT.Copy)
        w_bf = bf16_tile("w_bf")
        for slots in halves:
            nc.vector.tensor_copy(words_in_runs(w_bf[:, PACK * slots.start:PACK * slots.stop]),
                                  in_runs(w_picked[:, :, slots]))
        w_mx = mx_tiles("w")
        for slots in halves:
            quantize_part(w_mx, w_bf, E4M3, slots.start, slots.stop)

        x_mx = [mx_tiles("x%d" % u) for u in range(GROUPS)]
        x_bf = [bf16_tile("x_bf%d" % u) for u in range(GROUPS)]
        sig = [f32_tile("sig%d" % u, [P, PACK, N]) for u in range(GROUPS)]

        def interleave_x(copy, u, src, m0, j0, j1):
            words = slice(m0, m0 + src.shape[2] // PACK)
            copy(x_bf[u][:].rearrange("p (j m t) -> p m t j", j=PACK, t=PACK)[:, words, :, j0:j1],
                 src[:].rearrange("p t (m j) -> p m t j", j=PACK)[:, :, :, j0:j1])

        def sigmoids(u):
            for j in range(PACK):
                words = slice(j * P, (j + 1) * P)
                logits = bank(LOGIT_BANKS[u][j], "logits%d%d" % (u, j), [P, N])
                nc.tensor.matmul_mx(
                    out=logits[:],
                    lhsT=x_mx[u][0][:, words].bitcast(E4M3), lhsT_scale=x_mx[u][1][:, words],
                    rhs=w_mx[0][:].bitcast(E4M3), rhs_scale=w_mx[1][:],
                    start=True, stop=True)
                nc.scalar.activation(sig[u][:, j, :], logits[:], ACT.Sigmoid, scale=1.0 if u else -1.0)

        interleave_x(nc.scalar.copy, 0, x_raw0[0], 0, 0, PACK)
        interleave_x(nc.scalar.copy, 0, x_raw0[1], P // 2, 0, 2)
        interleave_x(nc.scalar.copy, 0, x_raw0[1], P // 2, 2, PACK)
        for j0, j1 in ((0, 1), (1, 2), (2, PACK)):
            quantize_part(x_mx[0], x_bf[0], E4M3, j0 * P, j1 * P)
        sigmoids(0)
        sums = [bank(2 + b, "sums%d" % b, [P, PACK, P]) for b in range(BLOCKS)]
        interleave_x(nc.vector.tensor_copy, 1, x_raw1[0], 0, 0, PACK)
        for j0 in (0, 2):
            interleave_x(nc.vector.tensor_copy, 1, x_raw1[1], P // 2, j0, j0 + 2)
        for j0 in (0, 2):
            quantize_part(x_mx[1], x_bf[1], E4M3, j0 * P, (j0 + 2) * P)
        sigmoids(1)
        for b in range(BLOCKS):
            terms = [(src, j) for j in range(PACK) for src in (y_raw0, sig[0])]
            for k, (src, j) in enumerate(terms):
                nc.tensor.matmul(sums[b][:, j, :], src[:, j, HALF + b * P:HALF + (b + 1) * P], identity[:],
                                 is_transpose=True, start=k == 0, stop=k == len(terms) - 1)

        g_mx = [mx_tiles("g%d" % u) for u in range(GROUPS)]

        g_bf = [bf16_tile("g_bf%d" % u) for u in range(GROUPS)]

        def g_words(u, slots):
            return words_in_runs(g_bf[u][:, PACK * slots.start:PACK * slots.stop])

        def weigh_fused(u, slots, err):
            runs = (slots.stop - slots.start) // RUN
            nc.vector.tensor_tensor(
                g_words(u, slots), in_runs(err),
                wt_sb[:, u, :].unsqueeze(1).unsqueeze(3).to_broadcast([P, runs, PACK, RUN]), ALU.mult)

        def weigh_apart(u, dst, src):
            for j in range(PACK):
                nc.scalar.activation(dst[:, j, :], src[:, j, :], ACT.Copy, scale=wt_sb[:, u, j:j + 1])

        def quantize_g(u, slots):
            quantize_part(g_mx[u], g_bf[u], E5M2, slots.start, slots.stop)

        err0 = [f32_tile("err0%d" % b, [P, PACK, P]) for b in range(BLOCKS)]
        g_turned_back = bf16_tile("g_turned_back", None, HALF)
        y_wt_early1 = f32_tile("y_wt_early1", [P, PACK, EARLY])
        g_early1 = f32_tile("g_early1", [P, PACK, EARLY])

        xm_bf_all = bf16_tile("xm_bf", None, 2 * K_PASS)
        xm_bf = [xm_bf_all[:, pair * PACK * K_PASS:(pair + 1) * PACK * K_PASS] for pair in range(2)]
        xm_mx = [mx_tiles("xm_pair0")]

        def interleave_xm(copy, groups, pair, words=slice(0, P)):
            copy(xm_bf[pair][:].rearrange("p (e u m j) -> p u m j e", u=GROUPS, e=2, j=PACK)[:, groups, words],
                 xm_raw[:].rearrange("p u j (m t) -> p u m j t", t=PACK)[:, groups, words, :, 2 * pair:2 * pair + 2])


        low_words = slice(VECTOR_PAIR1_WORDS, VECTOR_PAIR1_WORDS + P // 2)
        high_words = slice(low_words.stop, P)

        def gradient_matmul(dst, u, t, slots, start, stop):
            pair, e = divmod(t, 2)
            words = slice((2 * e + u) * P, (2 * e + u + 1) * P)
            nc.tensor.matmul_mx(
                out=dst,
                lhsT=xm_mx[pair][0][:, words].bitcast(E4M3), lhsT_scale=xm_mx[pair][1][:, words],
                rhs=g_mx[u][0][:, slots].bitcast(E5M2), rhs_scale=g_mx[u][1][:, slots],
                start=start, stop=stop)

        def early_gradient(dw, t):
            passes = [(u, slots) for u in range(GROUPS) for slots in early_parts]
            for k, (u, slots) in enumerate(passes):
                gradient_matmul(dw[:, slots], u, t, slots, k == 0, k == len(passes) - 1)

        def late_gradient(dst, t, slots):
            for u in range(GROUPS):
                gradient_matmul(dst, u, t, slots, u == 0, u == GROUPS - 1)

        for j0 in (0, 2):
            for b in range(BLOCKS):
                slots = slice(b * P, (b + 1) * P)
                nc.vector.scalar_tensor_tensor(err0[b][:, j0:j0 + 2, :], sig[0][:, j0:j0 + 2, slots], 1.0,
                                               y_raw0[:, j0:j0 + 2, slots], ALU.subtract, ALU.add)
        for b in range(BLOCKS):
            nc.vector.tensor_tensor(
                g_words(0, slice(b * P, (b + 1) * P)), in_runs(err0[b][:]),
                wt_neg[:].unsqueeze(1).unsqueeze(3).to_broadcast([P, P // RUN, PACK, RUN]), ALU.mult)
        turned_words = err0[0][:].rearrange("s (b j) i -> s b (j i)", b=BLOCKS)
        pairs = bank(7, "pairs", [P, BLOCKS, 2, P])
        for b in range(BLOCKS):
            nc.vector.scalar_tensor_tensor(turned_words[:, b, :].bitcast(BF16).rearrange("s (p j) -> s p j", j=PACK),
                                           sums[b][:].rearrange("s j p -> s p j"), 1.0, wt_row[:],
                                           ALU.subtract, ALU.mult)
            for e in range(2):
                nc.tensor.transpose(pairs[:, b, e, :], turned_words[:, b, e::2], identity[:])
        weigh_apart(1, y_wt_early1, y_early1)
        for j, slots in ((0, early), (1, early), (2, early), (3, early_parts[0]), (3, early_parts[1])):
            nc.vector.scalar_tensor_tensor(g_early1[:, j, slots], sig[1][:, j, slots], wt_sb[:, 1, j:j + 1],
                                           y_wt_early1[:, j, slots], ALU.mult, ALU.subtract)
        nc.scalar.copy(g_turned_back[:].bitcast(F32).rearrange("p (b n e) -> p b n e", b=BLOCKS, e=2),
                       pairs[:].rearrange("p b e n -> p b n e"))
        interleave_xm(nc.scalar.copy, 0, 0)
        interleave_xm(nc.scalar.copy, 0, 1, low_words)
        for slots in early_parts:
            nc.vector.tensor_copy(g_words(1, slots), in_runs(g_early1[:, :, slots]))
        for slots in early_parts:
            quantize_g(1, slots)
        quantize_g(0, halves[0])
        quantize(g_mx[0], halves[1], E5M2, g_turned_back[:])
        quantize_part(xm_mx[0], xm_bf[0], E4M3, 0, P)
        interleave_xm(nc.scalar.copy, 1, 0, slice(0, SCALAR_XM_WORDS))
        interleave_xm(nc.vector.tensor_copy, 1, 0, slice(SCALAR_XM_WORDS, P))
        interleave_xm(nc.scalar.copy, slice(0, GROUPS), 1, high_words)
        interleave_xm(nc.scalar.copy, 1, 1, low_words)
        quantize_part(xm_mx[0], xm_bf[0], E4M3, P, 2 * P)
        quantize_part(xm_mx[0], xm_bf[0], E4M3, 2 * P, 4 * P)
        dw_early = [bank(t, "dw_early%d" % t, [P, EARLY]) for t in range(PACK)]
        for t in range(2):
            early_gradient(dw_early[t], t)

        total = [f32_tile("total%d" % t, [P, SCALAR_SLOTS[t]]) for t in range(PACK)]

        def update_early(t):
            nc.vector.scalar_tensor_tensor(total[t][:], w_picked[:, t, scalar_part[t]], -(1.0 - LR * WD) / LR,
                                           dw_early[t][:, scalar_part[t]], ALU.mult, ALU.add)

        def scatter_early(t):
            nc.scalar.activation(result[t][:].indirect(list_part(scalar_part[t])), total[t][:], ACT.Copy, scale=-LR)

        def scatter_late(t, step):
            nc.vector.tensor_tensor(result[t][:].indirect(list_part(vector_part[t])), step, w_decayed[t][:], ALU.add)

        def store(t):
            nc.sync.dma_start(out_hbm[:, t, :], result[t][:])

        err_end = PACK * (K_PASS + 16)
        err_late1 = xm_bf_all[:, err_end - 2 * PACK * LATE:err_end].bitcast(F32).rearrange("p (j i) -> p j i", j=PACK)
        nc.vector.tensor_tensor(err_late1, sig[1][:, :, late], y_late1[:], ALU.subtract)
        update_early(0)
        scatter_early(0)
        weigh_fused(1, late, err_late1)
        interleave_xm(nc.vector.tensor_copy, slice(0, GROUPS), 1, slice(0, VECTOR_PAIR1_WORDS))
        quantize_g(1, late)
        dw_late0 = bank(0, "dw_late0", [P, HALF])
        late_gradient(dw_late0[:], 0, halves[1])

        xm_mx.append(mx_tiles("xm_pair1", K_PASS, "wt_sb"))
        quantize_part(xm_mx[1], xm_bf[1], E4M3, 0, K_PASS)

        def scale_step(t, dw):
            step = f32_tile("step%d" % t, [P, N - SCALAR_SLOTS[t]])
            nc.vector.tensor_scalar(step[:], dw, -LR, None, ALU.mult)
            return step

        step0 = scale_step(0, dw_late0[:, SCALAR_SLOTS[0] - HALF:])
        update_early(1)
        scatter_early(1)
        for t in (2, LAST):
            early_gradient(dw_early[t], t)
        dw_late12 = bank(1, "dw_late12", [P, 2, HALF])
        for t in (1, 2):
            late_gradient(dw_late12[:, t - 1, :], t, halves[1])
        dw_late3 = bank(6, "dw_late3", [P, N])
        late_gradient(dw_late3[:, :LATE], LAST, late)
        scatter_late(0, step0[:])
        store(0)
        step1 = scale_step(1, dw_late12[:, 0, SCALAR_SLOTS[1] - HALF:])
        for t in (2, LAST):
            update_early(t)
            scatter_early(t)
        scatter_late(1, step1[:])
        store(1)
        step2 = scale_step(2, dw_late12[:, 1, SCALAR_SLOTS[2] - HALF:])
        step3 = scale_step(LAST, dw_late3[:, :LATE])
        decay_late(LAST)
        scatter_late(2, step2[:])
        store(2)
        scatter_late(LAST, step3[:])
        store(LAST)
